import numpy as np
import ml_dtypes


def mxq(x, axis, fmt="e4m3"):
    dtype, down = {"e4m3": (ml_dtypes.float8_e4m3fn, 7), "e5m2": (ml_dtypes.float8_e5m2, 14)}[fmt]
    v = np.moveaxis(np.asarray(x, np.float32).astype(ml_dtypes.bfloat16).astype(np.float64), axis, -1)
    blocks = v.reshape(v.shape[:-1] + (-1, 32))
    amax = np.abs(blocks).max(-1, keepdims=True)
    byte = np.maximum(np.where(amax > 0, np.frexp(amax)[1] - 1 + 127, 0) - down, 1)
    scale = np.exp2(byte - 127.0)
    codes = (blocks / scale).astype(np.float32).astype(dtype).astype(np.float64)
    return np.moveaxis((codes * scale).reshape(v.shape), -1, axis)


WIDE = False


def mx_kscale(k):
    if not WIDE:
        return np.ones(k)
    levels = np.array([30, -30])
    if k % 512:
        return np.exp2(np.random.permutation(np.resize(levels, k // 32))).repeat(32)
    a = np.empty((k // 512, 16))
    for p in range(k // 512):
        a[p, :8] = np.random.permutation(np.resize(levels, 8))
        for g in range(8):
            far = levels[np.abs(levels - a[p, g]) >= 10]
            a[p, g + 8] = far[np.random.randint(len(far))]
    return np.exp2(a.ravel()).repeat(32)


def f64(x):
    return np.asarray(x).astype(np.float64)


def striped(idx):
    return np.tile(idx.reshape(-1, 16).T, (8, 1)).astype(np.uint16)


def unstriped(offs):
    return offs[:16].T.reshape(-1).astype(np.int64)


E2M1 = np.array([0.0, 0.5, 1.0, 1.5, 2.0, 3.0, 4.0, 6.0, -0.0, -0.5, -1.0, -1.5, -2.0, -3.0, -4.0, -6.0])


def pack_weight(w, fmt):
    k, n = w.shape
    w = f64(np.asarray(w, np.float32).astype(ml_dtypes.bfloat16)).reshape(k // 32, 32, n)
    amax = np.abs(w).max(1)
    if fmt == "e4m3":
        byte = np.frexp(amax)[1] - 1 + 127 - 7
    else:
        mant, ex = np.frexp(amax / 6.0)
        byte = np.where(mant > 0.5, ex, ex - 1) + 127
    byte = np.clip(np.where(amax > 0, byte, 1), 1, 254)
    scaled = (w * np.exp2(127.0 - byte)[:, None, :]).reshape(k, n).astype(np.float32)
    by_word = np.ascontiguousarray(scaled.reshape(k // 512, 128, 4, n).transpose(0, 1, 3, 2))
    if fmt == "e4m3":
        words = by_word.astype(ml_dtypes.float8_e4m3fn).view(np.uint8)
    else:
        c = by_word.astype(ml_dtypes.float4_e2m1fn).view(np.uint8) & 0xF
        words = (c[..., 0::2] | (c[..., 1::2] << 4)).reshape(k // 512, 128, 2 * n)
    return np.ascontiguousarray(words), np.ascontiguousarray(byte.astype(np.uint8).reshape(k // 512, 16, n))


def unpack_weight(words, scales, fmt):
    g, _, n = scales.shape
    words = np.ascontiguousarray(words).reshape(g, 128, n, -1)
    if fmt == "e4m3":
        vals = words.view(ml_dtypes.float8_e4m3fn).astype(np.float64)
    else:
        nib = np.empty((g, 128, n, 4), np.uint8)
        nib[..., 0::2] = words & 0xF
        nib[..., 1::2] = words >> 4
        vals = E2M1[nib]
    vals = vals * np.repeat(np.exp2(scales.astype(np.float64) - 127.0), 8, axis=1)[..., None]
    return vals.transpose(0, 1, 3, 2).reshape(g * 512, n)


def planes(y):
    n, m = y.shape
    v = y.astype(np.float32).astype(ml_dtypes.bfloat16).astype(np.float64).reshape(n // 32, 32, m)
    top = np.abs(v).max(1)
    byte = np.clip(np.where(top > 0, np.frexp(top)[1] - 1 + 127 - 7, 1), 1, 254)
    codes = (v * np.exp2(127.0 - byte)[:, None, :]).reshape(n, m).astype(np.float32).astype(ml_dtypes.float8_e4m3fn).view(np.uint8)
    words = codes.reshape(n // 512, 128, 4, m).transpose(0, 1, 3, 2)
    return np.ascontiguousarray(words), np.ascontiguousarray(byte.astype(np.uint8).reshape(n // 512, 16, m))


K, N, T, J = 512, 512, 2048, 1024


def setup_inputs():
    n = np.random.standard_normal
    s = mx_kscale(K)[:, None]
    m = np.exp(0.5 * n((1, J)))
    p_w = pack_weight(n((K, N)) / np.sqrt(K) / s, "e2m1")
    return {
        "dy": (m * n((K, J)) * s).astype(np.float32),
        "w_words": p_w[0],
        "w_scales": p_w[1],
        "res": (n((N, J))).astype(np.float32),
        "wgo": np.tile(np.random.uniform(0.5, 2.0, J), (128, 1)).astype(np.float32),
        "offs": striped(np.random.permutation(T)[:J]),
    }


def reference(dy, w_words, w_scales, res, wgo, offs):
    idx = unstriped(offs)
    dy_q_ = mxq(f64(dy), 0, "e5m2")
    dy_r_ = mxq(f64(dy) - dy_q_, 0, "e4m3")
    w_ = unpack_weight(w_words, w_scales, "e2m1")
    dx = w_.T @ dy_q_ + w_.T @ dy_r_
    out = np.zeros((N, T))
    out[:, idx] = f64(wgo)[0] * (dx + f64(res))
    return (out,) + planes(out)

@@ -1,0 +1,269 @@
+from contextlib import ExitStack
+
+import concourse.mybir as mybir
+
+K, N, T, J = 512, 512, 2048, 1024
+FLOPS = 1610612736
+
+F32 = mybir.dt.float32
+BF16 = mybir.dt.bfloat16
+I32 = mybir.dt.int32
+U32 = mybir.dt.uint32
+U16 = mybir.dt.uint16
+U8 = mybir.dt.uint8
+E4M3 = mybir.dt.float8_e4m3fn_x4
+E5M2 = mybir.dt.float8_e5m2_x4
+E2M1 = mybir.dt.float4_e2m1fn_x4
+ALU = mybir.AluOpType
+
+P = 128
+PACK = 4
+CHUNK = 512
+HALF = 256
+CHUNKS = J // CHUNK
+SCALAR_COLS = 960
+
+
+def weave(engine_copy, dst, src):
+    engine_copy(
+        dst.rearrange("p (c e) i -> p c i e", e=4),
+        src.rearrange("p i (c e) -> p c i e", e=4),
+    )
+
+
+def tile_list_embg_tgq4_resP_kernel(
+    tc, dy, w_words, w_scales, res, wgo, offs, out_0, out_1, out_2
+):
+    nc = tc.nc
+    dy_v = dy.rearrange("(p i) j -> p i j", i=PACK)
+    res_v = res.rearrange("(p i) j -> p i j", i=PACK)
+    out_v = out_0.rearrange("(p i) t -> p i t", i=PACK)
+    codes_v = out_1[0].rearrange("p t i -> p (t i)").bitcast(I32)
+    scales_v = out_2[0].bitcast(I32)
+
+    with ExitStack() as ctx:
+        held = ctx.enter_context(tc.tile_pool(name="held", bufs=1))
+        ring = ctx.enter_context(tc.tile_pool(name="ring", bufs=3))
+        psum = ctx.enter_context(tc.psum_pool(name="psum", bufs=1))
+
+        offsets = held.tile([P, J // 16], U16, name="offsets")
+        dy_raw = {}
+        for c in range(CHUNKS):
+            for h in range(2):
+                dy_raw[c, h] = held.tile([P, PACK, HALF], F32, name="dy%d%d" % (c, h))
+
+        def load_dy(c, h):
+            j0 = c * CHUNK + h * HALF
+            nc.sync.dma_start(dy_raw[c, h][:], dy_v[:, :, j0 : j0 + HALF])
+
+        w_raw = held.tile([P, 2 * N], U8, name="w_raw")
+        ws_raw = held.tile([P, N], U8, name="ws_raw")
+        gate = held.tile([P, J], F32, name="gate")
+        res_sb = {}
+
+        def load_res(i, c):
+            tag = "late%d" % (i + 2) if (c == 0 and i < 2) else "res%d%d" % (i, c)
+            res_sb[i, c] = held.tile([P, CHUNK], F32, name="res%d%d" % (i, c), tag=tag)
+            nc.sync.dma_start(res_sb[i, c][:], res_v[:, i, c * CHUNK : (c + 1) * CHUNK])
+
+        load_dy(0, 0)
+        load_dy(0, 1)
+        nc.vector.memset(ws_raw[:].bitcast(I32), 0)
+        for q in range(4):
+            nc.scalar.dma_start(
+                ws_raw[32 * q : 32 * q + 4, :].bitcast(I32),
+                w_scales[0, 4 * q : 4 * q + 4, :].bitcast(I32),
+            )
+        nc.sync.dma_start(w_raw[:].bitcast(I32), w_words[0].bitcast(I32))
+        load_dy(1, 0)
+        load_dy(1, 1)
+        nc.sync.dma_start(offsets[:], offs)
+        nc.sync.dma_start(gate[:, 0:CHUNK], wgo[:, 0:CHUNK])
+        for i in range(PACK):
+            load_res(i, 0)
+        nc.sync.dma_start(gate[:, CHUNK:J], wgo[:, CHUNK:J])
+        for i in range(PACK):
+            load_res(i, 1)
+
+        diag = held.tile([P, K + PACK], BF16, name="diag")
+        nc.gpsimd.memset(diag[:], 0.0)
+        nc.gpsimd.affine_select(
+            out=diag[:],
+            in_=diag[:],
+            compare_op=ALU.not_equal,
+            fill=1.0,
+            base=-(PACK - 1),
+            pattern=[[1, K + PACK]],
+            channel_multiplier=-PACK,
+        )
+        eye = held.tile([P, PACK, K], BF16, name="eye", align_bytes=64)
+        for i in range(PACK):
+            nc.scalar.copy(eye[:, i, :], diag[:, PACK - 1 - i : PACK - 1 - i + K])
+
+        window = {}
+        for i in range(2):
+            window[i] = held.tile([P, T], F32, name="window%d" % i)
+            nc.vector.memset(window[i][:], 0.0)
+
+        eye_codes = held.tile([P, K], U32, name="eye_codes", align_bytes=64)
+        eye_scales = held.tile([P, K], U8, name="eye_scales", align_bytes=64)
+        nc.vector.quantize_mx(
+            out=eye_codes[:].bitcast(E4M3),
+            scales=eye_scales[:],
+            in_=eye[:].rearrange("p i k -> p (i k)"),
+        )
+
+        hi_in, hi_codes, hi_scales = {}, {}, {}
+        lo_planes, lo_in, lo_codes, lo_scales = {}, {}, {}, {}
+        for c in range(CHUNKS):
+            for h in range(2):
+                hi_in[c, h] = held.tile([P, HALF, PACK], BF16, name="hi_in%d%d" % (c, h), align_bytes=64)
+            hi_codes[c] = held.tile([P, CHUNK], U32, name="hi_codes%d" % c, align_bytes=64)
+            hi_scales[c] = held.tile([P, CHUNK], U8, name="hi_scales%d" % c, align_bytes=64)
+            lo_planes[c] = held.tile([P, PACK, CHUNK], BF16, name="lo_planes%d" % c, align_bytes=64)
+            lo_in[c] = held.tile([P, CHUNK, PACK], BF16, name="lo_in%d" % c, align_bytes=64)
+            lo_codes[c] = held.tile([P, CHUNK], U32, name="lo_codes%d" % c, align_bytes=64)
+            lo_scales[c] = held.tile([P, CHUNK], U8, name="lo_scales%d" % c, align_bytes=64)
+
+        def quantize_hi(c, h):
+            cols = slice(h * HALF, (h + 1) * HALF)
+            nc.vector.quantize_mx(
+                out=hi_codes[c][:, cols].bitcast(E5M2),
+                scales=hi_scales[c][:, cols],
+                in_=hi_in[c, h][:].rearrange("p j i -> p (j i)"),
+            )
+
+        back = {}
+
+        def dequantize_hi(c):
+            for i in range(PACK):
+                back[c, i] = psum.tile([P, CHUNK], F32, name="back%d" % i)
+                nc.tensor.matmul_mx(
+                    out=back[c, i][:],
+                    lhsT=eye_codes[:, i * P : (i + 1) * P].bitcast(E4M3),
+                    lhsT_scale=eye_scales[:, i * P : (i + 1) * P],
+                    rhs=hi_codes[c][:].bitcast(E5M2),
+                    rhs_scale=hi_scales[c][:],
+                    start=True,
+                    stop=True,
+                )
+
+        def leftover(c):
+            for i in range(PACK):
+                for h in range(2):
+                    cols = slice(h * HALF, (h + 1) * HALF)
+                    nc.vector.tensor_tensor(
+                        lo_planes[c][:, i, cols], dy_raw[c, h][:, i, :], back[c, i][:, cols], ALU.subtract
+                    )
+
+        def quantize_lo(c):
+            nc.vector.quantize_mx(
+                out=lo_codes[c][:].bitcast(E4M3),
+                scales=lo_scales[c][:],
+                in_=lo_in[c][:].rearrange("p j i -> p (j i)"),
+            )
+
+        w_codes = held.tile([P, PACK, 2 * P], U8, name="w_codes", align_bytes=64)
+        w_sc = held.tile([P, PACK, P], U8, name="w_sc", align_bytes=64)
+        dx = {}
+
+        def product(i, c, codes, scales, fmt, first):
+            if first:
+                dx[i, c] = psum.tile([P, CHUNK], F32, name="dx%d" % i)
+            nc.tensor.matmul_mx(
+                out=dx[i, c][:],
+                lhsT=w_codes[:, i, :].bitcast(E2M1),
+                lhsT_scale=w_sc[:, i, :],
+                rhs=codes[c][:].bitcast(fmt),
+                rhs_scale=scales[c][:],
+                start=first,
+                stop=not first,
+            )
+
+        def place(i, c):
+            total = ring.tile([P, CHUNK], F32, name="total")
+            nc.vector.tensor_tensor(total[:], dx[i, c][:], res_sb[i, c][:], ALU.add)
+            if c == 0 and i < 2:
+                window[i + 2] = held.tile([P, T], F32, name="window%d" % (i + 2), tag="late%d" % (i + 2))
+                nc.gpsimd.memset(window[i + 2][:], 0.0)
+            nc.vector.tensor_tensor(
+                window[i][:].indirect(offsets[:, c * (CHUNK // 16) : (c + 1) * (CHUNK // 16)]),
+                total[:],
+                gate[:, c * CHUNK : (c + 1) * CHUNK],
+                ALU.mult,
+            )
+
+        weave(nc.scalar.copy, hi_in[0, 0][:], dy_raw[0, 0][:])
+        weave(nc.vector.tensor_copy, hi_in[0, 1][:], dy_raw[0, 1][:])
+        quantize_hi(0, 0)
+        quantize_hi(0, 1)
+        dequantize_hi(0)
+        nc.vector.tensor_copy(
+            w_codes[:].rearrange("p i (m b) -> p i m b", b=2),
+            w_raw[:].rearrange("p (m i b) -> p i m b", i=PACK, b=2),
+        )
+        nc.vector.tensor_copy(w_sc[:], ws_raw[:].rearrange("p (m i) -> p i m", i=PACK))
+        for h in range(2):
+            weave(nc.scalar.copy, hi_in[1, h][:], dy_raw[1, h][:])
+        leftover(0)
+        for i in range(PACK):
+            product(i, 0, hi_codes, hi_scales, E5M2, True)
+        split = 176
+        weave(nc.scalar.copy, lo_in[0][:, 0:split, :], lo_planes[0][:, :, 0:split])
+        weave(nc.vector.tensor_copy, lo_in[0][:, split:CHUNK, :], lo_planes[0][:, :, split:CHUNK])
+        quantize_hi(1, 0)
+        quantize_lo(0)
+        quantize_hi(1, 1)
+        for i in range(PACK):
+            product(i, 0, lo_codes, lo_scales, E4M3, False)
+        dequantize_hi(1)
+        place(0, 0)
+        leftover(1)
+        weave(nc.scalar.copy, lo_in[1][:], lo_planes[1][:])
+        place(1, 0)
+        quantize_lo(1)
+        place(2, 0)
+        place(3, 0)
+
+        y_planes = held.tile([P, PACK, T], BF16, name="y_planes", align_bytes=64)
+        y_in = held.tile([P, T, PACK], BF16, name="y_in", align_bytes=64)
+        y_codes = held.tile([P, T], U32, name="y_codes", align_bytes=64)
+        y_scales = held.tile([P, T], U8, name="y_scales", align_bytes=64)
+
+        for i in range(PACK):
+            product(i, 1, hi_codes, hi_scales, E5M2, True)
+            product(i, 1, lo_codes, lo_scales, E4M3, False)
+        for i in range(PACK):
+            place(i, 1)
+            nc.sync.dma_start(out_v[:, i, :], window[i][:])
+            if i < PACK - 1:
+                nc.scalar.copy(y_planes[:, i, :], window[i][:])
+
+        last = PACK - 1
+
+        def weave_y(engine_copy, a, b):
+            weave(engine_copy, y_in[:, a:b, :], y_planes[:, :, a:b])
+
+        def quantize_y(g):
+            cols = slice(g * CHUNK, (g + 1) * CHUNK)
+            nc.vector.quantize_mx(
+                out=y_codes[:, cols].bitcast(E4M3),
+                scales=y_scales[:, cols],
+                in_=y_in[:, cols, :].rearrange("p t i -> p (t i)"),
+            )
+            nc.sync.dma_start(codes_v[:, cols], y_codes[:, cols].bitcast(I32))
+
+        nc.scalar.copy(y_planes[:, last, 0:SCALAR_COLS], window[last][:, 0:SCALAR_COLS])
+        nc.vector.tensor_copy(y_planes[:, last, SCALAR_COLS:T], window[last][:, SCALAR_COLS:T])
+        weave_y(nc.scalar.copy, 0, CHUNK)
+        weave_y(nc.scalar.copy, CHUNK, SCALAR_COLS)
+        weave_y(nc.vector.tensor_copy, 2 * CHUNK, 3 * CHUNK)
+        weave_y(nc.vector.tensor_copy, SCALAR_COLS, 2 * CHUNK)
+        quantize_y(2)
+        weave_y(nc.vector.tensor_copy, 3 * CHUNK, T)
+        quantize_y(0)
+        quantize_y(3)
+        quantize_y(1)
+        for q in range(4):
+            queue = nc.scalar if q % 2 else nc.sync
+            queue.dma_start(scales_v[4 * q : 4 * q + 4, :], y_scales[32 * q : 32 * q + 4, :].bitcast(I32))

@@ -21,7 +21,9 @@ PACK = 4
 CHUNK = 512
 HALF = 256
 CHUNKS = J // CHUNK
-SCALAR_COLS = 960
+PARTS = {0: [(0, HALF), (HALF, CHUNK)], 1: [(0, HALF), (HALF, CHUNK)]}
+SCALAR_GROUPS = [(0, 512), (512, 768), (768, 1024)]
+VECTOR_GROUPS = [(1024, 1536), (1536, 2048)]
 
 
 def weave(engine_copy, dst, src):
@@ -46,37 +48,38 @@ def tile_list_embg_tgq4_resP_kernel(
         ring = ctx.enter_context(tc.tile_pool(name="ring", bufs=3))
         psum = ctx.enter_context(tc.psum_pool(name="psum", bufs=1))
 
-        offsets = held.tile([P, J // 16], U16, name="offsets")
-        dy_raw = {}
-        for c in range(CHUNKS):
-            for h in range(2):
-                dy_raw[c, h] = held.tile([P, PACK, HALF], F32, name="dy%d%d" % (c, h))
+        def part_tiles(name, shape, dtype):
+            made = {}
+            for c in range(CHUNKS):
+                for a, b in PARTS[c]:
+                    made[c, a] = held.tile(shape(b - a), dtype, name="%s%d_%d" % (name, c, a), align_bytes=64)
+            return made
 
-        def load_dy(c, h):
-            j0 = c * CHUNK + h * HALF
-            nc.sync.dma_start(dy_raw[c, h][:], dy_v[:, :, j0 : j0 + HALF])
+        offsets = held.tile([P, J // 16], U16, name="offsets")
+        dy_raw = part_tiles("dy", lambda n: [P, PACK, n], F32)
+
+        def load_dy(c):
+            for a, b in PARTS[c]:
+                nc.sync.dma_start(dy_raw[c, a][:], dy_v[:, :, c * CHUNK + a : c * CHUNK + b])
 
         w_raw = held.tile([P, 2 * N], U8, name="w_raw")
-        ws_raw = held.tile([P, N], U8, name="ws_raw")
+        ws_raw = held.tile([P, N], U8, name="ws_raw", tag="late2")
         gate = held.tile([P, J], F32, name="gate")
         res_sb = {}
 
         def load_res(i, c):
-            tag = "late%d" % (i + 2) if (c == 0 and i < 2) else "res%d%d" % (i, c)
-            res_sb[i, c] = held.tile([P, CHUNK], F32, name="res%d%d" % (i, c), tag=tag)
+            res_sb[i, c] = held.tile([P, CHUNK], F32, name="res%d%d" % (i, c))
             nc.sync.dma_start(res_sb[i, c][:], res_v[:, i, c * CHUNK : (c + 1) * CHUNK])
 
-        load_dy(0, 0)
-        load_dy(0, 1)
-        nc.vector.memset(ws_raw[:].bitcast(I32), 0)
+        nc.gpsimd.memset(ws_raw[:].bitcast(I32), 0)
+        load_dy(0)
         for q in range(4):
-            nc.scalar.dma_start(
+            nc.sync.dma_start(
                 ws_raw[32 * q : 32 * q + 4, :].bitcast(I32),
                 w_scales[0, 4 * q : 4 * q + 4, :].bitcast(I32),
             )
         nc.sync.dma_start(w_raw[:].bitcast(I32), w_words[0].bitcast(I32))
-        load_dy(1, 0)
-        load_dy(1, 1)
+        load_dy(1)
         nc.sync.dma_start(offsets[:], offs)
         nc.sync.dma_start(gate[:, 0:CHUNK], wgo[:, 0:CHUNK])
         for i in range(PACK):
@@ -113,25 +116,28 @@ def tile_list_embg_tgq4_resP_kernel(
             in_=eye[:].rearrange("p i k -> p (i k)"),
         )
 
-        hi_in, hi_codes, hi_scales = {}, {}, {}
-        lo_planes, lo_in, lo_codes, lo_scales = {}, {}, {}, {}
+        hi_in = part_tiles("hi_in", lambda n: [P, n, PACK], BF16)
+        lo_planes = part_tiles("lo_planes", lambda n: [P, PACK, n], BF16)
+        lo_in = part_tiles("lo_in", lambda n: [P, n, PACK], BF16)
+        hi_codes, hi_scales, lo_codes, lo_scales = {}, {}, {}, {}
         for c in range(CHUNKS):
-            for h in range(2):
-                hi_in[c, h] = held.tile([P, HALF, PACK], BF16, name="hi_in%d%d" % (c, h), align_bytes=64)
             hi_codes[c] = held.tile([P, CHUNK], U32, name="hi_codes%d" % c, align_bytes=64)
             hi_scales[c] = held.tile([P, CHUNK], U8, name="hi_scales%d" % c, align_bytes=64)
-            lo_planes[c] = held.tile([P, PACK, CHUNK], BF16, name="lo_planes%d" % c, align_bytes=64)
-            lo_in[c] = held.tile([P, CHUNK, PACK], BF16, name="lo_in%d" % c, align_bytes=64)
             lo_codes[c] = held.tile([P, CHUNK], U32, name="lo_codes%d" % c, align_bytes=64)
             lo_scales[c] = held.tile([P, CHUNK], U8, name="lo_scales%d" % c, align_bytes=64)
 
-        def quantize_hi(c, h):
-            cols = slice(h * HALF, (h + 1) * HALF)
+        def quantize(codes, scales, fmt, woven):
             nc.vector.quantize_mx(
-                out=hi_codes[c][:, cols].bitcast(E5M2),
-                scales=hi_scales[c][:, cols],
-                in_=hi_in[c, h][:].rearrange("p j i -> p (j i)"),
+                out=codes.bitcast(fmt), scales=scales, in_=woven[:].rearrange("p j i -> p (j i)")
             )
+
+        def quantize_hi(c, part):
+            a, b = PARTS[c][part]
+            quantize(hi_codes[c][:, a:b], hi_scales[c][:, a:b], E5M2, hi_in[c, a])
+
+        def quantize_lo(c, part):
+            a, b = PARTS[c][part]
+            quantize(lo_codes[c][:, a:b], lo_scales[c][:, a:b], E4M3, lo_in[c, a])
 
         back = {}
 
@@ -148,20 +154,12 @@ def tile_list_embg_tgq4_resP_kernel(
                     stop=True,
                 )
 
-        def leftover(c):
+        def leftover(c, part):
+            a, b = PARTS[c][part]
             for i in range(PACK):
-                for h in range(2):
-                    cols = slice(h * HALF, (h + 1) * HALF)
-                    nc.vector.tensor_tensor(
-                        lo_planes[c][:, i, cols], dy_raw[c, h][:, i, :], back[c, i][:, cols], ALU.subtract
-                    )
-
-        def quantize_lo(c):
-            nc.vector.quantize_mx(
-                out=lo_codes[c][:].bitcast(E4M3),
-                scales=lo_scales[c][:],
-                in_=lo_in[c][:].rearrange("p j i -> p (j i)"),
-            )
+                nc.vector.tensor_tensor(
+                    lo_planes[c, a][:, i, :], dy_raw[c, a][:, i, :], back[c, i][:, a:b], ALU.subtract
+                )
 
         w_codes = held.tile([P, PACK, 2 * P], U8, name="w_codes", align_bytes=64)
         w_sc = held.tile([P, PACK, P], U8, name="w_sc", align_bytes=64)
@@ -180,22 +178,37 @@ def tile_list_embg_tgq4_resP_kernel(
                 stop=not first,
             )
 
+        def clear_late(i):
+            window[i] = held.tile([P, T], F32, name="window%d" % i, tag="late%d" % i)
+            nc.gpsimd.memset(window[i][:], 0.0)
+
+        total = {}
+
+        def combine(i, c):
+            if (i, c) == (2, 0):
+                both = held.tile([P, CHUNK], F32, name="both20", tag="late3")
+            else:
+                both = ring.tile([P, CHUNK], F32, name="both")
+            total[i, c] = ring.tile([P, CHUNK], F32, name="total")
+            weight = gate[:, c * CHUNK : (c + 1) * CHUNK]
+            if (i, c) == (0, 0):
+                nc.vector.tensor_tensor(both[:], dx[i, c][:], res_sb[i, c][:], ALU.add)
+                nc.vector.tensor_tensor(total[i, c][:], both[:], weight, ALU.mult)
+            else:
+                plain = ring.tile([P, CHUNK], F32, name="plain")
+                nc.scalar.copy(plain[:], dx[i, c][:])
+                nc.gpsimd.tensor_tensor(both[:], plain[:], res_sb[i, c][:], ALU.add)
+                nc.gpsimd.tensor_tensor(total[i, c][:], both[:], weight, ALU.mult)
+
         def place(i, c):
-            total = ring.tile([P, CHUNK], F32, name="total")
-            nc.vector.tensor_tensor(total[:], dx[i, c][:], res_sb[i, c][:], ALU.add)
-            if c == 0 and i < 2:
-                window[i + 2] = held.tile([P, T], F32, name="window%d" % (i + 2), tag="late%d" % (i + 2))
-                nc.gpsimd.memset(window[i + 2][:], 0.0)
-            nc.vector.tensor_tensor(
+            nc.vector.tensor_copy(
                 window[i][:].indirect(offsets[:, c * (CHUNK // 16) : (c + 1) * (CHUNK // 16)]),
-                total[:],
-                gate[:, c * CHUNK : (c + 1) * CHUNK],
-                ALU.mult,
+                total[i, c][:],
             )
 
-        weave(nc.scalar.copy, hi_in[0, 0][:], dy_raw[0, 0][:])
-        weave(nc.vector.tensor_copy, hi_in[0, 1][:], dy_raw[0, 1][:])
+        weave(nc.vector.tensor_copy, hi_in[0, 0][:], dy_raw[0, 0][:])
         quantize_hi(0, 0)
+        weave(nc.vector.tensor_copy, hi_in[0, HALF][:], dy_raw[0, HALF][:])
         quantize_hi(0, 1)
         dequantize_hi(0)
         nc.vector.tensor_copy(
@@ -203,67 +216,71 @@ def tile_list_embg_tgq4_resP_kernel(
             w_raw[:].rearrange("p (m i b) -> p i m b", i=PACK, b=2),
         )
         nc.vector.tensor_copy(w_sc[:], ws_raw[:].rearrange("p (m i) -> p i m", i=PACK))
-        for h in range(2):
-            weave(nc.scalar.copy, hi_in[1, h][:], dy_raw[1, h][:])
-        leftover(0)
+        clear_late(2)
+        weave(nc.scalar.copy, hi_in[1, 0][:], dy_raw[1, 0][:])
+        weave(nc.scalar.copy, hi_in[1, HALF][:], dy_raw[1, HALF][:])
+        leftover(0, 0)
+        weave(nc.scalar.copy, lo_in[0, 0][:], lo_planes[0, 0][:])
+        leftover(0, 1)
         for i in range(PACK):
             product(i, 0, hi_codes, hi_scales, E5M2, True)
-        split = 176
-        weave(nc.scalar.copy, lo_in[0][:, 0:split, :], lo_planes[0][:, :, 0:split])
-        weave(nc.vector.tensor_copy, lo_in[0][:, split:CHUNK, :], lo_planes[0][:, :, split:CHUNK])
         quantize_hi(1, 0)
-        quantize_lo(0)
         quantize_hi(1, 1)
+        dequantize_hi(1)
+        weave(nc.vector.tensor_copy, lo_in[0, HALF][:], lo_planes[0, HALF][:])
+        quantize_lo(0, 0)
+        quantize_lo(0, 1)
         for i in range(PACK):
             product(i, 0, lo_codes, lo_scales, E4M3, False)
-        dequantize_hi(1)
+        leftover(1, 0)
+        weave(nc.scalar.copy, lo_in[1, 0][:], lo_planes[1, 0][:])
+        leftover(1, 1)
+        combine(0, 0)
+        combine(1, 0)
+        weave(nc.scalar.copy, lo_in[1, HALF][:], lo_planes[1, HALF][:])
+        quantize_lo(1, 0)
+        quantize_lo(1, 1)
         place(0, 0)
-        leftover(1)
-        weave(nc.scalar.copy, lo_in[1][:], lo_planes[1][:])
         place(1, 0)
-        quantize_lo(1)
+        combine(2, 0)
+        clear_late(3)
         place(2, 0)
+        combine(3, 0)
         place(3, 0)
 
-        y_planes = held.tile([P, PACK, T], BF16, name="y_planes", align_bytes=64)
-        y_in = held.tile([P, T, PACK], BF16, name="y_in", align_bytes=64)
+        groups = SCALAR_GROUPS + VECTOR_GROUPS
+        y_planes, y_in = {}, {}
+        for a, b in groups:
+            y_planes[a] = held.tile([P, PACK, b - a], BF16, name="y_planes%d" % a, align_bytes=64)
+            y_in[a] = held.tile([P, b - a, PACK], BF16, name="y_in%d" % a, align_bytes=64)
         y_codes = held.tile([P, T], U32, name="y_codes", align_bytes=64)
         y_scales = held.tile([P, T], U8, name="y_scales", align_bytes=64)
 
         for i in range(PACK):
             product(i, 1, hi_codes, hi_scales, E5M2, True)
             product(i, 1, lo_codes, lo_scales, E4M3, False)
+        last = PACK - 1
         for i in range(PACK):
+            combine(i, 1)
             place(i, 1)
             nc.sync.dma_start(out_v[:, i, :], window[i][:])
-            if i < PACK - 1:
-                nc.scalar.copy(y_planes[:, i, :], window[i][:])
+            if i < last:
+                for a, b in groups:
+                    nc.scalar.copy(y_planes[a][:, i, :], window[i][:, a:b])
 
-        last = PACK - 1
+        def quantize_y(a, b):
+            quantize(y_codes[:, a:b], y_scales[:, a:b], E4M3, y_in[a])
+            nc.sync.dma_start(codes_v[:, a:b], y_codes[:, a:b].bitcast(I32))
 
-        def weave_y(engine_copy, a, b):
-            weave(engine_copy, y_in[:, a:b, :], y_planes[:, :, a:b])
-
-        def quantize_y(g):
-            cols = slice(g * CHUNK, (g + 1) * CHUNK)
-            nc.vector.quantize_mx(
-                out=y_codes[:, cols].bitcast(E4M3),
-                scales=y_scales[:, cols],
-                in_=y_in[:, cols, :].rearrange("p t i -> p (t i)"),
-            )
-            nc.sync.dma_start(codes_v[:, cols], y_codes[:, cols].bitcast(I32))
-
-        nc.scalar.copy(y_planes[:, last, 0:SCALAR_COLS], window[last][:, 0:SCALAR_COLS])
-        nc.vector.tensor_copy(y_planes[:, last, SCALAR_COLS:T], window[last][:, SCALAR_COLS:T])
-        weave_y(nc.scalar.copy, 0, CHUNK)
-        weave_y(nc.scalar.copy, CHUNK, SCALAR_COLS)
-        weave_y(nc.vector.tensor_copy, 2 * CHUNK, 3 * CHUNK)
-        weave_y(nc.vector.tensor_copy, SCALAR_COLS, 2 * CHUNK)
-        quantize_y(2)
-        weave_y(nc.vector.tensor_copy, 3 * CHUNK, T)
-        quantize_y(0)
-        quantize_y(3)
-        quantize_y(1)
+        for a, b in SCALAR_GROUPS:
+            nc.scalar.copy(y_planes[a][:, last, :], window[last][:, a:b])
+            weave(nc.scalar.copy, y_in[a][:], y_planes[a][:])
+        for a, b in VECTOR_GROUPS:
+            nc.vector.tensor_copy(y_planes[a][:, last, :], window[last][:, a:b])
+        for a, b in VECTOR_GROUPS:
+            weave(nc.vector.tensor_copy, y_in[a][:], y_planes[a][:])
+        for a, b in VECTOR_GROUPS + SCALAR_GROUPS:
+            quantize_y(a, b)
         for q in range(4):
             queue = nc.scalar if q % 2 else nc.sync
             queue.dma_start(scales_v[4 * q : 4 * q + 4, :], y_scales[32 * q : 32 * q + 4, :].bitcast(I32))

@@ -22,8 +22,8 @@ CHUNK = 512
 HALF = 256
 CHUNKS = J // CHUNK
 PARTS = {0: [(0, HALF), (HALF, CHUNK)], 1: [(0, HALF), (HALF, CHUNK)]}
-SCALAR_GROUPS = [(0, 512), (512, 768), (768, 1024)]
-VECTOR_GROUPS = [(1024, 1536), (1536, 2048)]
+GROUPS = T // CHUNK
+ORDER = [(0, 0), (1, 0), (0, 1), (1, 1), (2, 0), (2, 1), (3, 0), (3, 1)]
 
 
 def weave(engine_copy, dst, src):
@@ -52,7 +52,8 @@ def tile_list_embg_tgq4_resP_kernel(
             made = {}
             for c in range(CHUNKS):
                 for a, b in PARTS[c]:
-                    made[c, a] = held.tile(shape(b - a), dtype, name="%s%d_%d" % (name, c, a), align_bytes=64)
+                    tag = "%s%d_%d" % (name, c, a)
+                    made[c, a] = held.tile(shape(b - a), dtype, name=tag, tag=tag, align_bytes=64)
             return made
 
         offsets = held.tile([P, J // 16], U16, name="offsets")
@@ -63,7 +64,7 @@ def tile_list_embg_tgq4_resP_kernel(
                 nc.sync.dma_start(dy_raw[c, a][:], dy_v[:, :, c * CHUNK + a : c * CHUNK + b])
 
         w_raw = held.tile([P, 2 * N], U8, name="w_raw")
-        ws_raw = held.tile([P, N], U8, name="ws_raw", tag="late2")
+        ws_raw = held.tile([P, N], U8, name="ws_raw", tag="ws_raw", align_bytes=64)
         gate = held.tile([P, J], F32, name="gate")
         res_sb = {}
 
@@ -82,11 +83,11 @@ def tile_list_embg_tgq4_resP_kernel(
         load_dy(1)
         nc.sync.dma_start(offsets[:], offs)
         nc.sync.dma_start(gate[:, 0:CHUNK], wgo[:, 0:CHUNK])
-        for i in range(PACK):
-            load_res(i, 0)
+        for i, c in ORDER[:2]:
+            load_res(i, c)
         nc.sync.dma_start(gate[:, CHUNK:J], wgo[:, CHUNK:J])
-        for i in range(PACK):
-            load_res(i, 1)
+        for i, c in ORDER[2:]:
+            load_res(i, c)
 
         diag = held.tile([P, K + PACK], BF16, name="diag")
         nc.gpsimd.memset(diag[:], 0.0)
@@ -178,24 +179,25 @@ def tile_list_embg_tgq4_resP_kernel(
                 stop=not first,
             )
 
-        def clear_late(i):
-            window[i] = held.tile([P, T], F32, name="window%d" % i, tag="late%d" % i)
+        def clear_late(i, tag):
+            window[i] = held.tile([P, T], F32, name="window%d" % i, tag=tag, align_bytes=64)
             nc.gpsimd.memset(window[i][:], 0.0)
 
         total = {}
 
         def combine(i, c):
-            if (i, c) == (2, 0):
-                both = held.tile([P, CHUNK], F32, name="both20", tag="late3")
-            else:
-                both = ring.tile([P, CHUNK], F32, name="both")
-            total[i, c] = ring.tile([P, CHUNK], F32, name="total")
             weight = gate[:, c * CHUNK : (c + 1) * CHUNK]
             if (i, c) == (0, 0):
+                both = held.tile([P, CHUNK], F32, name="both00")
+                total[i, c] = held.tile([P, CHUNK], F32, name="total00", tag="total00", align_bytes=64)
                 nc.vector.tensor_tensor(both[:], dx[i, c][:], res_sb[i, c][:], ALU.add)
                 nc.vector.tensor_tensor(total[i, c][:], both[:], weight, ALU.mult)
             else:
-                plain = ring.tile([P, CHUNK], F32, name="plain")
+                both = held.tile([P, CHUNK], F32, name="both", tag="lo_in1_%d" % HALF, align_bytes=64)
+                total[i, c] = ring.tile([P, CHUNK], F32, name="total", bufs=4)
+                late = {(1, 0): "lo_planes1_%d" % HALF, (2, 0): "lo_in1_0", (3, 0): "total00"}
+                name = "plain%d%d" % (i, c)
+                plain = held.tile([P, CHUNK], F32, name=name, tag=late.get((i, c), name), align_bytes=64)
                 nc.scalar.copy(plain[:], dx[i, c][:])
                 nc.gpsimd.tensor_tensor(both[:], plain[:], res_sb[i, c][:], ALU.add)
                 nc.gpsimd.tensor_tensor(total[i, c][:], both[:], weight, ALU.mult)
@@ -216,7 +218,7 @@ def tile_list_embg_tgq4_resP_kernel(
             w_raw[:].rearrange("p (m i b) -> p i m b", i=PACK, b=2),
         )
         nc.vector.tensor_copy(w_sc[:], ws_raw[:].rearrange("p (m i) -> p i m", i=PACK))
-        clear_late(2)
+        clear_late(2, "ws_raw")
         weave(nc.scalar.copy, hi_in[1, 0][:], dy_raw[1, 0][:])
         weave(nc.scalar.copy, hi_in[1, HALF][:], dy_raw[1, HALF][:])
         leftover(0, 0)
@@ -230,57 +232,54 @@ def tile_list_embg_tgq4_resP_kernel(
         weave(nc.vector.tensor_copy, lo_in[0, HALF][:], lo_planes[0, HALF][:])
         quantize_lo(0, 0)
         quantize_lo(0, 1)
+        clear_late(3, "lo_in0_%d" % HALF)
         for i in range(PACK):
             product(i, 0, lo_codes, lo_scales, E4M3, False)
         leftover(1, 0)
         weave(nc.scalar.copy, lo_in[1, 0][:], lo_planes[1, 0][:])
         leftover(1, 1)
-        combine(0, 0)
-        combine(1, 0)
         weave(nc.scalar.copy, lo_in[1, HALF][:], lo_planes[1, HALF][:])
+        combine(0, 0)
         quantize_lo(1, 0)
         quantize_lo(1, 1)
         place(0, 0)
-        place(1, 0)
-        combine(2, 0)
-        clear_late(3)
-        place(2, 0)
-        combine(3, 0)
-        place(3, 0)
+        for i, c in ORDER[1:]:
+            if c == 1:
+                product(i, 1, hi_codes, hi_scales, E5M2, True)
+                product(i, 1, lo_codes, lo_scales, E4M3, False)
+            combine(i, c)
+            place(i, c)
 
-        groups = SCALAR_GROUPS + VECTOR_GROUPS
-        y_planes, y_in = {}, {}
-        for a, b in groups:
-            y_planes[a] = held.tile([P, PACK, b - a], BF16, name="y_planes%d" % a, align_bytes=64)
-            y_in[a] = held.tile([P, b - a, PACK], BF16, name="y_in%d" % a, align_bytes=64)
-        y_codes = held.tile([P, T], U32, name="y_codes", align_bytes=64)
+        y_in = [held.tile([P, CHUNK, PACK], BF16, name="y_in%d" % g, tag="y_in%d" % g, align_bytes=64) for g in range(GROUPS)]
         y_scales = held.tile([P, T], U8, name="y_scales", align_bytes=64)
 
+        one = held.tile([P, 1], F32, name="one", tag="lo_in1_%d" % HALF, align_bytes=64)
+        nc.gpsimd.memset(one[:], 1.0)
+
+        def round_gpsimd(dst, src):
+            nc.gpsimd.tensor_scalar(dst, src, one[:], 0.0, ALU.mult, ALU.add)
+
+        rounders = {
+            0: [nc.scalar.copy] * GROUPS,
+            1: [nc.scalar.copy] * GROUPS,
+            2: [nc.scalar.copy] + [round_gpsimd] * (GROUPS - 1),
+            3: [nc.scalar.copy] * 2 + [nc.vector.tensor_copy] * 2,
+        }
         for i in range(PACK):
-            product(i, 1, hi_codes, hi_scales, E5M2, True)
-            product(i, 1, lo_codes, lo_scales, E4M3, False)
-        last = PACK - 1
-        for i in range(PACK):
-            combine(i, 1)
-            place(i, 1)
             nc.sync.dma_start(out_v[:, i, :], window[i][:])
-            if i < last:
-                for a, b in groups:
-                    nc.scalar.copy(y_planes[a][:, i, :], window[i][:, a:b])
+            for g in range(GROUPS):
+                src = window[i][:, g * CHUNK : (g + 1) * CHUNK]
+                if i == 2 and g > 0:
+                    rounders[i][g](y_in[g][:, :, 2:4], src.unsqueeze(2).to_broadcast([P, CHUNK, 2]))
+                else:
+                    rounders[i][g](y_in[g][:, :, i], src)
 
-        def quantize_y(a, b):
-            quantize(y_codes[:, a:b], y_scales[:, a:b], E4M3, y_in[a])
-            nc.sync.dma_start(codes_v[:, a:b], y_codes[:, a:b].bitcast(I32))
-
-        for a, b in SCALAR_GROUPS:
-            nc.scalar.copy(y_planes[a][:, last, :], window[last][:, a:b])
-            weave(nc.scalar.copy, y_in[a][:], y_planes[a][:])
-        for a, b in VECTOR_GROUPS:
-            nc.vector.tensor_copy(y_planes[a][:, last, :], window[last][:, a:b])
-        for a, b in VECTOR_GROUPS:
-            weave(nc.vector.tensor_copy, y_in[a][:], y_planes[a][:])
-        for a, b in VECTOR_GROUPS + SCALAR_GROUPS:
-            quantize_y(a, b)
+        for g in (2, 3, 0, 1):
+            cols = slice(g * CHUNK, (g + 1) * CHUNK)
+            tag = "y_in%d" % (g + 2) if g < 2 else "y_codes%d" % g
+            y_codes = held.tile([P, CHUNK], U32, name="y_codes%d" % g, tag=tag, align_bytes=64)
+            quantize(y_codes[:], y_scales[:, cols], E4M3, y_in[g])
+            nc.sync.dma_start(codes_v[:, cols], y_codes[:].bitcast(I32))
         for q in range(4):
             queue = nc.scalar if q % 2 else nc.sync
             queue.dma_start(scales_v[4 * q : 4 * q + 4, :], y_scales[32 * q : 32 * q + 4, :].bitcast(I32))

@@ -89,7 +89,7 @@ def tile_list_embg_tgq4_resP_kernel(
         for i, c in ORDER[2:]:
             load_res(i, c)
 
-        diag = held.tile([P, K + PACK], BF16, name="diag")
+        diag = held.tile([P, K + PACK], BF16, name="diag", tag="hi_in1_0", align_bytes=64)
         nc.gpsimd.memset(diag[:], 0.0)
         nc.gpsimd.affine_select(
             out=diag[:],
@@ -100,7 +100,7 @@ def tile_list_embg_tgq4_resP_kernel(
             pattern=[[1, K + PACK]],
             channel_multiplier=-PACK,
         )
-        eye = held.tile([P, PACK, K], BF16, name="eye", align_bytes=64)
+        eye = held.tile([P, PACK, K], BF16, name="eye", tag="hi_in1_%d" % HALF, align_bytes=64)
         for i in range(PACK):
             nc.scalar.copy(eye[:, i, :], diag[:, PACK - 1 - i : PACK - 1 - i + K])
 
@@ -122,7 +122,8 @@ def tile_list_embg_tgq4_resP_kernel(
         lo_in = part_tiles("lo_in", lambda n: [P, n, PACK], BF16)
         hi_codes, hi_scales, lo_codes, lo_scales = {}, {}, {}, {}
         for c in range(CHUNKS):
-            hi_codes[c] = held.tile([P, CHUNK], U32, name="hi_codes%d" % c, align_bytes=64)
+            hi_tag = "dy0_0" if c else "hi_codes0"
+            hi_codes[c] = held.tile([P, CHUNK], U32, name="hi_codes%d" % c, tag=hi_tag, align_bytes=64)
             hi_scales[c] = held.tile([P, CHUNK], U8, name="hi_scales%d" % c, align_bytes=64)
             lo_codes[c] = held.tile([P, CHUNK], U32, name="lo_codes%d" % c, align_bytes=64)
             lo_scales[c] = held.tile([P, CHUNK], U8, name="lo_scales%d" % c, align_bytes=64)
@@ -144,7 +145,7 @@ def tile_list_embg_tgq4_resP_kernel(
 
         def dequantize_hi(c):
             for i in range(PACK):
-                back[c, i] = psum.tile([P, CHUNK], F32, name="back%d" % i)
+                back[c, i] = psum.tile([P, CHUNK], F32, name="bank%d%d" % (c, i))
                 nc.tensor.matmul_mx(
                     out=back[c, i][:],
                     lhsT=eye_codes[:, i * P : (i + 1) * P].bitcast(E4M3),
@@ -168,7 +169,7 @@ def tile_list_embg_tgq4_resP_kernel(
 
         def product(i, c, codes, scales, fmt, first):
             if first:
-                dx[i, c] = psum.tile([P, CHUNK], F32, name="dx%d" % i)
+                dx[i, c] = psum.tile([P, CHUNK], F32, name="bank%d%d" % (c, i))
             nc.tensor.matmul_mx(
                 out=dx[i, c][:],
                 lhsT=w_codes[:, i, :].bitcast(E2M1),
@@ -250,7 +251,11 @@ def tile_list_embg_tgq4_resP_kernel(
             combine(i, c)
             place(i, c)
 
-        y_in = [held.tile([P, CHUNK, PACK], BF16, name="y_in%d" % g, tag="y_in%d" % g, align_bytes=64) for g in range(GROUPS)]
+        spans = [(2 * CHUNK, 3 * CHUNK), (3 * CHUNK, T - HALF), (0, CHUNK), (CHUNK, 2 * CHUNK), (T - HALF, T)]
+        y_in = [
+            held.tile([P, b - a, PACK], BF16, name="y_in%d" % g, tag="y_in%d" % g, align_bytes=64)
+            for g, (a, b) in enumerate(spans)
+        ]
         y_scales = held.tile([P, T], U8, name="y_scales", align_bytes=64)
 
         one = held.tile([P, 1], F32, name="one", tag="lo_in1_%d" % HALF, align_bytes=64)
@@ -259,27 +264,22 @@ def tile_list_embg_tgq4_resP_kernel(
         def round_gpsimd(dst, src):
             nc.gpsimd.tensor_scalar(dst, src, one[:], 0.0, ALU.mult, ALU.add)
 
-        rounders = {
-            0: [nc.scalar.copy] * GROUPS,
-            1: [nc.scalar.copy] * GROUPS,
-            2: [nc.scalar.copy] + [round_gpsimd] * (GROUPS - 1),
-            3: [nc.scalar.copy] * 2 + [nc.vector.tensor_copy] * 2,
-        }
         for i in range(PACK):
             nc.sync.dma_start(out_v[:, i, :], window[i][:])
-            for g in range(GROUPS):
-                src = window[i][:, g * CHUNK : (g + 1) * CHUNK]
-                if i == 2 and g > 0:
-                    rounders[i][g](y_in[g][:, :, 2:4], src.unsqueeze(2).to_broadcast([P, CHUNK, 2]))
+            for g, (a, b) in enumerate(spans):
+                src = window[i][:, a:b]
+                if i == 2 and g != 2:
+                    round_gpsimd(y_in[g][:, :, 2:4], src.unsqueeze(2).to_broadcast([P, b - a, 2]))
+                elif i == 3 and g < 2:
+                    nc.vector.tensor_copy(y_in[g][:, :, i], src)
                 else:
-                    rounders[i][g](y_in[g][:, :, i], src)
+                    nc.scalar.copy(y_in[g][:, :, i], src)
 
-        for g in (2, 3, 0, 1):
-            cols = slice(g * CHUNK, (g + 1) * CHUNK)
-            tag = "y_in%d" % (g + 2) if g < 2 else "y_codes%d" % g
-            y_codes = held.tile([P, CHUNK], U32, name="y_codes%d" % g, tag=tag, align_bytes=64)
-            quantize(y_codes[:], y_scales[:, cols], E4M3, y_in[g])
-            nc.sync.dma_start(codes_v[:, cols], y_codes[:].bitcast(I32))
+        for g, (a, b) in enumerate(spans):
+            tag = "y_in%d" % (g - 2) if g >= 2 else "y_codes%d" % g
+            y_codes = held.tile([P, b - a], U32, name="y_codes%d" % g, tag=tag, align_bytes=64)
+            quantize(y_codes[:], y_scales[:, a:b], E4M3, y_in[g])
+            nc.sync.dma_start(codes_v[:, a:b], y_codes[:].bitcast(I32))
         for q in range(4):
             queue = nc.scalar if q % 2 else nc.sync
             queue.dma_start(scales_v[4 * q : 4 * q + 4, :], y_scales[32 * q : 32 * q + 4, :].bitcast(I32))

@@ -18,19 +18,14 @@ ALU = mybir.AluOpType
 
 P = 128
 PACK = 4
+UNIT = 128
+UNITS = J // UNIT
 CHUNK = 512
-HALF = 256
-CHUNKS = J // CHUNK
-PARTS = {0: [(0, HALF), (HALF, CHUNK)], 1: [(0, HALF), (HALF, CHUNK)]}
-GROUPS = T // CHUNK
+HALF = CHUNK // 2
+QUARTER = T // 4
+LOADS = [(0, 1), (1, 2), (2, 4), (4, 6), (6, 8)]
+LO_RUNS = [(0, 2), (2, 4), (4, 7), (7, 8)]
 ORDER = [(0, 0), (1, 0), (0, 1), (1, 1), (2, 0), (2, 1), (3, 0), (3, 1)]
-
-
-def weave(engine_copy, dst, src):
-    engine_copy(
-        dst.rearrange("p (c e) i -> p c i e", e=4),
-        src.rearrange("p i (c e) -> p c i e", e=4),
-    )
 
 
 def tile_list_embg_tgq4_resP_kernel(
@@ -38,58 +33,51 @@ def tile_list_embg_tgq4_resP_kernel(
 ):
     nc = tc.nc
     dy_v = dy.rearrange("(p i) j -> p i j", i=PACK)
-    res_v = res.rearrange("(p i) j -> p i j", i=PACK)
-    out_v = out_0.rearrange("(p i) t -> p i t", i=PACK)
-    codes_v = out_1[0].rearrange("p t i -> p (t i)").bitcast(I32)
-    scales_v = out_2[0].bitcast(I32)
 
     with ExitStack() as ctx:
         held = ctx.enter_context(tc.tile_pool(name="held", bufs=1))
-        ring = ctx.enter_context(tc.tile_pool(name="ring", bufs=3))
         psum = ctx.enter_context(tc.psum_pool(name="psum", bufs=1))
 
-        def part_tiles(name, shape, dtype):
-            made = {}
-            for c in range(CHUNKS):
-                for a, b in PARTS[c]:
-                    tag = "%s%d_%d" % (name, c, a)
-                    made[c, a] = held.tile(shape(b - a), dtype, name=tag, tag=tag, align_bytes=64)
-            return made
+        def sb(name, shape, dtype, tag=None):
+            return held.tile(shape, dtype, name=name, tag=tag or name, align_bytes=64)
+
+        def bank(name, index, shape):
+            return psum.tile(shape, F32, name=name, tag="bank%d" % index)
 
         offsets = held.tile([P, J // 16], U16, name="offsets")
-        dy_raw = part_tiles("dy", lambda n: [P, PACK, n], F32)
-
-        def load_dy(c):
-            for a, b in PARTS[c]:
-                nc.sync.dma_start(dy_raw[c, a][:], dy_v[:, :, c * CHUNK + a : c * CHUNK + b])
-
-        w_raw = held.tile([P, 2 * N], U8, name="w_raw")
-        ws_raw = held.tile([P, N], U8, name="ws_raw", tag="ws_raw", align_bytes=64)
-        gate = held.tile([P, J], F32, name="gate")
+        w_raw = sb("w_raw", [P, 2 * N], U8)
+        ws_raw = sb("ws_raw", [P, N], U8)
+        gate = [sb("gate%d" % c, [P, CHUNK], F32) for c in range(2)]
+        nc.gpsimd.memset(ws_raw[:].bitcast(I32), 0)
+        dy_unit = {}
+        for a, b in LOADS:
+            raw = sb("dy%d" % a, [P, PACK, (b - a) * UNIT], F32)
+            nc.sync.dma_start(raw[:], dy_v[:, :, a * UNIT : b * UNIT])
+            for u in range(a, b):
+                dy_unit[u] = raw[:, :, (u - a) * UNIT : (u - a + 1) * UNIT]
+            if a == 2:
+                for q in range(4):
+                    nc.sync.dma_start(
+                        ws_raw[32 * q : 32 * q + 4, :].bitcast(I32),
+                        w_scales[0, 4 * q : 4 * q + 4, :].bitcast(I32),
+                    )
+        nc.sync.dma_start(w_raw[:].bitcast(I32), w_words[0].bitcast(I32))
         res_sb = {}
 
-        def load_res(i, c):
-            res_sb[i, c] = held.tile([P, CHUNK], F32, name="res%d%d" % (i, c))
-            nc.sync.dma_start(res_sb[i, c][:], res_v[:, i, c * CHUNK : (c + 1) * CHUNK])
+        def load_res(b, c):
+            res_sb[b, c] = sb("res%d%d" % (b, c), [P, CHUNK], F32)
+            nc.sync.dma_start(res_sb[b, c][:], res[b * P : (b + 1) * P, c * CHUNK : (c + 1) * CHUNK])
 
-        nc.gpsimd.memset(ws_raw[:].bitcast(I32), 0)
-        load_dy(0)
-        for q in range(4):
-            nc.sync.dma_start(
-                ws_raw[32 * q : 32 * q + 4, :].bitcast(I32),
-                w_scales[0, 4 * q : 4 * q + 4, :].bitcast(I32),
-            )
-        nc.sync.dma_start(w_raw[:].bitcast(I32), w_words[0].bitcast(I32))
-        load_dy(1)
+        load_res(0, 0)
+        nc.sync.dma_start(gate[0][:], wgo[:, 0:CHUNK])
         nc.sync.dma_start(offsets[:], offs)
-        nc.sync.dma_start(gate[:, 0:CHUNK], wgo[:, 0:CHUNK])
-        for i, c in ORDER[:2]:
-            load_res(i, c)
-        nc.sync.dma_start(gate[:, CHUNK:J], wgo[:, CHUNK:J])
-        for i, c in ORDER[2:]:
-            load_res(i, c)
+        load_res(1, 0)
+        load_res(0, 1)
+        nc.sync.dma_start(gate[1][:], wgo[:, CHUNK:J])
+        for b, c in ORDER[3:]:
+            load_res(b, c)
 
-        diag = held.tile([P, K + PACK], BF16, name="diag", tag="hi_in1_0", align_bytes=64)
+        diag = sb("diag", [P, K + PACK], BF16, tag="hi_in1")
         nc.gpsimd.memset(diag[:], 0.0)
         nc.gpsimd.affine_select(
             out=diag[:],
@@ -100,186 +88,218 @@ def tile_list_embg_tgq4_resP_kernel(
             pattern=[[1, K + PACK]],
             channel_multiplier=-PACK,
         )
-        eye = held.tile([P, PACK, K], BF16, name="eye", tag="hi_in1_%d" % HALF, align_bytes=64)
+        eye = sb("eye", [P, PACK, K], BF16, tag="hi_in0")
         for i in range(PACK):
             nc.scalar.copy(eye[:, i, :], diag[:, PACK - 1 - i : PACK - 1 - i + K])
+        ident = sb("ident", [P, P], F32)
+        nc.scalar.copy(ident[:], diag[:, PACK - 1 : PACK - 1 + K : PACK])
 
         window = {}
-        for i in range(2):
-            window[i] = held.tile([P, T], F32, name="window%d" % i)
-            nc.vector.memset(window[i][:], 0.0)
+        for b in range(2):
+            window[b] = sb("window%d" % b, [P, T], F32)
+            nc.vector.memset(window[b][:], 0.0)
 
-        eye_codes = held.tile([P, K], U32, name="eye_codes", align_bytes=64)
-        eye_scales = held.tile([P, K], U8, name="eye_scales", align_bytes=64)
+        eye_codes = sb("eye_codes", [P, K], U32)
+        eye_scales = sb("eye_scales", [P, K], U8)
         nc.vector.quantize_mx(
             out=eye_codes[:].bitcast(E4M3),
             scales=eye_scales[:],
             in_=eye[:].rearrange("p i k -> p (i k)"),
         )
 
-        hi_in = part_tiles("hi_in", lambda n: [P, n, PACK], BF16)
-        lo_planes = part_tiles("lo_planes", lambda n: [P, PACK, n], BF16)
-        lo_in = part_tiles("lo_in", lambda n: [P, n, PACK], BF16)
-        hi_codes, hi_scales, lo_codes, lo_scales = {}, {}, {}, {}
-        for c in range(CHUNKS):
-            hi_tag = "dy0_0" if c else "hi_codes0"
-            hi_codes[c] = held.tile([P, CHUNK], U32, name="hi_codes%d" % c, tag=hi_tag, align_bytes=64)
-            hi_scales[c] = held.tile([P, CHUNK], U8, name="hi_scales%d" % c, align_bytes=64)
-            lo_codes[c] = held.tile([P, CHUNK], U32, name="lo_codes%d" % c, align_bytes=64)
-            lo_scales[c] = held.tile([P, CHUNK], U8, name="lo_scales%d" % c, align_bytes=64)
+        hi_codes = [sb("hi_codes%d" % c, [P, CHUNK], U32) for c in range(2)]
+        hi_scales = [sb("hi_scales%d" % c, [P, CHUNK], U8) for c in range(2)]
+        lo_codes = [sb("lo_codes%d" % c, [P, CHUNK], U32) for c in range(2)]
+        lo_scales = [sb("lo_scales%d" % c, [P, CHUNK], U8) for c in range(2)]
+        lo_in = {a: sb("lo_in%d" % a, [P, (b - a) * UNIT, PACK], BF16) for a, b in LO_RUNS}
+        hi_first = sb("hi_in0", [P, UNIT, PACK], BF16)
+        hi_rest = sb("hi_in1", [P, J - UNIT, PACK], BF16)
+        hi_in, back = {}, {}
 
-        def quantize(codes, scales, fmt, woven):
-            nc.vector.quantize_mx(
-                out=codes.bitcast(fmt), scales=scales, in_=woven[:].rearrange("p j i -> p (j i)")
+        def unit_cols(u):
+            return u // 4, slice((u % 4) * UNIT, (u % 4 + 1) * UNIT)
+
+        def weave(u):
+            hi_in[u] = hi_rest[:, (u - 1) * UNIT : u * UNIT, :] if u else hi_first[:]
+            copy = nc.scalar.copy if u else nc.vector.tensor_copy
+            copy(
+                hi_in[u].rearrange("p (c e) i -> p c i e", e=4),
+                dy_unit[u].rearrange("p i (c e) -> p c i e", e=4),
             )
 
-        def quantize_hi(c, part):
-            a, b = PARTS[c][part]
-            quantize(hi_codes[c][:, a:b], hi_scales[c][:, a:b], E5M2, hi_in[c, a])
-
-        def quantize_lo(c, part):
-            a, b = PARTS[c][part]
-            quantize(lo_codes[c][:, a:b], lo_scales[c][:, a:b], E4M3, lo_in[c, a])
-
-        back = {}
-
-        def dequantize_hi(c):
+        def first_tier(u):
+            c, cols = unit_cols(u)
+            nc.vector.quantize_mx(
+                out=hi_codes[c][:, cols].bitcast(E5M2),
+                scales=hi_scales[c][:, cols],
+                in_=hi_in[u].rearrange("p j i -> p (j i)"),
+            )
+            back[u] = bank("back%d" % u, (0, 1, 2, 0, 1, 2, 6, 7)[u], [P, PACK, UNIT])
             for i in range(PACK):
-                back[c, i] = psum.tile([P, CHUNK], F32, name="bank%d%d" % (c, i))
                 nc.tensor.matmul_mx(
-                    out=back[c, i][:],
+                    out=back[u][:, i, :],
                     lhsT=eye_codes[:, i * P : (i + 1) * P].bitcast(E4M3),
                     lhsT_scale=eye_scales[:, i * P : (i + 1) * P],
-                    rhs=hi_codes[c][:].bitcast(E5M2),
-                    rhs_scale=hi_scales[c][:],
+                    rhs=hi_codes[c][:, cols].bitcast(E5M2),
+                    rhs_scale=hi_scales[c][:, cols],
                     start=True,
                     stop=True,
                 )
 
-        def leftover(c, part):
-            a, b = PARTS[c][part]
-            for i in range(PACK):
-                nc.vector.tensor_tensor(
-                    lo_planes[c, a][:, i, :], dy_raw[c, a][:, i, :], back[c, i][:, a:b], ALU.subtract
+        def leftover(u):
+            first = max(a for a, b in LO_RUNS if a <= u)
+            dst = lo_in[first][:, (u - first) * UNIT : (u - first + 1) * UNIT, :]
+            nc.vector.tensor_tensor(
+                dst.rearrange("p (c e) i -> p c i e", e=2),
+                dy_unit[u].rearrange("p i (c e) -> p c i e", e=2),
+                back[u][:].rearrange("p i (c e) -> p c i e", e=2),
+                ALU.subtract,
+            )
+
+        def second_tier(run):
+            a, b = LO_RUNS[run]
+            c, cols = a // 4, slice((a % 4) * UNIT, (a % 4 + b - a) * UNIT)
+            nc.vector.quantize_mx(
+                out=lo_codes[c][:, cols].bitcast(E4M3),
+                scales=lo_scales[c][:, cols],
+                in_=lo_in[a][:].rearrange("p j i -> p (j i)"),
+            )
+
+        plain, total = {}, {}
+
+        def product(b, c, index, a, z):
+            dx = bank("dx%d%d_%d" % (b, c, a), index, [P, z - a])
+            for codes, scales, fmt, first in (
+                (hi_codes, hi_scales, E5M2, True),
+                (lo_codes, lo_scales, E4M3, False),
+            ):
+                nc.tensor.matmul_mx(
+                    out=dx[:],
+                    lhsT=w_raw[:, 2 * P * b : 2 * P * (b + 1)].bitcast(E2M1),
+                    lhsT_scale=ws_raw[:, P * b : P * (b + 1)],
+                    rhs=codes[c][:, a:z].bitcast(fmt),
+                    rhs_scale=scales[c][:, a:z],
+                    start=first,
+                    stop=not first,
                 )
+            plain[b, c, a] = sb("plain%d%d_%d" % (b, c, a), [P, z - a], F32)
+            nc.scalar.copy(plain[b, c, a][:], dx[:])
 
-        w_codes = held.tile([P, PACK, 2 * P], U8, name="w_codes", align_bytes=64)
-        w_sc = held.tile([P, PACK, P], U8, name="w_sc", align_bytes=64)
-        dx = {}
+        def combine(b, c, a, z, tag):
+            both = sb("both", [P, z - a], F32, tag=tag)
+            if a == 0:
+                total[b, c] = sb("total%d%d" % (b, c), [P, CHUNK], F32)
+            nc.gpsimd.tensor_tensor(both[:], plain[b, c, a][:], res_sb[b, c][:, a:z], ALU.add)
+            nc.gpsimd.tensor_tensor(total[b, c][:, a:z], both[:], gate[c][:, a:z], ALU.mult)
 
-        def product(i, c, codes, scales, fmt, first):
-            if first:
-                dx[i, c] = psum.tile([P, CHUNK], F32, name="bank%d%d" % (c, i))
-            nc.tensor.matmul_mx(
-                out=dx[i, c][:],
-                lhsT=w_codes[:, i, :].bitcast(E2M1),
-                lhsT_scale=w_sc[:, i, :],
-                rhs=codes[c][:].bitcast(fmt),
-                rhs_scale=scales[c][:],
-                start=first,
-                stop=not first,
-            )
-
-        def clear_late(i, tag):
-            window[i] = held.tile([P, T], F32, name="window%d" % i, tag=tag, align_bytes=64)
-            nc.gpsimd.memset(window[i][:], 0.0)
-
-        total = {}
-
-        def combine(i, c):
-            weight = gate[:, c * CHUNK : (c + 1) * CHUNK]
-            if (i, c) == (0, 0):
-                both = held.tile([P, CHUNK], F32, name="both00")
-                total[i, c] = held.tile([P, CHUNK], F32, name="total00", tag="total00", align_bytes=64)
-                nc.vector.tensor_tensor(both[:], dx[i, c][:], res_sb[i, c][:], ALU.add)
-                nc.vector.tensor_tensor(total[i, c][:], both[:], weight, ALU.mult)
-            else:
-                both = held.tile([P, CHUNK], F32, name="both", tag="lo_in1_%d" % HALF, align_bytes=64)
-                total[i, c] = ring.tile([P, CHUNK], F32, name="total", bufs=4)
-                late = {(1, 0): "lo_planes1_%d" % HALF, (2, 0): "lo_in1_0", (3, 0): "total00"}
-                name = "plain%d%d" % (i, c)
-                plain = held.tile([P, CHUNK], F32, name=name, tag=late.get((i, c), name), align_bytes=64)
-                nc.scalar.copy(plain[:], dx[i, c][:])
-                nc.gpsimd.tensor_tensor(both[:], plain[:], res_sb[i, c][:], ALU.add)
-                nc.gpsimd.tensor_tensor(total[i, c][:], both[:], weight, ALU.mult)
-
-        def place(i, c):
+        def place(b, c):
             nc.vector.tensor_copy(
-                window[i][:].indirect(offsets[:, c * (CHUNK // 16) : (c + 1) * (CHUNK // 16)]),
-                total[i, c][:],
+                window[b][:].indirect(offsets[:, c * (CHUNK // 16) : (c + 1) * (CHUNK // 16)]),
+                total[b, c][:],
             )
 
-        weave(nc.vector.tensor_copy, hi_in[0, 0][:], dy_raw[0, 0][:])
-        quantize_hi(0, 0)
-        weave(nc.vector.tensor_copy, hi_in[0, HALF][:], dy_raw[0, HALF][:])
-        quantize_hi(0, 1)
-        dequantize_hi(0)
-        nc.vector.tensor_copy(
-            w_codes[:].rearrange("p i (m b) -> p i m b", b=2),
-            w_raw[:].rearrange("p (m i b) -> p i m b", i=PACK, b=2),
-        )
-        nc.vector.tensor_copy(w_sc[:], ws_raw[:].rearrange("p (m i) -> p i m", i=PACK))
-        clear_late(2, "ws_raw")
-        weave(nc.scalar.copy, hi_in[1, 0][:], dy_raw[1, 0][:])
-        weave(nc.scalar.copy, hi_in[1, HALF][:], dy_raw[1, HALF][:])
-        leftover(0, 0)
-        weave(nc.scalar.copy, lo_in[0, 0][:], lo_planes[0, 0][:])
-        leftover(0, 1)
-        for i in range(PACK):
-            product(i, 0, hi_codes, hi_scales, E5M2, True)
-        quantize_hi(1, 0)
-        quantize_hi(1, 1)
-        dequantize_hi(1)
-        weave(nc.vector.tensor_copy, lo_in[0, HALF][:], lo_planes[0, HALF][:])
-        quantize_lo(0, 0)
-        quantize_lo(0, 1)
-        clear_late(3, "lo_in0_%d" % HALF)
-        for i in range(PACK):
-            product(i, 0, lo_codes, lo_scales, E4M3, False)
-        leftover(1, 0)
-        weave(nc.scalar.copy, lo_in[1, 0][:], lo_planes[1, 0][:])
-        leftover(1, 1)
-        weave(nc.scalar.copy, lo_in[1, HALF][:], lo_planes[1, HALF][:])
-        combine(0, 0)
-        quantize_lo(1, 0)
-        quantize_lo(1, 1)
+        y_scales = sb("y_scales", [P, QUARTER], U8)
+
+        def turn(b, m, copy):
+            turned = bank("turned%d%d" % (b, m), m, [P, 4, P])
+            for q in range(4):
+                a = q * QUARTER + m * P
+                nc.tensor.transpose(turned[:, q, :], window[b][:, a : a + P], ident[:])
+            pairs = sb("pairs%d%d" % (b, m), [P, 2, P, 2], BF16, tag="pairs%d" % m)
+            copy(pairs[:], turned[:].rearrange("p q (r u e) -> p u (q r) e", u=2, e=2))
+            return pairs
+
+        def turn_back(pairs, dst):
+            words = pairs[:].rearrange("p u g e -> p (u g e)").bitcast(F32)
+            for u in range(2):
+                nc.tensor.transpose(dst[:, u, :], words[:, u * P : (u + 1) * P], ident[:])
+
+        def store_codes(b, codes):
+            rows = out_1[0, 32 * b : 32 * (b + 1)].rearrange("r (q c) i -> q r (c i)", q=4)
+            nc.sync.dma_start(rows.bitcast(I32), codes[:].bitcast(I32))
+
+        def planes(b, y_tag):
+            nc.sync.dma_start(out_0[b * P : (b + 1) * P, :], window[b][:])
+            y_in = sb("y_in%d" % b, [P, QUARTER, 2], F32)
+            for h in range(2):
+                pairs = [turn(b, 2 * h + s, nc.scalar.copy) for s in range(2)]
+                again = bank("again%d%d" % (b, h), 4 + h, [P, 2, 2, P])
+                for s in range(2):
+                    turn_back(pairs[s], again[:, s])
+                nc.scalar.copy(
+                    y_in[:, 2 * h * P : 2 * (h + 1) * P, :].rearrange("p (s t) u -> p s t u", s=2),
+                    again[:].rearrange("p s u t -> p s t u"),
+                )
+            return y_in
+
+        def quantize_planes(b, y_in, y_tag):
+            codes = sb("y_codes%d" % b, [P, QUARTER], U32, tag=y_tag)
+            nc.vector.quantize_mx(
+                out=codes[:].bitcast(E4M3),
+                scales=y_scales[4 * b : P, :],
+                in_=y_in[:].rearrange("p t u -> p (t u)").bitcast(BF16),
+            )
+            store_codes(b, codes)
+
+        for u in range(UNITS):
+            weave(u)
+            first_tier(u)
+            if 1 <= u <= 4:
+                leftover(u - 1)
+            if u in (3, 5):
+                half = (u - 3) // 2
+                second_tier(half)
+                product(0, 0, 3 + half, half * HALF, (half + 1) * HALF)
+                combine(0, 0, half * HALF, (half + 1) * HALF, "both")
+        for u in range(4, UNITS):
+            leftover(u)
+        product(1, 0, 5, 0, CHUNK)
+        second_tier(2)
+        second_tier(3)
+        for number in range(2, 8):
+            product(ORDER[number][0], ORDER[number][1], 3 + (number + 1) % 5, 0, CHUNK)
+
+        y_in = {}
         place(0, 0)
-        for i, c in ORDER[1:]:
-            if c == 1:
-                product(i, 1, hi_codes, hi_scales, E5M2, True)
-                product(i, 1, lo_codes, lo_scales, E4M3, False)
-            combine(i, c)
-            place(i, c)
+        for number in range(1, 8):
+            b, c = ORDER[number]
+            combine(b, c, 0, CHUNK, "lo_in7")
+            if number == 2:
+                window[2] = sb("window2", [P, T], F32, tag="plain01_0")
+                nc.gpsimd.memset(window[2][:], 0.0)
+            if number == 6:
+                window[3] = window[0]
+            if number == 7:
+                for d in range(2):
+                    quantize_planes(d, y_in[d], "plain3%d_0" % d)
+            place(b, c)
+            if c == 1 and b < 3:
+                y_in[b] = planes(b, None)
+        quantize_planes(2, y_in[2], "total31")
 
-        spans = [(2 * CHUNK, 3 * CHUNK), (3 * CHUNK, T - HALF), (0, CHUNK), (CHUNK, 2 * CHUNK), (T - HALF, T)]
-        y_in = [
-            held.tile([P, b - a, PACK], BF16, name="y_in%d" % g, tag="y_in%d" % g, align_bytes=64)
-            for g, (a, b) in enumerate(spans)
-        ]
-        y_scales = held.tile([P, T], U8, name="y_scales", align_bytes=64)
-
-        one = held.tile([P, 1], F32, name="one", tag="lo_in1_%d" % HALF, align_bytes=64)
-        nc.gpsimd.memset(one[:], 1.0)
-
-        def round_gpsimd(dst, src):
-            nc.gpsimd.tensor_scalar(dst, src, one[:], 0.0, ALU.mult, ALU.add)
-
-        for i in range(PACK):
-            nc.sync.dma_start(out_v[:, i, :], window[i][:])
-            for g, (a, b) in enumerate(spans):
-                src = window[i][:, a:b]
-                if i == 2 and g != 2:
-                    round_gpsimd(y_in[g][:, :, 2:4], src.unsqueeze(2).to_broadcast([P, b - a, 2]))
-                elif i == 3 and g < 2:
-                    nc.vector.tensor_copy(y_in[g][:, :, i], src)
-                else:
-                    nc.scalar.copy(y_in[g][:, :, i], src)
-
-        for g, (a, b) in enumerate(spans):
-            tag = "y_in%d" % (g - 2) if g >= 2 else "y_codes%d" % g
-            y_codes = held.tile([P, b - a], U32, name="y_codes%d" % g, tag=tag, align_bytes=64)
-            quantize(y_codes[:], y_scales[:, a:b], E4M3, y_in[g])
-            nc.sync.dma_start(codes_v[:, a:b], y_codes[:].bitcast(I32))
+        b = 3
+        nc.sync.dma_start(out_0[b * P : (b + 1) * P, :], window[b][:])
+        codes = sb("y_codes3", [P, QUARTER], U32)
+        pairs = [turn(b, m, nc.vector.tensor_copy if m % 2 else nc.scalar.copy) for m in range(4)]
+        for m in range(4):
+            again = bank("again3%d" % m, 4 + m, [P, 2, P])
+            turn_back(pairs[m], again)
+            last = sb("last%d" % m, [P, P, 2], F32)
+            copy = nc.vector.tensor_copy if m % 2 else nc.scalar.copy
+            copy(last[:], again[:].rearrange("p u t -> p t u"))
+            nc.vector.quantize_mx(
+                out=codes[:, m * P : (m + 1) * P].bitcast(E4M3),
+                scales=y_scales[4 * b : P, m * P : (m + 1) * P],
+                in_=last[:].rearrange("p t u -> p (t u)").bitcast(BF16),
+            )
         for q in range(4):
-            queue = nc.scalar if q % 2 else nc.sync
-            queue.dma_start(scales_v[4 * q : 4 * q + 4, :], y_scales[32 * q : 32 * q + 4, :].bitcast(I32))
+            first, second = (nc.sync, nc.scalar) if q % 2 else (nc.scalar, nc.sync)
+            rows = out_1[0, 32 * b : 32 * (b + 1), q * QUARTER : (q + 1) * QUARTER, :]
+            first.dma_start(
+                rows.rearrange("r c i -> r (c i)").bitcast(I32),
+                codes[32 * q : 32 * (q + 1), :].bitcast(I32),
+            )
+            second.dma_start(
+                out_2[0, :, q * QUARTER : (q + 1) * QUARTER].bitcast(I32),
+                y_scales[32 * q : 32 * q + 16, :].bitcast(I32),
+            )

@@ -33,6 +33,10 @@ def tile_list_embg_tgq4_resP_kernel(
 ):
     nc = tc.nc
     dy_v = dy.rearrange("(p i) j -> p i j", i=PACK)
+    res_v = res.rearrange("(p i) j -> p i j", i=PACK)
+    out_v = out_0.rearrange("(p i) t -> p i t", i=PACK)
+    codes_v = out_1[0].rearrange("p t i -> p (t i)").bitcast(I32)
+    scales_v = out_2[0].bitcast(I32)
 
     with ExitStack() as ctx:
         held = ctx.enter_context(tc.tile_pool(name="held", bufs=1))
@@ -55,18 +59,18 @@ def tile_list_embg_tgq4_resP_kernel(
             nc.sync.dma_start(raw[:], dy_v[:, :, a * UNIT : b * UNIT])
             for u in range(a, b):
                 dy_unit[u] = raw[:, :, (u - a) * UNIT : (u - a + 1) * UNIT]
-            if a == 2:
+            if a == 0:
+                nc.sync.dma_start(w_raw[:].bitcast(I32), w_words[0].bitcast(I32))
                 for q in range(4):
                     nc.sync.dma_start(
                         ws_raw[32 * q : 32 * q + 4, :].bitcast(I32),
                         w_scales[0, 4 * q : 4 * q + 4, :].bitcast(I32),
                     )
-        nc.sync.dma_start(w_raw[:].bitcast(I32), w_words[0].bitcast(I32))
         res_sb = {}
 
         def load_res(b, c):
             res_sb[b, c] = sb("res%d%d" % (b, c), [P, CHUNK], F32)
-            nc.sync.dma_start(res_sb[b, c][:], res[b * P : (b + 1) * P, c * CHUNK : (c + 1) * CHUNK])
+            nc.sync.dma_start(res_sb[b, c][:], res_v[:, b, c * CHUNK : (c + 1) * CHUNK])
 
         load_res(0, 0)
         nc.sync.dma_start(gate[0][:], wgo[:, 0:CHUNK])
@@ -91,8 +95,6 @@ def tile_list_embg_tgq4_resP_kernel(
         eye = sb("eye", [P, PACK, K], BF16, tag="hi_in0")
         for i in range(PACK):
             nc.scalar.copy(eye[:, i, :], diag[:, PACK - 1 - i : PACK - 1 - i + K])
-        ident = sb("ident", [P, P], F32)
-        nc.scalar.copy(ident[:], diag[:, PACK - 1 : PACK - 1 + K : PACK])
 
         window = {}
         for b in range(2):
@@ -165,7 +167,18 @@ def tile_list_embg_tgq4_resP_kernel(
                 in_=lo_in[a][:].rearrange("p j i -> p (j i)"),
             )
 
-        plain, total = {}, {}
+        plain, total, dealt = {}, {}, {}
+
+        def deal_codes():
+            dealt["codes"] = sb("w_codes", [P, PACK, 2 * P], U8, tag="hi_in0")
+            nc.vector.tensor_copy(
+                dealt["codes"][:].rearrange("p i (m b) -> p i m b", b=2),
+                w_raw[:].rearrange("p (m i b) -> p i m b", i=PACK, b=2),
+            )
+
+        def deal_scales():
+            dealt["scales"] = sb("w_sc", [P, PACK, P], U8, tag="dy0")
+            nc.vector.tensor_copy(dealt["scales"][:], ws_raw[:].rearrange("p (m i) -> p i m", i=PACK))
 
         def product(b, c, index, a, z):
             dx = bank("dx%d%d_%d" % (b, c, a), index, [P, z - a])
@@ -175,8 +188,8 @@ def tile_list_embg_tgq4_resP_kernel(
             ):
                 nc.tensor.matmul_mx(
                     out=dx[:],
-                    lhsT=w_raw[:, 2 * P * b : 2 * P * (b + 1)].bitcast(E2M1),
-                    lhsT_scale=ws_raw[:, P * b : P * (b + 1)],
+                    lhsT=dealt["codes"][:, b, :].bitcast(E2M1),
+                    lhsT_scale=dealt["scales"][:, b, :],
                     rhs=codes[c][:, a:z].bitcast(fmt),
                     rhs_scale=scales[c][:, a:z],
                     start=first,
@@ -198,54 +211,15 @@ def tile_list_embg_tgq4_resP_kernel(
                 total[b, c][:],
             )
 
-        y_scales = sb("y_scales", [P, QUARTER], U8)
-
-        def turn(b, m, copy):
-            turned = bank("turned%d%d" % (b, m), m, [P, 4, P])
-            for q in range(4):
-                a = q * QUARTER + m * P
-                nc.tensor.transpose(turned[:, q, :], window[b][:, a : a + P], ident[:])
-            pairs = sb("pairs%d%d" % (b, m), [P, 2, P, 2], BF16, tag="pairs%d" % m)
-            copy(pairs[:], turned[:].rearrange("p q (r u e) -> p u (q r) e", u=2, e=2))
-            return pairs
-
-        def turn_back(pairs, dst):
-            words = pairs[:].rearrange("p u g e -> p (u g e)").bitcast(F32)
-            for u in range(2):
-                nc.tensor.transpose(dst[:, u, :], words[:, u * P : (u + 1) * P], ident[:])
-
-        def store_codes(b, codes):
-            rows = out_1[0, 32 * b : 32 * (b + 1)].rearrange("r (q c) i -> q r (c i)", q=4)
-            nc.sync.dma_start(rows.bitcast(I32), codes[:].bitcast(I32))
-
-        def planes(b, y_tag):
-            nc.sync.dma_start(out_0[b * P : (b + 1) * P, :], window[b][:])
-            y_in = sb("y_in%d" % b, [P, QUARTER, 2], F32)
-            for h in range(2):
-                pairs = [turn(b, 2 * h + s, nc.scalar.copy) for s in range(2)]
-                again = bank("again%d%d" % (b, h), 4 + h, [P, 2, 2, P])
-                for s in range(2):
-                    turn_back(pairs[s], again[:, s])
-                nc.scalar.copy(
-                    y_in[:, 2 * h * P : 2 * (h + 1) * P, :].rearrange("p (s t) u -> p s t u", s=2),
-                    again[:].rearrange("p s u t -> p s t u"),
-                )
-            return y_in
-
-        def quantize_planes(b, y_in, y_tag):
-            codes = sb("y_codes%d" % b, [P, QUARTER], U32, tag=y_tag)
-            nc.vector.quantize_mx(
-                out=codes[:].bitcast(E4M3),
-                scales=y_scales[4 * b : P, :],
-                in_=y_in[:].rearrange("p t u -> p (t u)").bitcast(BF16),
-            )
-            store_codes(b, codes)
-
         for u in range(UNITS):
             weave(u)
             first_tier(u)
+            if u == 0:
+                deal_codes()
             if 1 <= u <= 4:
                 leftover(u - 1)
+            if u == 1:
+                deal_scales()
             if u in (3, 5):
                 half = (u - 3) // 2
                 second_tier(half)
@@ -259,7 +233,31 @@ def tile_list_embg_tgq4_resP_kernel(
         for number in range(2, 8):
             product(ORDER[number][0], ORDER[number][1], 3 + (number + 1) % 5, 0, CHUNK)
 
-        y_in = {}
+        spans = [(2 * CHUNK, 3 * CHUNK), (3 * CHUNK, T - HALF), (0, CHUNK), (CHUNK, 2 * CHUNK), (T - HALF, T)]
+        y_in = [sb("y_in%d" % g, [P, b - a, PACK], BF16) for g, (a, b) in enumerate(spans)]
+        y_scales = sb("y_scales", [P, T], U8)
+
+        def finish(i):
+            nc.sync.dma_start(out_v[:, i, :], window[i][:])
+            if i == 2:
+                one = sb("one", [P, 1], F32, tag="lo_in7")
+                nc.gpsimd.memset(one[:], 1.0)
+            for g, (a, b) in enumerate(spans):
+                src = window[i][:, a:b]
+                if i == 2 and g != 2:
+                    nc.gpsimd.tensor_scalar(
+                        y_in[g][:, :, 2:4],
+                        src.unsqueeze(2).to_broadcast([P, b - a, 2]),
+                        one[:],
+                        0.0,
+                        ALU.mult,
+                        ALU.add,
+                    )
+                elif i == 3 and g < 2:
+                    nc.vector.tensor_copy(y_in[g][:, :, i], src)
+                else:
+                    nc.scalar.copy(y_in[g][:, :, i], src)
+
         place(0, 0)
         for number in range(1, 8):
             b, c = ORDER[number]
@@ -269,37 +267,21 @@ def tile_list_embg_tgq4_resP_kernel(
                 nc.gpsimd.memset(window[2][:], 0.0)
             if number == 6:
                 window[3] = window[0]
-            if number == 7:
-                for d in range(2):
-                    quantize_planes(d, y_in[d], "plain3%d_0" % d)
             place(b, c)
-            if c == 1 and b < 3:
-                y_in[b] = planes(b, None)
-        quantize_planes(2, y_in[2], "total31")
+            if number in (2, 3):
+                finish(b)
+        finish(2)
+        finish(3)
 
-        b = 3
-        nc.sync.dma_start(out_0[b * P : (b + 1) * P, :], window[b][:])
-        codes = sb("y_codes3", [P, QUARTER], U32)
-        pairs = [turn(b, m, nc.vector.tensor_copy if m % 2 else nc.scalar.copy) for m in range(4)]
-        for m in range(4):
-            again = bank("again3%d" % m, 4 + m, [P, 2, P])
-            turn_back(pairs[m], again)
-            last = sb("last%d" % m, [P, P, 2], F32)
-            copy = nc.vector.tensor_copy if m % 2 else nc.scalar.copy
-            copy(last[:], again[:].rearrange("p u t -> p t u"))
+        for g, (a, b) in enumerate(spans):
+            tag = "y_in%d" % (g - 2) if g >= 2 else "y_codes%d" % g
+            y_codes = sb("y_codes%d" % g, [P, b - a], U32, tag=tag)
             nc.vector.quantize_mx(
-                out=codes[:, m * P : (m + 1) * P].bitcast(E4M3),
-                scales=y_scales[4 * b : P, m * P : (m + 1) * P],
-                in_=last[:].rearrange("p t u -> p (t u)").bitcast(BF16),
+                out=y_codes[:].bitcast(E4M3),
+                scales=y_scales[:, a:b],
+                in_=y_in[g][:].rearrange("p j i -> p (j i)"),
             )
+            nc.sync.dma_start(codes_v[:, a:b], y_codes[:].bitcast(I32))
         for q in range(4):
-            first, second = (nc.sync, nc.scalar) if q % 2 else (nc.scalar, nc.sync)
-            rows = out_1[0, 32 * b : 32 * (b + 1), q * QUARTER : (q + 1) * QUARTER, :]
-            first.dma_start(
-                rows.rearrange("r c i -> r (c i)").bitcast(I32),
-                codes[32 * q : 32 * (q + 1), :].bitcast(I32),
-            )
-            second.dma_start(
-                out_2[0, :, q * QUARTER : (q + 1) * QUARTER].bitcast(I32),
-                y_scales[32 * q : 32 * q + 16, :].bitcast(I32),
-            )
+            queue = nc.scalar if q % 2 else nc.sync
+            queue.dma_start(scales_v[4 * q : 4 * q + 4, :], y_scales[32 * q : 32 * q + 4, :].bitcast(I32))

@@ -25,7 +25,8 @@ HALF = CHUNK // 2
 QUARTER = T // 4
 LOADS = [(0, 1), (1, 2), (2, 4), (4, 6), (6, 8)]
 LO_RUNS = [(0, 2), (2, 4), (4, 7), (7, 8)]
-ORDER = [(0, 0), (1, 0), (0, 1), (1, 1), (2, 0), (2, 1), (3, 0), (3, 1)]
+ORDER = [(b, c) for b in range(PACK) for c in range(2)]
+SPANS = [(0, 512), (512, 896), (896, 1408), (1408, 1792), (1792, 2048)]
 
 
 def tile_list_embg_tgq4_resP_kernel(
@@ -81,7 +82,7 @@ def tile_list_embg_tgq4_resP_kernel(
         for b, c in ORDER[3:]:
             load_res(b, c)
 
-        diag = sb("diag", [P, K + PACK], BF16, tag="hi_in1")
+        diag = sb("diag", [P, K + PACK], BF16, tag="hi_in0")
         nc.gpsimd.memset(diag[:], 0.0)
         nc.gpsimd.affine_select(
             out=diag[:],
@@ -92,14 +93,18 @@ def tile_list_embg_tgq4_resP_kernel(
             pattern=[[1, K + PACK]],
             channel_multiplier=-PACK,
         )
-        eye = sb("eye", [P, PACK, K], BF16, tag="hi_in0")
+        eye = sb("eye", [P, PACK, K], BF16, tag="hi_in1")
         for i in range(PACK):
             nc.scalar.copy(eye[:, i, :], diag[:, PACK - 1 - i : PACK - 1 - i + K])
 
         window = {}
         for b in range(2):
-            window[b] = sb("window%d" % b, [P, T], F32)
-            nc.vector.memset(window[b][:], 0.0)
+            window[b] = window[b + 2] = sb("window%d" % b, [P, T], F32)
+        for a, z in ((0, 767), (768, T), (767, 768)):
+            nc.vector.memset(window[0][:, a:z], 0.0)
+        nc.vector.memset(window[1][:], 0.0)
+        one = sb("one", [P, 1], F32)
+        nc.gpsimd.memset(one[:], 1.0)
 
         eye_codes = sb("eye_codes", [P, K], U32)
         eye_scales = sb("eye_scales", [P, K], U8)
@@ -123,8 +128,7 @@ def tile_list_embg_tgq4_resP_kernel(
 
         def weave(u):
             hi_in[u] = hi_rest[:, (u - 1) * UNIT : u * UNIT, :] if u else hi_first[:]
-            copy = nc.scalar.copy if u else nc.vector.tensor_copy
-            copy(
+            nc.scalar.copy(
                 hi_in[u].rearrange("p (c e) i -> p c i e", e=4),
                 dy_unit[u].rearrange("p i (c e) -> p c i e", e=4),
             )
@@ -201,14 +205,15 @@ def tile_list_embg_tgq4_resP_kernel(
         def combine(b, c, a, z, tag):
             both = sb("both", [P, z - a], F32, tag=tag)
             if a == 0:
-                total[b, c] = sb("total%d%d" % (b, c), [P, CHUNK], F32)
+                tag = "plain01_%d" % HALF if (b, c) == (1, 0) else None
+                total[b, c] = sb("total%d%d" % (b, c), [P, CHUNK], F32, tag=tag)
             nc.gpsimd.tensor_tensor(both[:], plain[b, c, a][:], res_sb[b, c][:, a:z], ALU.add)
             nc.gpsimd.tensor_tensor(total[b, c][:, a:z], both[:], gate[c][:, a:z], ALU.mult)
 
-        def place(b, c):
+        def place(b, c, a, z):
             nc.vector.tensor_copy(
-                window[b][:].indirect(offsets[:, c * (CHUNK // 16) : (c + 1) * (CHUNK // 16)]),
-                total[b, c][:],
+                window[b][:].indirect(offsets[:, (c * CHUNK + a) // 16 : (c * CHUNK + z) // 16]),
+                total[b, c][:, a:z],
             )
 
         for u in range(UNITS):
@@ -224,56 +229,49 @@ def tile_list_embg_tgq4_resP_kernel(
                 half = (u - 3) // 2
                 second_tier(half)
                 product(0, 0, 3 + half, half * HALF, (half + 1) * HALF)
-                combine(0, 0, half * HALF, (half + 1) * HALF, "both")
+        for half in range(2):
+            combine(0, 0, half * HALF, (half + 1) * HALF, "hi_in1")
         for u in range(4, UNITS):
             leftover(u)
         product(1, 0, 5, 0, CHUNK)
         second_tier(2)
         second_tier(3)
-        for number in range(2, 8):
-            product(ORDER[number][0], ORDER[number][1], 3 + (number + 1) % 5, 0, CHUNK)
+        for half in range(2):
+            product(0, 1, 6 + half, half * HALF, (half + 1) * HALF)
+        for number in range(3, 8):
+            product(ORDER[number][0], ORDER[number][1], 3 + number % 5, 0, CHUNK)
 
-        spans = [(2 * CHUNK, 3 * CHUNK), (3 * CHUNK, T - HALF), (0, CHUNK), (CHUNK, 2 * CHUNK), (T - HALF, T)]
-        y_in = [sb("y_in%d" % g, [P, b - a, PACK], BF16) for g, (a, b) in enumerate(spans)]
+        y_in = [sb("y_in%d" % g, [P, b - a, PACK], BF16) for g, (a, b) in enumerate(SPANS)]
         y_scales = sb("y_scales", [P, T], U8)
 
         def finish(i):
             nc.sync.dma_start(out_v[:, i, :], window[i][:])
-            if i == 2:
-                one = sb("one", [P, 1], F32, tag="lo_in7")
-                nc.gpsimd.memset(one[:], 1.0)
-            for g, (a, b) in enumerate(spans):
+            for g, (a, b) in enumerate(SPANS):
                 src = window[i][:, a:b]
-                if i == 2 and g != 2:
-                    nc.gpsimd.tensor_scalar(
-                        y_in[g][:, :, 2:4],
-                        src.unsqueeze(2).to_broadcast([P, b - a, 2]),
-                        one[:],
-                        0.0,
-                        ALU.mult,
-                        ALU.add,
-                    )
+                dst = y_in[g][:, :, i]
+                if i == 2 and g < 2:
+                    src = src.unsqueeze(2).to_broadcast([P, b - a, 2])
+                    dst = y_in[g][:, :, 2:4]
+                if (i, g) in ((0, 4), (1, 4), (2, 0)):
+                    nc.gpsimd.tensor_scalar(dst, src, one[:], 0.0, ALU.mult, ALU.add)
                 elif i == 3 and g < 2:
-                    nc.vector.tensor_copy(y_in[g][:, :, i], src)
+                    nc.vector.tensor_copy(dst, src)
                 else:
-                    nc.scalar.copy(y_in[g][:, :, i], src)
+                    nc.scalar.copy(dst, src)
 
-        place(0, 0)
-        for number in range(1, 8):
-            b, c = ORDER[number]
-            combine(b, c, 0, CHUNK, "lo_in7")
-            if number == 2:
-                window[2] = sb("window2", [P, T], F32, tag="plain01_0")
-                nc.gpsimd.memset(window[2][:], 0.0)
-            if number == 6:
-                window[3] = window[0]
-            place(b, c)
-            if number in (2, 3):
-                finish(b)
-        finish(2)
+        place(0, 0, 0, CHUNK)
+        for half in range(2):
+            combine(0, 1, half * HALF, (half + 1) * HALF, "both")
+            place(0, 1, half * HALF, (half + 1) * HALF)
+        for b in range(1, PACK):
+            combine(b, 0, 0, CHUNK, "lo_in7")
+            place(b, 0, 0, CHUNK)
+            combine(b, 1, 0, CHUNK, "both")
+            finish(b - 1)
+            place(b, 1, 0, CHUNK)
         finish(3)
 
-        for g, (a, b) in enumerate(spans):
+        for g, (a, b) in enumerate(SPANS):
             tag = "y_in%d" % (g - 2) if g >= 2 else "y_codes%d" % g
             y_codes = sb("y_codes%d" % g, [P, b - a], U32, tag=tag)
             nc.vector.quantize_mx(

@@ -23,7 +23,7 @@ UNITS = J // UNIT
 CHUNK = 512
 HALF = CHUNK // 2
 QUARTER = T // 4
-LOADS = [(0, 1), (1, 2), (2, 4), (4, 6), (6, 8)]
+LOADS = [(0, 1), (1, 2), (2, 3), (3, 4), (4, 6), (6, 8)]
 LO_RUNS = [(0, 2), (2, 4), (4, 7), (7, 8)]
 ORDER = [(b, c) for b in range(PACK) for c in range(2)]
 SPANS = [(0, 512), (512, 896), (896, 1408), (1408, 1792), (1792, 2048)]
@@ -60,13 +60,12 @@ def tile_list_embg_tgq4_resP_kernel(
             nc.sync.dma_start(raw[:], dy_v[:, :, a * UNIT : b * UNIT])
             for u in range(a, b):
                 dy_unit[u] = raw[:, :, (u - a) * UNIT : (u - a + 1) * UNIT]
-            if a == 0:
-                nc.sync.dma_start(w_raw[:].bitcast(I32), w_words[0].bitcast(I32))
-                for q in range(4):
-                    nc.sync.dma_start(
-                        ws_raw[32 * q : 32 * q + 4, :].bitcast(I32),
-                        w_scales[0, 4 * q : 4 * q + 4, :].bitcast(I32),
-                    )
+        nc.sync.dma_start(w_raw[:].bitcast(I32), w_words[0].bitcast(I32))
+        for q in range(4):
+            nc.sync.dma_start(
+                ws_raw[32 * q : 32 * q + 4, :].bitcast(I32),
+                w_scales[0, 4 * q : 4 * q + 4, :].bitcast(I32),
+            )
         res_sb = {}
 
         def load_res(b, c):
@@ -76,10 +75,9 @@ def tile_list_embg_tgq4_resP_kernel(
         load_res(0, 0)
         nc.sync.dma_start(gate[0][:], wgo[:, 0:CHUNK])
         nc.sync.dma_start(offsets[:], offs)
-        load_res(1, 0)
         load_res(0, 1)
         nc.sync.dma_start(gate[1][:], wgo[:, CHUNK:J])
-        for b, c in ORDER[3:]:
+        for b, c in ORDER[2:]:
             load_res(b, c)
 
         diag = sb("diag", [P, K + PACK], BF16, tag="hi_in0")
@@ -99,12 +97,11 @@ def tile_list_embg_tgq4_resP_kernel(
 
         window = {}
         for b in range(2):
-            window[b] = window[b + 2] = sb("window%d" % b, [P, T], F32)
+            window[b] = sb("window%d" % b, [P, T], F32)
+        window[3] = window[0]
         for a, z in ((0, 767), (768, T), (767, 768)):
             nc.vector.memset(window[0][:, a:z], 0.0)
         nc.vector.memset(window[1][:], 0.0)
-        one = sb("one", [P, 1], F32)
-        nc.gpsimd.memset(one[:], 1.0)
 
         eye_codes = sb("eye_codes", [P, K], U32)
         eye_scales = sb("eye_scales", [P, K], U8)
@@ -140,6 +137,9 @@ def tile_list_embg_tgq4_resP_kernel(
                 scales=hi_scales[c][:, cols],
                 in_=hi_in[u].rearrange("p j i -> p (j i)"),
             )
+
+        def values(u):
+            c, cols = unit_cols(u)
             back[u] = bank("back%d" % u, (0, 1, 2, 0, 1, 2, 6, 7)[u], [P, PACK, UNIT])
             for i in range(PACK):
                 nc.tensor.matmul_mx(
@@ -174,14 +174,14 @@ def tile_list_embg_tgq4_resP_kernel(
         plain, total, dealt = {}, {}, {}
 
         def deal_codes():
-            dealt["codes"] = sb("w_codes", [P, PACK, 2 * P], U8, tag="hi_in0")
+            dealt["codes"] = sb("w_codes", [P, PACK, 2 * P], U8, tag="dy2")
             nc.vector.tensor_copy(
-                dealt["codes"][:].rearrange("p i (m b) -> p i m b", b=2),
-                w_raw[:].rearrange("p (m i b) -> p i m b", i=PACK, b=2),
+                dealt["codes"][:].bitcast(U16),
+                w_raw[:].bitcast(U16).rearrange("p (m i) -> p i m", i=PACK),
             )
 
         def deal_scales():
-            dealt["scales"] = sb("w_sc", [P, PACK, P], U8, tag="dy0")
+            dealt["scales"] = sb("w_sc", [P, PACK, P], U8, tag="dy3")
             nc.vector.tensor_copy(dealt["scales"][:], ws_raw[:].rearrange("p (m i) -> p i m", i=PACK))
 
         def product(b, c, index, a, z):
@@ -199,16 +199,22 @@ def tile_list_embg_tgq4_resP_kernel(
                     start=first,
                     stop=not first,
                 )
-            plain[b, c, a] = sb("plain%d%d_%d" % (b, c, a), [P, z - a], F32)
+            return dx
+
+        def empty(b, c, a, dx):
+            plain[b, c, a] = sb("plain%d%d_%d" % (b, c, a), dx.shape, F32)
             nc.scalar.copy(plain[b, c, a][:], dx[:])
 
-        def combine(b, c, a, z, tag):
-            both = sb("both", [P, z - a], F32, tag=tag)
+        def weigh(b, c, a, z, both):
             if a == 0:
-                tag = "plain01_%d" % HALF if (b, c) == (1, 0) else None
-                total[b, c] = sb("total%d%d" % (b, c), [P, CHUNK], F32, tag=tag)
+                total[b, c] = sb("total%d%d" % (b, c), [P, CHUNK], F32)
+            nc.gpsimd.tensor_tensor(total[b, c][:, a:z], both, gate[c][:, a:z], ALU.mult)
+
+        def combine(b, c, a, z, step, tag):
+            both = sb("both", [P, z - a], F32, tag=tag)
             nc.gpsimd.tensor_tensor(both[:], plain[b, c, a][:], res_sb[b, c][:, a:z], ALU.add)
-            nc.gpsimd.tensor_tensor(total[b, c][:, a:z], both[:], gate[c][:, a:z], ALU.mult)
+            for s in range(a, z, step):
+                weigh(b, c, s, s + step, both[:, s - a : s - a + step])
 
         def place(b, c, a, z):
             nc.vector.tensor_copy(
@@ -216,64 +222,78 @@ def tile_list_embg_tgq4_resP_kernel(
                 total[b, c][:, a:z],
             )
 
-        for u in range(UNITS):
+        def start(u):
             weave(u)
             first_tier(u)
-            if u == 0:
-                deal_codes()
-            if 1 <= u <= 4:
-                leftover(u - 1)
-            if u == 1:
-                deal_scales()
-            if u in (3, 5):
-                half = (u - 3) // 2
-                second_tier(half)
-                product(0, 0, 3 + half, half * HALF, (half + 1) * HALF)
-        for half in range(2):
-            combine(0, 0, half * HALF, (half + 1) * HALF, "hi_in1")
-        for u in range(4, UNITS):
+            values(u)
+
+        start(0)
+        for u in range(3):
+            start(u + 1)
             leftover(u)
-        product(1, 0, 5, 0, CHUNK)
+        second_tier(0)
+        leftover(3)
+        start(4)
+        start(5)
+        second_tier(1)
+        deal_codes()
+        deal_scales()
+        start(6)
+        leftover(4)
+        start(7)
+        empty(0, 0, 0, product(0, 0, 3, 0, HALF))
+        combine(0, 0, 0, HALF, HALF, "hi_in1")
+        own = product(0, 0, 4, HALF, CHUNK)
+        for u in range(5, UNITS):
+            leftover(u)
         second_tier(2)
         second_tier(3)
+        both = sb("both_own", [P, HALF], F32, tag="lo_in4")
+        nc.vector.tensor_tensor(both[:], own[:], res_sb[0, 0][:, HALF:CHUNK], ALU.add)
+        weigh(0, 0, HALF, CHUNK, both[:])
+        for number in range(1, 8):
+            b, c = ORDER[number]
+            empty(b, c, 0, product(b, c, (6, 5, 7, 0, 1, 2, 3)[number - 1], 0, CHUNK))
+        window[2] = sb("window2", [P, T], F32, tag="hi_in0")
         for half in range(2):
-            product(0, 1, 6 + half, half * HALF, (half + 1) * HALF)
-        for number in range(3, 8):
-            product(ORDER[number][0], ORDER[number][1], 3 + number % 5, 0, CHUNK)
+            nc.vector.memset(window[2][:, half * J : (half + 1) * J], 0.0)
 
         y_in = [sb("y_in%d" % g, [P, b - a, PACK], BF16) for g, (a, b) in enumerate(SPANS)]
         y_scales = sb("y_scales", [P, T], U8)
 
         def finish(i):
             nc.sync.dma_start(out_v[:, i, :], window[i][:])
+            if i == 2:
+                one = sb("one", [P, 1], F32, tag="plain31_0")
+                nc.gpsimd.memset(one[:], 1.0)
             for g, (a, b) in enumerate(SPANS):
                 src = window[i][:, a:b]
                 dst = y_in[g][:, :, i]
-                if i == 2 and g < 2:
+                if i == 2 and g != 2:
                     src = src.unsqueeze(2).to_broadcast([P, b - a, 2])
                     dst = y_in[g][:, :, 2:4]
-                if (i, g) in ((0, 4), (1, 4), (2, 0)):
+                if i == 2 and g > 2:
                     nc.gpsimd.tensor_scalar(dst, src, one[:], 0.0, ALU.mult, ALU.add)
                 elif i == 3 and g < 2:
                     nc.vector.tensor_copy(dst, src)
                 else:
                     nc.scalar.copy(dst, src)
 
-        place(0, 0, 0, CHUNK)
         for half in range(2):
-            combine(0, 1, half * HALF, (half + 1) * HALF, "both")
+            place(0, 0, half * HALF, (half + 1) * HALF)
+        combine(0, 1, 0, CHUNK, HALF, "both")
+        for half in range(2):
             place(0, 1, half * HALF, (half + 1) * HALF)
         for b in range(1, PACK):
-            combine(b, 0, 0, CHUNK, "lo_in7")
+            combine(b, 0, 0, CHUNK, CHUNK, "plain%d1_0" % (b - 1))
             place(b, 0, 0, CHUNK)
-            combine(b, 1, 0, CHUNK, "both")
+            combine(b, 1, 0, CHUNK, CHUNK, "plain%d0_0" % b)
             finish(b - 1)
             place(b, 1, 0, CHUNK)
         finish(3)
 
         for g, (a, b) in enumerate(SPANS):
-            tag = "y_in%d" % (g - 2) if g >= 2 else "y_codes%d" % g
-            y_codes = sb("y_codes%d" % g, [P, b - a], U32, tag=tag)
+            y_codes = sb("y_codes%d" % g, [P, b - a], U32)
             nc.vector.quantize_mx(
                 out=y_codes[:].bitcast(E4M3),
                 scales=y_scales[:, a:b],

@@ -23,7 +23,7 @@ UNITS = J // UNIT
 CHUNK = 512
 HALF = CHUNK // 2
 QUARTER = T // 4
-LOADS = [(0, 1), (1, 2), (2, 3), (3, 4), (4, 6), (6, 8)]
+LOADS = [(0, 1), (1, 2), (2, 4), (4, 6), (6, 8)]
 LO_RUNS = [(0, 2), (2, 4), (4, 7), (7, 8)]
 ORDER = [(b, c) for b in range(PACK) for c in range(2)]
 SPANS = [(0, 512), (512, 896), (896, 1408), (1408, 1792), (1792, 2048)]
@@ -60,12 +60,13 @@ def tile_list_embg_tgq4_resP_kernel(
             nc.sync.dma_start(raw[:], dy_v[:, :, a * UNIT : b * UNIT])
             for u in range(a, b):
                 dy_unit[u] = raw[:, :, (u - a) * UNIT : (u - a + 1) * UNIT]
-        nc.sync.dma_start(w_raw[:].bitcast(I32), w_words[0].bitcast(I32))
-        for q in range(4):
-            nc.sync.dma_start(
-                ws_raw[32 * q : 32 * q + 4, :].bitcast(I32),
-                w_scales[0, 4 * q : 4 * q + 4, :].bitcast(I32),
-            )
+            if a == 0:
+                nc.sync.dma_start(w_raw[:].bitcast(I32), w_words[0].bitcast(I32))
+                for q in range(4):
+                    nc.sync.dma_start(
+                        ws_raw[32 * q : 32 * q + 4, :].bitcast(I32),
+                        w_scales[0, 4 * q : 4 * q + 4, :].bitcast(I32),
+                    )
         res_sb = {}
 
         def load_res(b, c):
@@ -80,28 +81,29 @@ def tile_list_embg_tgq4_resP_kernel(
         for b, c in ORDER[2:]:
             load_res(b, c)
 
-        diag = sb("diag", [P, K + PACK], BF16, tag="hi_in0")
-        nc.gpsimd.memset(diag[:], 0.0)
+        diag = sb("diag", [P, K + PACK], BF16, tag="hi_in1")
+        ones = sb("ones", [P, K + PACK], BF16, tag="window1")
+        nc.gpsimd.memset(ones[:], 1.0)
         nc.gpsimd.affine_select(
             out=diag[:],
-            in_=diag[:],
-            compare_op=ALU.not_equal,
-            fill=1.0,
+            in_=ones[:],
+            compare_op=ALU.is_equal,
+            fill=0.0,
             base=-(PACK - 1),
             pattern=[[1, K + PACK]],
             channel_multiplier=-PACK,
         )
-        eye = sb("eye", [P, PACK, K], BF16, tag="hi_in1")
+        eye = sb("eye", [P, PACK, K], BF16, tag="hi_in0")
         for i in range(PACK):
             nc.scalar.copy(eye[:, i, :], diag[:, PACK - 1 - i : PACK - 1 - i + K])
 
         window = {}
         for b in range(2):
-            window[b] = sb("window%d" % b, [P, T], F32)
-        window[3] = window[0]
-        for a, z in ((0, 767), (768, T), (767, 768)):
-            nc.vector.memset(window[0][:, a:z], 0.0)
-        nc.vector.memset(window[1][:], 0.0)
+            window[b] = window[b + 2] = sb("window%d" % b, [P, T], F32)
+        for a, z in ((0, J - 1), (J - 1, T)):
+            nc.vector.memset(window[0][:, a:z].bitcast(I32), 0)
+        nc.gpsimd.memset(window[1][:, 0:1280].bitcast(I32), 0)
+        nc.vector.memset(window[1][:, 1280:T].bitcast(I32), 0)
 
         eye_codes = sb("eye_codes", [P, K], U32)
         eye_scales = sb("eye_scales", [P, K], U8)
@@ -125,7 +127,8 @@ def tile_list_embg_tgq4_resP_kernel(
 
         def weave(u):
             hi_in[u] = hi_rest[:, (u - 1) * UNIT : u * UNIT, :] if u else hi_first[:]
-            nc.scalar.copy(
+            copy = nc.scalar.copy if u else nc.vector.tensor_copy
+            copy(
                 hi_in[u].rearrange("p (c e) i -> p c i e", e=4),
                 dy_unit[u].rearrange("p i (c e) -> p c i e", e=4),
             )
@@ -174,14 +177,14 @@ def tile_list_embg_tgq4_resP_kernel(
         plain, total, dealt = {}, {}, {}
 
         def deal_codes():
-            dealt["codes"] = sb("w_codes", [P, PACK, 2 * P], U8, tag="dy2")
+            dealt["codes"] = sb("w_codes", [P, PACK, 2 * P], U8, tag="hi_in0")
             nc.vector.tensor_copy(
                 dealt["codes"][:].bitcast(U16),
                 w_raw[:].bitcast(U16).rearrange("p (m i) -> p i m", i=PACK),
             )
 
         def deal_scales():
-            dealt["scales"] = sb("w_sc", [P, PACK, P], U8, tag="dy3")
+            dealt["scales"] = sb("w_sc", [P, PACK, P], U8, tag="dy1")
             nc.vector.tensor_copy(dealt["scales"][:], ws_raw[:].rearrange("p (m i) -> p i m", i=PACK))
 
         def product(b, c, index, a, z):
@@ -228,16 +231,16 @@ def tile_list_embg_tgq4_resP_kernel(
             values(u)
 
         start(0)
+        deal_codes()
         for u in range(3):
             start(u + 1)
             leftover(u)
+        deal_scales()
         second_tier(0)
         leftover(3)
         start(4)
         start(5)
         second_tier(1)
-        deal_codes()
-        deal_scales()
         start(6)
         leftover(4)
         start(7)
@@ -254,29 +257,32 @@ def tile_list_embg_tgq4_resP_kernel(
         for number in range(1, 8):
             b, c = ORDER[number]
             empty(b, c, 0, product(b, c, (6, 5, 7, 0, 1, 2, 3)[number - 1], 0, CHUNK))
-        window[2] = sb("window2", [P, T], F32, tag="hi_in0")
-        for half in range(2):
-            nc.vector.memset(window[2][:, half * J : (half + 1) * J], 0.0)
 
         y_in = [sb("y_in%d" % g, [P, b - a, PACK], BF16) for g, (a, b) in enumerate(SPANS)]
         y_scales = sb("y_scales", [P, T], U8)
 
+        flat = sb("flat", [P, 2, T], BF16)
+
         def finish(i):
             nc.sync.dma_start(out_v[:, i, :], window[i][:])
+            if i < 2:
+                nc.scalar.copy(flat[:, i, :], window[i][:])
             if i == 2:
                 one = sb("one", [P, 1], F32, tag="plain31_0")
                 nc.gpsimd.memset(one[:], 1.0)
             for g, (a, b) in enumerate(SPANS):
                 src = window[i][:, a:b]
                 dst = y_in[g][:, :, i]
-                if i == 2 and g != 2:
+                if i == 1:
+                    nc.scalar.copy(y_in[g][:, :, 0:2], flat[:, :, a:b].rearrange("p e t -> p t e"))
+                if i == 2 and g < 4:
                     src = src.unsqueeze(2).to_broadcast([P, b - a, 2])
                     dst = y_in[g][:, :, 2:4]
-                if i == 2 and g > 2:
+                if i == 2 and g in (2, 3):
                     nc.gpsimd.tensor_scalar(dst, src, one[:], 0.0, ALU.mult, ALU.add)
                 elif i == 3 and g < 2:
                     nc.vector.tensor_copy(dst, src)
-                else:
+                elif i >= 2:
                     nc.scalar.copy(dst, src)
 
         for half in range(2):

@@ -52,7 +52,8 @@ def tile_list_embg_tgq4_resP_kernel(
         offsets = held.tile([P, J // 16], U16, name="offsets")
         w_raw = sb("w_raw", [P, 2 * N], U8)
         ws_raw = sb("ws_raw", [P, N], U8)
-        gate = [sb("gate%d" % c, [P, CHUNK], F32) for c in range(2)]
+        gates = sb("gates", [P, J], F32)
+        gate = [gates[:, c * CHUNK : (c + 1) * CHUNK] for c in range(2)]
         nc.gpsimd.memset(ws_raw[:].bitcast(I32), 0)
         dy_unit = {}
         for a, b in LOADS:
@@ -74,12 +75,14 @@ def tile_list_embg_tgq4_resP_kernel(
             nc.sync.dma_start(res_sb[b, c][:], res_v[:, b, c * CHUNK : (c + 1) * CHUNK])
 
         load_res(0, 0)
-        nc.sync.dma_start(gate[0][:], wgo[:, 0:CHUNK])
+        nc.sync.dma_start(gate[0], wgo[:, 0:CHUNK])
         nc.sync.dma_start(offsets[:], offs)
         load_res(0, 1)
-        nc.sync.dma_start(gate[1][:], wgo[:, CHUNK:J])
-        for b, c in ORDER[2:]:
+        nc.sync.dma_start(gate[1], wgo[:, CHUNK:J])
+        for b, c in ORDER[2:6]:
             load_res(b, c)
+        res_last = sb("res_last", [P, J], F32)
+        nc.sync.dma_start(res_last[:], res_v[:, 3, :])
 
         diag = sb("diag", [P, K + PACK], BF16, tag="hi_in1")
         ones = sb("ones", [P, K + PACK], BF16, tag="window1")
@@ -133,12 +136,13 @@ def tile_list_embg_tgq4_resP_kernel(
                 dy_unit[u].rearrange("p i (c e) -> p c i e", e=4),
             )
 
-        def first_tier(u):
-            c, cols = unit_cols(u)
+        def first_tier(a, b):
+            c, cols = a // 4, slice((a % 4) * UNIT, (a % 4 + b - a) * UNIT)
+            woven = hi_rest[:, (a - 1) * UNIT : (b - 1) * UNIT, :] if a else hi_first[:]
             nc.vector.quantize_mx(
                 out=hi_codes[c][:, cols].bitcast(E5M2),
                 scales=hi_scales[c][:, cols],
-                in_=hi_in[u].rearrange("p j i -> p (j i)"),
+                in_=woven.rearrange("p j i -> p (j i)"),
             )
 
         def values(u):
@@ -225,38 +229,48 @@ def tile_list_embg_tgq4_resP_kernel(
                 total[b, c][:, a:z],
             )
 
-        def start(u):
-            weave(u)
-            first_tier(u)
-            values(u)
+        def start(a, b):
+            for u in range(a, b):
+                weave(u)
+            first_tier(a, b)
+            for u in range(a, b):
+                values(u)
 
-        start(0)
+        start(0, 1)
         deal_codes()
         for u in range(3):
-            start(u + 1)
+            start(u + 1, u + 2)
             leftover(u)
         deal_scales()
         second_tier(0)
         leftover(3)
-        start(4)
-        start(5)
+        start(4, 6)
         second_tier(1)
-        start(6)
         leftover(4)
-        start(7)
-        empty(0, 0, 0, product(0, 0, 3, 0, HALF))
-        combine(0, 0, 0, HALF, HALF, "hi_in1")
-        own = product(0, 0, 4, HALF, CHUNK)
+        start(6, 8)
+        total[0, 0] = sb("total00", [P, HALF], F32)
+        sums = sb("sums", [P, CHUNK], F32, tag="hi_in1")
+        for a in (0, HALF):
+            empty(0, 0, a, product(0, 0, 3 + a // HALF, a, a + HALF))
+            nc.gpsimd.tensor_tensor(
+                sums[:, a : a + HALF], plain[0, 0, a][:], res_sb[0, 0][:, a : a + HALF], ALU.add
+            )
+        nc.gpsimd.tensor_tensor(total[0, 0][:], sums[:, 0:HALF], gate[0][:, 0:HALF], ALU.mult)
         for u in range(5, UNITS):
             leftover(u)
         second_tier(2)
         second_tier(3)
-        both = sb("both_own", [P, HALF], F32, tag="lo_in4")
-        nc.vector.tensor_tensor(both[:], own[:], res_sb[0, 0][:, HALF:CHUNK], ALU.add)
-        weigh(0, 0, HALF, CHUNK, both[:])
-        for number in range(1, 8):
+        second = sb("second", [P, HALF], F32, tag="lo_in7")
+        nc.gpsimd.tensor_tensor(second[:], sums[:, HALF:CHUNK], gate[0][:, HALF:CHUNK], ALU.mult)
+        plain[0, 1, 0] = sb("plain01_0", [P, CHUNK], F32)
+        for a in (0, HALF):
+            nc.scalar.copy(plain[0, 1, 0][:, a : a + HALF], product(0, 1, a // HALF, a, a + HALF)[:])
+        for number in range(2, 6):
             b, c = ORDER[number]
-            empty(b, c, 0, product(b, c, (6, 5, 7, 0, 1, 2, 3)[number - 1], 0, CHUNK))
+            empty(b, c, 0, product(b, c, (5, 7, 6, 2)[number - 2], 0, CHUNK))
+        plain_last = sb("plain_last", [P, J], F32)
+        for c in range(2):
+            nc.scalar.copy(plain_last[:, c * CHUNK : (c + 1) * CHUNK], product(3, c, 3 + c, 0, CHUNK)[:])
 
         y_in = [sb("y_in%d" % g, [P, b - a, PACK], BF16) for g, (a, b) in enumerate(SPANS)]
         y_scales = sb("y_scales", [P, T], U8)
@@ -268,7 +282,7 @@ def tile_list_embg_tgq4_resP_kernel(
             if i < 2:
                 nc.scalar.copy(flat[:, i, :], window[i][:])
             if i == 2:
-                one = sb("one", [P, 1], F32, tag="plain31_0")
+                one = sb("one", [P, 1], F32, tag="plain_last")
                 nc.gpsimd.memset(one[:], 1.0)
             for g, (a, b) in enumerate(SPANS):
                 src = window[i][:, a:b]
@@ -285,17 +299,23 @@ def tile_list_embg_tgq4_resP_kernel(
                 elif i >= 2:
                     nc.scalar.copy(dst, src)
 
-        for half in range(2):
-            place(0, 0, half * HALF, (half + 1) * HALF)
+        place(0, 0, 0, HALF)
+        nc.vector.tensor_copy(window[0][:].indirect(offsets[:, HALF // 16 : CHUNK // 16]), second[:])
         combine(0, 1, 0, CHUNK, HALF, "both")
         for half in range(2):
             place(0, 1, half * HALF, (half + 1) * HALF)
-        for b in range(1, PACK):
+        for b in range(1, PACK - 1):
             combine(b, 0, 0, CHUNK, CHUNK, "plain%d1_0" % (b - 1))
             place(b, 0, 0, CHUNK)
             combine(b, 1, 0, CHUNK, CHUNK, "plain%d0_0" % b)
             finish(b - 1)
             place(b, 1, 0, CHUNK)
+        last = sb("last", [P, J], F32)
+        both = sb("both", [P, J], F32, tag="plain21_0")
+        nc.gpsimd.tensor_tensor(both[:], plain_last[:], res_last[:], ALU.add)
+        nc.gpsimd.tensor_tensor(last[:], both[:], gates[:], ALU.mult)
+        finish(2)
+        nc.vector.tensor_copy(window[3][:].indirect(offsets[:]), last[:])
         finish(3)
 
         for g, (a, b) in enumerate(SPANS):

@@ -96,25 +96,27 @@ def tile_list_embg_tgq4_resP_kernel(
             pattern=[[1, K + PACK]],
             channel_multiplier=-PACK,
         )
-        eye = sb("eye", [P, PACK, K], BF16, tag="hi_in0")
+        eye = [sb("eye%d" % h, [P, 2, K], BF16, tag=("hi_in0", "w_codes")[h]) for h in range(2)]
         for i in range(PACK):
-            nc.scalar.copy(eye[:, i, :], diag[:, PACK - 1 - i : PACK - 1 - i + K])
+            nc.scalar.copy(eye[i // 2][:, i % 2, :], diag[:, PACK - 1 - i : PACK - 1 - i + K])
 
         window = {}
         for b in range(2):
             window[b] = window[b + 2] = sb("window%d" % b, [P, T], F32)
         for a, z in ((0, J - 1), (J - 1, T)):
             nc.vector.memset(window[0][:, a:z].bitcast(I32), 0)
-        nc.gpsimd.memset(window[1][:, 0:1280].bitcast(I32), 0)
-        nc.vector.memset(window[1][:, 1280:T].bitcast(I32), 0)
+        nc.gpsimd.memset(window[1][:, 0:1440].bitcast(I32), 0)
+        for a, z in ((1440, T - 1), (T - 1, T)):
+            nc.vector.memset(window[1][:, a:z].bitcast(I32), 0)
 
         eye_codes = sb("eye_codes", [P, K], U32)
         eye_scales = sb("eye_scales", [P, K], U8)
-        nc.vector.quantize_mx(
-            out=eye_codes[:].bitcast(E4M3),
-            scales=eye_scales[:],
-            in_=eye[:].rearrange("p i k -> p (i k)"),
-        )
+        for h in range(2):
+            nc.vector.quantize_mx(
+                out=eye_codes[:, h * HALF : (h + 1) * HALF].bitcast(E4M3),
+                scales=eye_scales[:, h * HALF : (h + 1) * HALF],
+                in_=eye[h][:].rearrange("p i k -> p (i k)"),
+            )
 
         hi_codes = [sb("hi_codes%d" % c, [P, CHUNK], U32) for c in range(2)]
         hi_scales = [sb("hi_scales%d" % c, [P, CHUNK], U8) for c in range(2)]
@@ -181,14 +183,14 @@ def tile_list_embg_tgq4_resP_kernel(
         plain, total, dealt = {}, {}, {}
 
         def deal_codes():
-            dealt["codes"] = sb("w_codes", [P, PACK, 2 * P], U8, tag="hi_in0")
+            dealt["codes"] = sb("w_codes", [P, PACK, 2 * P], U8)
             nc.vector.tensor_copy(
                 dealt["codes"][:].bitcast(U16),
                 w_raw[:].bitcast(U16).rearrange("p (m i) -> p i m", i=PACK),
             )
 
         def deal_scales():
-            dealt["scales"] = sb("w_sc", [P, PACK, P], U8, tag="dy1")
+            dealt["scales"] = sb("w_sc", [P, PACK, P], U8, tag="hi_in0")
             nc.vector.tensor_copy(dealt["scales"][:], ws_raw[:].rearrange("p (m i) -> p i m", i=PACK))
 
         def product(b, c, index, a, z):
@@ -238,39 +240,40 @@ def tile_list_embg_tgq4_resP_kernel(
 
         start(0, 1)
         deal_codes()
+        deal_scales()
         for u in range(3):
             start(u + 1, u + 2)
             leftover(u)
-        deal_scales()
         second_tier(0)
         leftover(3)
         start(4, 6)
         second_tier(1)
         leftover(4)
         start(6, 8)
-        total[0, 0] = sb("total00", [P, HALF], F32)
+        total[0, 0] = sb("total00", [P, CHUNK], F32)
         sums = sb("sums", [P, CHUNK], F32, tag="hi_in1")
         for a in (0, HALF):
             empty(0, 0, a, product(0, 0, 3 + a // HALF, a, a + HALF))
             nc.gpsimd.tensor_tensor(
                 sums[:, a : a + HALF], plain[0, 0, a][:], res_sb[0, 0][:, a : a + HALF], ALU.add
             )
-        nc.gpsimd.tensor_tensor(total[0, 0][:], sums[:, 0:HALF], gate[0][:, 0:HALF], ALU.mult)
+        nc.gpsimd.tensor_tensor(total[0, 0][:, 0:HALF], sums[:, 0:HALF], gate[0][:, 0:HALF], ALU.mult)
         for u in range(5, UNITS):
             leftover(u)
         second_tier(2)
+        nc.vector.tensor_tensor(
+            total[0, 0][:, HALF:CHUNK], sums[:, HALF:CHUNK], gate[0][:, HALF:CHUNK], ALU.mult
+        )
         second_tier(3)
-        second = sb("second", [P, HALF], F32, tag="lo_in7")
-        nc.gpsimd.tensor_tensor(second[:], sums[:, HALF:CHUNK], gate[0][:, HALF:CHUNK], ALU.mult)
         plain[0, 1, 0] = sb("plain01_0", [P, CHUNK], F32)
         for a in (0, HALF):
             nc.scalar.copy(plain[0, 1, 0][:, a : a + HALF], product(0, 1, a // HALF, a, a + HALF)[:])
         for number in range(2, 6):
             b, c = ORDER[number]
-            empty(b, c, 0, product(b, c, (5, 7, 6, 2)[number - 2], 0, CHUNK))
+            empty(b, c, 0, product(b, c, (2, 5, 0, 3)[number - 2], 0, CHUNK))
         plain_last = sb("plain_last", [P, J], F32)
         for c in range(2):
-            nc.scalar.copy(plain_last[:, c * CHUNK : (c + 1) * CHUNK], product(3, c, 3 + c, 0, CHUNK)[:])
+            nc.scalar.copy(plain_last[:, c * CHUNK : (c + 1) * CHUNK], product(3, c, (1, 4)[c], 0, CHUNK)[:])
 
         y_in = [sb("y_in%d" % g, [P, b - a, PACK], BF16) for g, (a, b) in enumerate(SPANS)]
         y_scales = sb("y_scales", [P, T], U8)
@@ -299,11 +302,14 @@ def tile_list_embg_tgq4_resP_kernel(
                 elif i >= 2:
                     nc.scalar.copy(dst, src)
 
-        place(0, 0, 0, HALF)
-        nc.vector.tensor_copy(window[0][:].indirect(offsets[:, HALF // 16 : CHUNK // 16]), second[:])
-        combine(0, 1, 0, CHUNK, HALF, "both")
-        for half in range(2):
-            place(0, 1, half * HALF, (half + 1) * HALF)
+        place(0, 0, 0, CHUNK)
+        both = sb("both", [P, CHUNK], F32)
+        for a in (0, HALF):
+            nc.gpsimd.tensor_tensor(
+                both[:, a : a + HALF], plain[0, 1, 0][:, a : a + HALF], res_sb[0, 1][:, a : a + HALF], ALU.add
+            )
+        weigh(0, 1, 0, CHUNK, both[:])
+        place(0, 1, 0, CHUNK)
         for b in range(1, PACK - 1):
             combine(b, 0, 0, CHUNK, CHUNK, "plain%d1_0" % (b - 1))
             place(b, 0, 0, CHUNK)

@@ -24,7 +24,7 @@ CHUNK = 512
 HALF = CHUNK // 2
 QUARTER = T // 4
 LOADS = [(0, 1), (1, 2), (2, 4), (4, 6), (6, 8)]
-LO_RUNS = [(0, 2), (2, 4), (4, 7), (7, 8)]
+LO_RUNS = [(0, 2), (2, 4), (4, 8)]
 ORDER = [(b, c) for b in range(PACK) for c in range(2)]
 SPANS = [(0, 512), (512, 896), (896, 1408), (1408, 1792), (1792, 2048)]
 
@@ -79,10 +79,11 @@ def tile_list_embg_tgq4_resP_kernel(
         nc.sync.dma_start(offsets[:], offs)
         load_res(0, 1)
         nc.sync.dma_start(gate[1], wgo[:, CHUNK:J])
-        for b, c in ORDER[2:6]:
-            load_res(b, c)
-        res_last = sb("res_last", [P, J], F32)
-        nc.sync.dma_start(res_last[:], res_v[:, 3, :])
+        load_res(1, 0)
+        load_res(1, 1)
+        for b in (2, 3):
+            res_sb[b] = sb("res%d" % b, [P, J], F32)
+            nc.sync.dma_start(res_sb[b][:], res_v[:, b, :])
 
         diag = sb("diag", [P, K + PACK], BF16, tag="hi_in1")
         ones = sb("ones", [P, K + PACK], BF16, tag="window1")
@@ -214,22 +215,8 @@ def tile_list_embg_tgq4_resP_kernel(
             plain[b, c, a] = sb("plain%d%d_%d" % (b, c, a), dx.shape, F32)
             nc.scalar.copy(plain[b, c, a][:], dx[:])
 
-        def weigh(b, c, a, z, both):
-            if a == 0:
-                total[b, c] = sb("total%d%d" % (b, c), [P, CHUNK], F32)
-            nc.gpsimd.tensor_tensor(total[b, c][:, a:z], both, gate[c][:, a:z], ALU.mult)
-
-        def combine(b, c, a, z, step, tag):
-            both = sb("both", [P, z - a], F32, tag=tag)
-            nc.gpsimd.tensor_tensor(both[:], plain[b, c, a][:], res_sb[b, c][:, a:z], ALU.add)
-            for s in range(a, z, step):
-                weigh(b, c, s, s + step, both[:, s - a : s - a + step])
-
-        def place(b, c, a, z):
-            nc.vector.tensor_copy(
-                window[b][:].indirect(offsets[:, (c * CHUNK + a) // 16 : (c * CHUNK + z) // 16]),
-                total[b, c][:, a:z],
-            )
+        def place(b, a, z, values):
+            nc.vector.tensor_copy(window[b][:].indirect(offsets[:, a // 16 : z // 16]), values)
 
         def start(a, b):
             for u in range(a, b):
@@ -250,30 +237,33 @@ def tile_list_embg_tgq4_resP_kernel(
         second_tier(1)
         leftover(4)
         start(6, 8)
-        total[0, 0] = sb("total00", [P, CHUNK], F32)
-        sums = sb("sums", [P, CHUNK], F32, tag="hi_in1")
-        for a in (0, HALF):
-            empty(0, 0, a, product(0, 0, 3 + a // HALF, a, a + HALF))
-            nc.gpsimd.tensor_tensor(
-                sums[:, a : a + HALF], plain[0, 0, a][:], res_sb[0, 0][:, a : a + HALF], ALU.add
-            )
-        nc.gpsimd.tensor_tensor(total[0, 0][:, 0:HALF], sums[:, 0:HALF], gate[0][:, 0:HALF], ALU.mult)
+        def vector_sum(name, dx, b, a, tag):
+            both = sb(name, [P, HALF], F32, tag=tag)
+            nc.vector.tensor_tensor(both[:], dx, res_sb[b, 0][:, a : a + HALF], ALU.add)
+            return both
+
+        empty(0, 0, 0, product(0, 0, 3, 0, HALF))
+        both = sb("sum_first", [P, HALF], F32, tag="hi_in1")
+        nc.gpsimd.tensor_tensor(both[:], plain[0, 0, 0][:], res_sb[0, 0][:, 0:HALF], ALU.add)
+        first = sb("first", [P, HALF], F32)
+        nc.gpsimd.tensor_tensor(first[:], both[:], gate[0][:, 0:HALF], ALU.mult)
+        own = product(0, 0, 4, HALF, CHUNK)
         for u in range(5, UNITS):
             leftover(u)
+        both = vector_sum("sum_second", own[:], 0, HALF, "dy4")
         second_tier(2)
-        nc.vector.tensor_tensor(
-            total[0, 0][:, HALF:CHUNK], sums[:, HALF:CHUNK], gate[0][:, HALF:CHUNK], ALU.mult
-        )
-        second_tier(3)
+        second = sb("second", [P, HALF], F32, tag="lo_in4")
+        nc.gpsimd.tensor_tensor(second[:], both[:], gate[0][:, HALF:CHUNK], ALU.mult)
         plain[0, 1, 0] = sb("plain01_0", [P, CHUNK], F32)
         for a in (0, HALF):
             nc.scalar.copy(plain[0, 1, 0][:, a : a + HALF], product(0, 1, a // HALF, a, a + HALF)[:])
-        for number in range(2, 6):
-            b, c = ORDER[number]
-            empty(b, c, 0, product(b, c, (2, 5, 0, 3)[number - 2], 0, CHUNK))
-        plain_last = sb("plain_last", [P, J], F32)
-        for c in range(2):
-            nc.scalar.copy(plain_last[:, c * CHUNK : (c + 1) * CHUNK], product(3, c, (1, 4)[c], 0, CHUNK)[:])
+        kept = product(1, 0, 2, 0, CHUNK)
+        empty(1, 1, 0, product(1, 1, 5, 0, CHUNK))
+        for b in (2, 3):
+            plain[b] = sb("plain%d" % b, [P, J], F32)
+            for c in range(2):
+                dx = product(b, c, ((0, 3), (1, 6))[b - 2][c], 0, CHUNK)
+                nc.scalar.copy(plain[b][:, c * CHUNK : (c + 1) * CHUNK], dx[:])
 
         y_in = [sb("y_in%d" % g, [P, b - a, PACK], BF16) for g, (a, b) in enumerate(SPANS)]
         y_scales = sb("y_scales", [P, T], U8)
@@ -285,7 +275,7 @@ def tile_list_embg_tgq4_resP_kernel(
             if i < 2:
                 nc.scalar.copy(flat[:, i, :], window[i][:])
             if i == 2:
-                one = sb("one", [P, 1], F32, tag="plain_last")
+                one = sb("one", [P, 1], F32, tag="plain3")
                 nc.gpsimd.memset(one[:], 1.0)
             for g, (a, b) in enumerate(SPANS):
                 src = window[i][:, a:b]
@@ -302,26 +292,36 @@ def tile_list_embg_tgq4_resP_kernel(
                 elif i >= 2:
                     nc.scalar.copy(dst, src)
 
-        place(0, 0, 0, CHUNK)
+        place(0, 0, HALF, first[:])
+        sums = [vector_sum("sum10_0", kept[:, 0:HALF], 1, 0, "dy6")]
+        place(0, HALF, CHUNK, second[:])
+        sums.append(vector_sum("sum10_1", kept[:, HALF:CHUNK], 1, HALF, "dy4"))
         both = sb("both", [P, CHUNK], F32)
         for a in (0, HALF):
             nc.gpsimd.tensor_tensor(
                 both[:, a : a + HALF], plain[0, 1, 0][:, a : a + HALF], res_sb[0, 1][:, a : a + HALF], ALU.add
             )
-        weigh(0, 1, 0, CHUNK, both[:])
-        place(0, 1, 0, CHUNK)
-        for b in range(1, PACK - 1):
-            combine(b, 0, 0, CHUNK, CHUNK, "plain%d1_0" % (b - 1))
-            place(b, 0, 0, CHUNK)
-            combine(b, 1, 0, CHUNK, CHUNK, "plain%d0_0" % b)
+        total = sb("total01", [P, CHUNK], F32)
+        nc.gpsimd.tensor_tensor(total[:], both[:], gate[1], ALU.mult)
+        place(0, CHUNK, J, total[:])
+        total = sb("total10", [P, CHUNK], F32, tag="plain01_0")
+        for h in range(2):
+            cols = slice(h * HALF, (h + 1) * HALF)
+            nc.gpsimd.tensor_tensor(total[:, cols], sums[h][:], gate[0][:, cols], ALU.mult)
+        place(1, 0, CHUNK, total[:])
+        both = sb("both", [P, CHUNK], F32)
+        nc.gpsimd.tensor_tensor(both[:], plain[1, 1, 0][:], res_sb[1, 1][:], ALU.add)
+        total = sb("total11", [P, CHUNK], F32)
+        nc.gpsimd.tensor_tensor(total[:], both[:], gate[1], ALU.mult)
+        finish(0)
+        place(1, CHUNK, J, total[:])
+        for b in (2, 3):
+            both = sb("both%d" % b, [P, J], F32, tag=("plain11_0", "plain2")[b - 2])
+            nc.gpsimd.tensor_tensor(both[:], plain[b][:], res_sb[b][:], ALU.add)
+            total = sb("total%d" % b, [P, J], F32)
+            nc.gpsimd.tensor_tensor(total[:], both[:], gates[:], ALU.mult)
             finish(b - 1)
-            place(b, 1, 0, CHUNK)
-        last = sb("last", [P, J], F32)
-        both = sb("both", [P, J], F32, tag="plain21_0")
-        nc.gpsimd.tensor_tensor(both[:], plain_last[:], res_last[:], ALU.add)
-        nc.gpsimd.tensor_tensor(last[:], both[:], gates[:], ALU.mult)
-        finish(2)
-        nc.vector.tensor_copy(window[3][:].indirect(offsets[:]), last[:])
+            place(b, 0, J, total[:])
         finish(3)
 
         for g, (a, b) in enumerate(SPANS):

@@ -22,7 +22,7 @@ UNIT = 128
 UNITS = J // UNIT
 CHUNK = 512
 HALF = CHUNK // 2
-QUARTER = T // 4
+DIRECT = 512
 LOADS = [(0, 1), (1, 2), (2, 4), (4, 6), (6, 8)]
 LO_RUNS = [(0, 2), (2, 4), (4, 8)]
 ORDER = [(b, c) for b in range(PACK) for c in range(2)]
@@ -77,9 +77,9 @@ def tile_list_embg_tgq4_resP_kernel(
         load_res(0, 0)
         nc.sync.dma_start(gate[0], wgo[:, 0:CHUNK])
         nc.sync.dma_start(offsets[:], offs)
+        load_res(1, 0)
         load_res(0, 1)
         nc.sync.dma_start(gate[1], wgo[:, CHUNK:J])
-        load_res(1, 0)
         load_res(1, 1)
         for b in (2, 3):
             res_sb[b] = sb("res%d" % b, [P, J], F32)
@@ -243,10 +243,12 @@ def tile_list_embg_tgq4_resP_kernel(
             return both
 
         empty(0, 0, 0, product(0, 0, 3, 0, HALF))
-        both = sb("sum_first", [P, HALF], F32, tag="hi_in1")
-        nc.gpsimd.tensor_tensor(both[:], plain[0, 0, 0][:], res_sb[0, 0][:, 0:HALF], ALU.add)
+        empty(1, 0, HALF, product(1, 0, 1, HALF, CHUNK))
+        early = sb("sums_early", [P, 2, HALF], F32, tag="hi_in1")
+        nc.gpsimd.tensor_tensor(early[:, 0, :], plain[0, 0, 0][:], res_sb[0, 0][:, 0:HALF], ALU.add)
+        nc.gpsimd.tensor_tensor(early[:, 1, :], plain[1, 0, HALF][:], res_sb[1, 0][:, HALF:CHUNK], ALU.add)
         first = sb("first", [P, HALF], F32)
-        nc.gpsimd.tensor_tensor(first[:], both[:], gate[0][:, 0:HALF], ALU.mult)
+        nc.gpsimd.tensor_tensor(first[:], early[:, 0, :], gate[0][:, 0:HALF], ALU.mult)
         own = product(0, 0, 4, HALF, CHUNK)
         for u in range(5, UNITS):
             leftover(u)
@@ -254,26 +256,33 @@ def tile_list_embg_tgq4_resP_kernel(
         second_tier(2)
         second = sb("second", [P, HALF], F32, tag="lo_in4")
         nc.gpsimd.tensor_tensor(second[:], both[:], gate[0][:, HALF:CHUNK], ALU.mult)
-        plain[0, 1, 0] = sb("plain01_0", [P, CHUNK], F32)
-        for a in (0, HALF):
-            nc.scalar.copy(plain[0, 1, 0][:, a : a + HALF], product(0, 1, a // HALF, a, a + HALF)[:])
-        kept = product(1, 0, 2, 0, CHUNK)
+        kept = product(1, 0, 2, 0, HALF)
+        empty(0, 1, 0, product(0, 1, 0, 0, CHUNK))
         empty(1, 1, 0, product(1, 1, 5, 0, CHUNK))
         for b in (2, 3):
             plain[b] = sb("plain%d" % b, [P, J], F32)
             for c in range(2):
-                dx = product(b, c, ((0, 3), (1, 6))[b - 2][c], 0, CHUNK)
+                dx = product(b, c, ((0, 3), (5, 6))[b - 2][c], 0, CHUNK)
                 nc.scalar.copy(plain[b][:, c * CHUNK : (c + 1) * CHUNK], dx[:])
 
         y_in = [sb("y_in%d" % g, [P, b - a, PACK], BF16) for g, (a, b) in enumerate(SPANS)]
         y_scales = sb("y_scales", [P, T], U8)
 
-        flat = sb("flat", [P, 2, T], BF16)
+        flat = [sb("flat0", [P, 2, DIRECT], BF16), sb("flat1", [P, 2, T - DIRECT], BF16)]
 
         def finish(i):
-            nc.sync.dma_start(out_v[:, i, :], window[i][:])
-            if i < 2:
-                nc.scalar.copy(flat[:, i, :], window[i][:])
+            if i == 0:
+                staged = sb("staged", [P, T - DIRECT], F32)
+                nc.sync.dma_start(out_v[:, i, 0:DIRECT], window[i][:, 0:DIRECT])
+                nc.scalar.copy(staged[:], window[i][:, DIRECT:T])
+                nc.scalar.copy(flat[0][:, i, :], window[i][:, 0:DIRECT])
+                nc.sync.dma_start(out_v[:, i, DIRECT:T], staged[:])
+                nc.scalar.copy(flat[1][:, i, :], staged[:])
+            else:
+                nc.sync.dma_start(out_v[:, i, :], window[i][:])
+            if i == 1:
+                nc.scalar.copy(flat[0][:, i, :], window[i][:, 0:DIRECT])
+                nc.scalar.copy(flat[1][:, i, :], window[i][:, DIRECT:T])
             if i == 2:
                 one = sb("one", [P, 1], F32, tag="plain3")
                 nc.gpsimd.memset(one[:], 1.0)
@@ -281,11 +290,12 @@ def tile_list_embg_tgq4_resP_kernel(
                 src = window[i][:, a:b]
                 dst = y_in[g][:, :, i]
                 if i == 1:
-                    nc.scalar.copy(y_in[g][:, :, 0:2], flat[:, :, a:b].rearrange("p e t -> p t e"))
-                if i == 2 and g < 4:
+                    pair = flat[1][:, :, a - DIRECT : b - DIRECT] if g else flat[0][:]
+                    nc.scalar.copy(y_in[g][:, :, 0:2], pair.rearrange("p e t -> p t e"))
+                if i == 2:
                     src = src.unsqueeze(2).to_broadcast([P, b - a, 2])
                     dst = y_in[g][:, :, 2:4]
-                if i == 2 and g in (2, 3):
+                if i == 2 and g >= 2:
                     nc.gpsimd.tensor_scalar(dst, src, one[:], 0.0, ALU.mult, ALU.add)
                 elif i == 3 and g < 2:
                     nc.vector.tensor_copy(dst, src)
@@ -293,28 +303,23 @@ def tile_list_embg_tgq4_resP_kernel(
                     nc.scalar.copy(dst, src)
 
         place(0, 0, HALF, first[:])
-        sums = [vector_sum("sum10_0", kept[:, 0:HALF], 1, 0, "dy6")]
+        sums = [vector_sum("sum10_0", kept[:], 1, 0, "dy6")[:], early[:, 1, :]]
         place(0, HALF, CHUNK, second[:])
-        sums.append(vector_sum("sum10_1", kept[:, HALF:CHUNK], 1, HALF, "dy4"))
-        both = sb("both", [P, CHUNK], F32)
-        for a in (0, HALF):
-            nc.gpsimd.tensor_tensor(
-                both[:, a : a + HALF], plain[0, 1, 0][:, a : a + HALF], res_sb[0, 1][:, a : a + HALF], ALU.add
-            )
-        total = sb("total01", [P, CHUNK], F32)
-        nc.gpsimd.tensor_tensor(total[:], both[:], gate[1], ALU.mult)
-        place(0, CHUNK, J, total[:])
-        total = sb("total10", [P, CHUNK], F32, tag="plain01_0")
+        total = sb("total10", [P, CHUNK], F32, tag="dy4")
         for h in range(2):
             cols = slice(h * HALF, (h + 1) * HALF)
-            nc.gpsimd.tensor_tensor(total[:, cols], sums[h][:], gate[0][:, cols], ALU.mult)
+            nc.gpsimd.tensor_tensor(total[:, cols], sums[h], gate[0][:, cols], ALU.mult)
         place(1, 0, CHUNK, total[:])
-        both = sb("both", [P, CHUNK], F32)
-        nc.gpsimd.tensor_tensor(both[:], plain[1, 1, 0][:], res_sb[1, 1][:], ALU.add)
-        total = sb("total11", [P, CHUNK], F32)
-        nc.gpsimd.tensor_tensor(total[:], both[:], gate[1], ALU.mult)
-        finish(0)
-        place(1, CHUNK, J, total[:])
+        sums = []
+        for b in range(2):
+            sums.append(sb("both%d" % b, [P, CHUNK], F32, tag=("both0", "dy6")[b]))
+            nc.gpsimd.tensor_tensor(sums[b][:], plain[b, 1, 0][:], res_sb[b, 1][:], ALU.add)
+        for b in range(2):
+            total = sb("total%d1" % b, [P, CHUNK], F32)
+            nc.gpsimd.tensor_tensor(total[:], sums[b][:], gate[1], ALU.mult)
+            place(b, CHUNK, J, total[:])
+            if b == 0:
+                finish(0)
         for b in (2, 3):
             both = sb("both%d" % b, [P, J], F32, tag=("plain11_0", "plain2")[b - 2])
             nc.gpsimd.tensor_tensor(both[:], plain[b][:], res_sb[b][:], ALU.add)

@@ -23,7 +23,7 @@ UNITS = J // UNIT
 CHUNK = 512
 HALF = CHUNK // 2
 DIRECT = 512
-LOADS = [(0, 1), (1, 2), (2, 4), (4, 6), (6, 8)]
+LOADS = [(0, 2), (2, 4), (4, 6), (6, 8)]
 LO_RUNS = [(0, 2), (2, 4), (4, 8)]
 ORDER = [(b, c) for b in range(PACK) for c in range(2)]
 SPANS = [(0, 512), (512, 896), (896, 1408), (1408, 1792), (1792, 2048)]

@@ -106,9 +106,7 @@ def tile_list_embg_tgq4_resP_kernel(
             window[b] = window[b + 2] = sb("window%d" % b, [P, T], F32)
         for a, z in ((0, J - 1), (J - 1, T)):
             nc.vector.memset(window[0][:, a:z].bitcast(I32), 0)
-        nc.gpsimd.memset(window[1][:, 0:1440].bitcast(I32), 0)
-        for a, z in ((1440, T - 1), (T - 1, T)):
-            nc.vector.memset(window[1][:, a:z].bitcast(I32), 0)
+        nc.vector.memset(window[1][:].bitcast(I32), 0)
 
         eye_codes = sb("eye_codes", [P, K], U32)
         eye_scales = sb("eye_scales", [P, K], U8)

@@ -54,7 +54,7 @@ def tile_list_embg_tgq4_resP_kernel(
         ws_raw = sb("ws_raw", [P, N], U8)
         gates = sb("gates", [P, J], F32)
         gate = [gates[:, c * CHUNK : (c + 1) * CHUNK] for c in range(2)]
-        nc.gpsimd.memset(ws_raw[:].bitcast(I32), 0)
+        nc.vector.memset(ws_raw[:].bitcast(I32), 0)
         dy_unit = {}
         for a, b in LOADS:
             raw = sb("dy%d" % a, [P, PACK, (b - a) * UNIT], F32)
@@ -85,18 +85,20 @@ def tile_list_embg_tgq4_resP_kernel(
             res_sb[b] = sb("res%d" % b, [P, J], F32)
             nc.sync.dma_start(res_sb[b][:], res_v[:, b, :])
 
-        diag = sb("diag", [P, K + PACK], BF16, tag="hi_in1")
-        ones = sb("ones", [P, K + PACK], BF16, tag="window1")
-        nc.gpsimd.memset(ones[:], 1.0)
+        pairs = (K + PACK) // 2
+        diag_words = sb("diag", [P, pairs], F32, tag="hi_in1")
+        zeros = sb("zeros", [P, pairs], F32, tag="window1")
+        nc.gpsimd.memset(zeros[:], 0.0)
         nc.gpsimd.affine_select(
-            out=diag[:],
-            in_=ones[:],
-            compare_op=ALU.is_equal,
-            fill=0.0,
-            base=-(PACK - 1),
-            pattern=[[1, K + PACK]],
-            channel_multiplier=-PACK,
+            out=diag_words[:],
+            in_=zeros[:],
+            compare_op=ALU.not_equal,
+            fill=1.0,
+            base=-1,
+            pattern=[[1, pairs]],
+            channel_multiplier=-2,
         )
+        diag = diag_words[:].bitcast(BF16)
         eye = [sb("eye%d" % h, [P, 2, K], BF16, tag=("hi_in0", "w_codes")[h]) for h in range(2)]
         for i in range(PACK):
             nc.scalar.copy(eye[i // 2][:, i % 2, :], diag[:, PACK - 1 - i : PACK - 1 - i + K])
@@ -104,9 +106,10 @@ def tile_list_embg_tgq4_resP_kernel(
         window = {}
         for b in range(2):
             window[b] = window[b + 2] = sb("window%d" % b, [P, T], F32)
-        for a, z in ((0, J - 1), (J - 1, T)):
-            nc.vector.memset(window[0][:, a:z].bitcast(I32), 0)
+        nc.vector.memset(window[0][:, 0 : J - 1].bitcast(I32), 0)
         nc.vector.memset(window[1][:].bitcast(I32), 0)
+        for a, z in ((J - 1, T - 1), (T - 1, T)):
+            nc.vector.memset(window[0][:, a:z].bitcast(I32), 0)
 
         eye_codes = sb("eye_codes", [P, K], U32)
         eye_scales = sb("eye_scales", [P, K], U8)

@@ -19,13 +19,11 @@ ALU = mybir.AluOpType
 P = 128
 PACK = 4
 UNIT = 128
-UNITS = J // UNIT
-CHUNK = 512
-HALF = CHUNK // 2
+QUARTER = 256
+CHUNK = 2 * QUARTER
+LATE = 3 * QUARTER
 DIRECT = 512
-LOADS = [(0, 2), (2, 4), (4, 6), (6, 8)]
-LO_RUNS = [(0, 2), (2, 4), (4, 8)]
-ORDER = [(b, c) for b in range(PACK) for c in range(2)]
+BESIDE = 639
 SPANS = [(0, 512), (512, 896), (896, 1408), (1408, 1792), (1792, 2048)]
 
 
@@ -53,37 +51,41 @@ def tile_list_embg_tgq4_resP_kernel(
         w_raw = sb("w_raw", [P, 2 * N], U8)
         ws_raw = sb("ws_raw", [P, N], U8)
         gates = sb("gates", [P, J], F32)
-        gate = [gates[:, c * CHUNK : (c + 1) * CHUNK] for c in range(2)]
         nc.vector.memset(ws_raw[:].bitcast(I32), 0)
-        dy_unit = {}
-        for a, b in LOADS:
-            raw = sb("dy%d" % a, [P, PACK, (b - a) * UNIT], F32)
-            nc.sync.dma_start(raw[:], dy_v[:, :, a * UNIT : b * UNIT])
-            for u in range(a, b):
-                dy_unit[u] = raw[:, :, (u - a) * UNIT : (u - a + 1) * UNIT]
-            if a == 0:
-                nc.sync.dma_start(w_raw[:].bitcast(I32), w_words[0].bitcast(I32))
-                for q in range(4):
-                    nc.sync.dma_start(
-                        ws_raw[32 * q : 32 * q + 4, :].bitcast(I32),
-                        w_scales[0, 4 * q : 4 * q + 4, :].bitcast(I32),
-                    )
-        res_sb = {}
+        dy_sb, dy_unit, res_sb = {}, {}, {}
 
-        def load_res(b, c):
-            res_sb[b, c] = sb("res%d%d" % (b, c), [P, CHUNK], F32)
-            nc.sync.dma_start(res_sb[b, c][:], res_v[:, b, c * CHUNK : (c + 1) * CHUNK])
+        def load_dy(q):
+            raw = dy_sb[q] = sb("dy%d" % q, [P, PACK, QUARTER], F32)
+            nc.sync.dma_start(raw[:], dy_v[:, :, q * QUARTER : (q + 1) * QUARTER])
+            for h in range(2):
+                dy_unit[2 * q + h] = raw[:, :, h * UNIT : (h + 1) * UNIT]
 
-        load_res(0, 0)
-        nc.sync.dma_start(gate[0], wgo[:, 0:CHUNK])
+        def load_res(b, a, z):
+            res_sb[b, a] = sb("res%d_%d" % (b, a), [P, z - a], F32)
+            nc.sync.dma_start(res_sb[b, a][:], res_v[:, b, a:z])
+
+        def load_gate(a, z):
+            nc.sync.dma_start(gates[:, a:z], wgo[:, a:z])
+
+        load_dy(0)
+        nc.sync.dma_start(w_raw[:].bitcast(I32), w_words[0].bitcast(I32))
+        for q in range(4):
+            nc.sync.dma_start(
+                ws_raw[32 * q : 32 * q + 4, :].bitcast(I32),
+                w_scales[0, 4 * q : 4 * q + 4, :].bitcast(I32),
+            )
+        load_dy(1)
+        load_dy(2)
+        load_dy(3)
+        load_res(0, 0, CHUNK)
+        load_res(1, 0, CHUNK)
+        load_gate(0, CHUNK)
         nc.sync.dma_start(offsets[:], offs)
-        load_res(1, 0)
-        load_res(0, 1)
-        nc.sync.dma_start(gate[1], wgo[:, CHUNK:J])
-        load_res(1, 1)
-        for b in (2, 3):
-            res_sb[b] = sb("res%d" % b, [P, J], F32)
-            nc.sync.dma_start(res_sb[b][:], res_v[:, b, :])
+        load_res(0, CHUNK, J)
+        load_res(1, CHUNK, J)
+        load_gate(CHUNK, J)
+        load_res(2, 0, J)
+        load_res(3, 0, J)
 
         pairs = (K + PACK) // 2
         diag_words = sb("diag", [P, pairs], F32, tag="hi_in1")
@@ -106,51 +108,60 @@ def tile_list_embg_tgq4_resP_kernel(
         window = {}
         for b in range(2):
             window[b] = window[b + 2] = sb("window%d" % b, [P, T], F32)
-        nc.vector.memset(window[0][:, 0 : J - 1].bitcast(I32), 0)
+        nc.vector.memset(window[0][:, 0:BESIDE].bitcast(I32), 0)
         nc.vector.memset(window[1][:].bitcast(I32), 0)
-        for a, z in ((J - 1, T - 1), (T - 1, T)):
+        for a, z in ((BESIDE, T - 1), (T - 1, T)):
             nc.vector.memset(window[0][:, a:z].bitcast(I32), 0)
 
         eye_codes = sb("eye_codes", [P, K], U32)
         eye_scales = sb("eye_scales", [P, K], U8)
         for h in range(2):
             nc.vector.quantize_mx(
-                out=eye_codes[:, h * HALF : (h + 1) * HALF].bitcast(E4M3),
-                scales=eye_scales[:, h * HALF : (h + 1) * HALF],
+                out=eye_codes[:, h * QUARTER : (h + 1) * QUARTER].bitcast(E4M3),
+                scales=eye_scales[:, h * QUARTER : (h + 1) * QUARTER],
                 in_=eye[h][:].rearrange("p i k -> p (i k)"),
             )
 
-        hi_codes = [sb("hi_codes%d" % c, [P, CHUNK], U32) for c in range(2)]
-        hi_scales = [sb("hi_scales%d" % c, [P, CHUNK], U8) for c in range(2)]
-        lo_codes = [sb("lo_codes%d" % c, [P, CHUNK], U32) for c in range(2)]
-        lo_scales = [sb("lo_scales%d" % c, [P, CHUNK], U8) for c in range(2)]
-        lo_in = {a: sb("lo_in%d" % a, [P, (b - a) * UNIT, PACK], BF16) for a, b in LO_RUNS}
-        hi_first = sb("hi_in0", [P, UNIT, PACK], BF16)
-        hi_rest = sb("hi_in1", [P, J - UNIT, PACK], BF16)
-        hi_in, back = {}, {}
+        hi_codes = [sb("hi_codes0", [P, LATE], U32)]
+        hi_scales = [sb("hi_scales%d" % c, [P, w], U8) for c, w in enumerate((LATE, QUARTER))]
+        lo_codes = sb("lo_codes", [P, J], U32)
+        lo_scales = sb("lo_scales", [P, J], U8)
+        lo_in = {
+            0: sb("lo_in0", [P, QUARTER, PACK], BF16),
+            2: sb("lo_in2", [P, QUARTER, PACK], BF16),
+            4: sb("lo_in4", [P, CHUNK, PACK], BF16),
+        }
+        hi_in = {0: sb("hi_in0", [P, UNIT, PACK], BF16), 1: sb("hi_in1", [P, J - UNIT, PACK], BF16)}
+        back = {}
 
-        def unit_cols(u):
-            return u // 4, slice((u % 4) * UNIT, (u % 4 + 1) * UNIT)
+        def run_of(runs, u):
+            first = max(a for a in runs if a <= u)
+            return runs[first], u - first
 
-        def weave(u):
-            hi_in[u] = hi_rest[:, (u - 1) * UNIT : u * UNIT, :] if u else hi_first[:]
-            copy = nc.scalar.copy if u else nc.vector.tensor_copy
+        def part(a, z):
+            c = a // LATE
+            return c, slice(a - c * LATE, z - c * LATE)
+
+        def weave(a, b):
+            tile, k = run_of(hi_in, a)
+            copy = nc.scalar.copy if a else nc.vector.tensor_copy
+            rows = dy_sb[a // 2][:, :, a % 2 * UNIT : (a % 2 + b - a) * UNIT]
             copy(
-                hi_in[u].rearrange("p (c e) i -> p c i e", e=4),
-                dy_unit[u].rearrange("p i (c e) -> p c i e", e=4),
+                tile[:, k * UNIT : (k + b - a) * UNIT, :].rearrange("p (c e) i -> p c i e", e=4),
+                rows.rearrange("p i (c e) -> p c i e", e=4),
             )
 
         def first_tier(a, b):
-            c, cols = a // 4, slice((a % 4) * UNIT, (a % 4 + b - a) * UNIT)
-            woven = hi_rest[:, (a - 1) * UNIT : (b - 1) * UNIT, :] if a else hi_first[:]
+            tile, k = run_of(hi_in, a)
+            c, cols = part(a * UNIT, b * UNIT)
             nc.vector.quantize_mx(
                 out=hi_codes[c][:, cols].bitcast(E5M2),
                 scales=hi_scales[c][:, cols],
-                in_=woven.rearrange("p j i -> p (j i)"),
+                in_=tile[:, k * UNIT : (k + b - a) * UNIT, :].rearrange("p j i -> p (j i)"),
             )
 
         def values(u):
-            c, cols = unit_cols(u)
+            c, cols = part(u * UNIT, (u + 1) * UNIT)
             back[u] = bank("back%d" % u, (0, 1, 2, 0, 1, 2, 6, 7)[u], [P, PACK, UNIT])
             for i in range(PACK):
                 nc.tensor.matmul_mx(
@@ -164,25 +175,23 @@ def tile_list_embg_tgq4_resP_kernel(
                 )
 
         def leftover(u):
-            first = max(a for a, b in LO_RUNS if a <= u)
-            dst = lo_in[first][:, (u - first) * UNIT : (u - first + 1) * UNIT, :]
+            tile, k = run_of(lo_in, u)
             nc.vector.tensor_tensor(
-                dst.rearrange("p (c e) i -> p c i e", e=2),
+                tile[:, k * UNIT : (k + 1) * UNIT, :].rearrange("p (c e) i -> p c i e", e=2),
                 dy_unit[u].rearrange("p i (c e) -> p c i e", e=2),
                 back[u][:].rearrange("p i (c e) -> p c i e", e=2),
                 ALU.subtract,
             )
 
-        def second_tier(run):
-            a, b = LO_RUNS[run]
-            c, cols = a // 4, slice((a % 4) * UNIT, (a % 4 + b - a) * UNIT)
+        def second_tier(a, b):
+            cols = slice(a * UNIT, b * UNIT)
             nc.vector.quantize_mx(
-                out=lo_codes[c][:, cols].bitcast(E4M3),
-                scales=lo_scales[c][:, cols],
+                out=lo_codes[:, cols].bitcast(E4M3),
+                scales=lo_scales[:, cols],
                 in_=lo_in[a][:].rearrange("p j i -> p (j i)"),
             )
 
-        plain, total, dealt = {}, {}, {}
+        dealt = {}
 
         def deal_codes():
             dealt["codes"] = sb("w_codes", [P, PACK, 2 * P], U8)
@@ -195,33 +204,47 @@ def tile_list_embg_tgq4_resP_kernel(
             dealt["scales"] = sb("w_sc", [P, PACK, P], U8, tag="hi_in0")
             nc.vector.tensor_copy(dealt["scales"][:], ws_raw[:].rearrange("p (m i) -> p i m", i=PACK))
 
-        def product(b, c, index, a, z):
-            dx = bank("dx%d%d_%d" % (b, c, a), index, [P, z - a])
-            for codes, scales, fmt, first in (
-                (hi_codes, hi_scales, E5M2, True),
-                (lo_codes, lo_scales, E4M3, False),
-            ):
-                nc.tensor.matmul_mx(
-                    out=dx[:],
-                    lhsT=dealt["codes"][:, b, :].bitcast(E2M1),
-                    lhsT_scale=dealt["scales"][:, b, :],
-                    rhs=codes[c][:, a:z].bitcast(fmt),
-                    rhs_scale=scales[c][:, a:z],
-                    start=first,
-                    stop=not first,
-                )
+        def product(b, a, z, index, lo_first=False):
+            dx = bank("dx%d_%d" % (b, a), index, [P, z - a])
+            cuts = [a, LATE, z] if a < LATE < z else [a, z]
+            for x, y in zip(cuts, cuts[1:]):
+                c, cols = part(x, y)
+                tiers = [
+                    (hi_codes[c][:, cols], hi_scales[c][:, cols], E5M2),
+                    (lo_codes[:, x:y], lo_scales[:, x:y], E4M3),
+                ]
+                for n, (codes, scales, fmt) in enumerate(tiers[::-1] if lo_first else tiers):
+                    nc.tensor.matmul_mx(
+                        out=dx[:, x - a : y - a],
+                        lhsT=dealt["codes"][:, b, :].bitcast(E2M1),
+                        lhsT_scale=dealt["scales"][:, b, :],
+                        rhs=codes.bitcast(fmt),
+                        rhs_scale=scales,
+                        start=n == 0,
+                        stop=n == 1,
+                    )
             return dx
 
-        def empty(b, c, a, dx):
-            plain[b, c, a] = sb("plain%d%d_%d" % (b, c, a), dx.shape, F32)
-            nc.scalar.copy(plain[b, c, a][:], dx[:])
+        def empty(name, dx):
+            plain = sb(name, dx.shape, F32)
+            nc.scalar.copy(plain[:], dx[:])
+            return plain
 
-        def place(b, a, z, values):
-            nc.vector.tensor_copy(window[b][:].indirect(offsets[:, a // 16 : z // 16]), values)
+        def add(engine, both, dx, b, a):
+            first = max(x for plane, x in res_sb if plane == b and x <= a)
+            engine.tensor_tensor(both, dx[:], res_sb[b, first][:, a - first : a - first + dx.shape[1]], ALU.add)
+
+        def weigh(name, both, a, tag=None):
+            total = sb(name, both.shape, F32, tag=tag)
+            nc.gpsimd.tensor_tensor(total[:], both[:], gates[:, a : a + both.shape[1]], ALU.mult)
+            return total
+
+        def place(b, a, total):
+            z = a + total.shape[1]
+            nc.vector.tensor_copy(window[b][:].indirect(offsets[:, a // 16 : z // 16]), total[:])
 
         def start(a, b):
-            for u in range(a, b):
-                weave(u)
+            weave(a, b)
             first_tier(a, b)
             for u in range(a, b):
                 values(u)
@@ -229,41 +252,42 @@ def tile_list_embg_tgq4_resP_kernel(
         start(0, 1)
         deal_codes()
         deal_scales()
-        for u in range(3):
-            start(u + 1, u + 2)
-            leftover(u)
-        second_tier(0)
-        leftover(3)
+        start(1, 2)
+        leftover(0)
+        start(2, 3)
+        leftover(1)
+        start(3, 4)
+        leftover(2)
+        second_tier(0, 2)
+        dx00 = product(0, 0, QUARTER, 3)
         start(4, 6)
-        second_tier(1)
+        leftover(3)
+        both0 = sb("both00", [P, CHUNK], F32)
+        add(nc.vector, both0[:, 0:QUARTER], dx00, 0, 0)
+        second_tier(2, 4)
+        dx01 = product(0, QUARTER, CHUNK, 4)
         leftover(4)
+        hi_codes.append(sb("hi_codes1", [P, QUARTER], U32, tag="lo_in2"))
         start(6, 8)
-        def vector_sum(name, dx, b, a, tag):
-            both = sb(name, [P, HALF], F32, tag=tag)
-            nc.vector.tensor_tensor(both[:], dx, res_sb[b, 0][:, a : a + HALF], ALU.add)
-            return both
-
-        empty(0, 0, 0, product(0, 0, 3, 0, HALF))
-        empty(1, 0, HALF, product(1, 0, 1, HALF, CHUNK))
-        early = sb("sums_early", [P, 2, HALF], F32, tag="hi_in1")
-        nc.gpsimd.tensor_tensor(early[:, 0, :], plain[0, 0, 0][:], res_sb[0, 0][:, 0:HALF], ALU.add)
-        nc.gpsimd.tensor_tensor(early[:, 1, :], plain[1, 0, HALF][:], res_sb[1, 0][:, HALF:CHUNK], ALU.add)
-        first = sb("first", [P, HALF], F32)
-        nc.gpsimd.tensor_tensor(first[:], early[:, 0, :], gate[0][:, 0:HALF], ALU.mult)
-        own = product(0, 0, 4, HALF, CHUNK)
-        for u in range(5, UNITS):
-            leftover(u)
-        both = vector_sum("sum_second", own[:], 0, HALF, "dy4")
-        second_tier(2)
-        second = sb("second", [P, HALF], F32, tag="lo_in4")
-        nc.gpsimd.tensor_tensor(second[:], both[:], gate[0][:, HALF:CHUNK], ALU.mult)
-        kept = product(1, 0, 2, 0, HALF)
-        empty(0, 1, 0, product(0, 1, 0, 0, CHUNK))
-        empty(1, 1, 0, product(1, 1, 5, 0, CHUNK))
+        plain10 = empty("plain10", product(1, 0, QUARTER, 5, lo_first=True))
+        dx11 = product(1, QUARTER, CHUNK, 0, lo_first=True)
+        leftover(5)
+        add(nc.vector, both0[:, QUARTER:CHUNK], dx01, 0, QUARTER)
+        both1 = sb("both10", [P, CHUNK], F32, tag="hi_in1")
+        add(nc.gpsimd, both1[:, 0:QUARTER], plain10, 1, 0)
+        total = {(0, 0): weigh("total00", both0, 0)}
+        leftover(6)
+        leftover(7)
+        add(nc.vector, both1[:, QUARTER:CHUNK], dx11, 1, QUARTER)
+        second_tier(4, 8)
+        place(0, 0, total[0, 0])
+        place(1, 0, weigh("total10", both1, 0, tag="lo_in4"))
+        late = [empty("plain%d1" % b, product(b, CHUNK, J, 1 + b)) for b in range(2)]
+        plain = {}
         for b in (2, 3):
             plain[b] = sb("plain%d" % b, [P, J], F32)
             for c in range(2):
-                dx = product(b, c, ((0, 3), (5, 6))[b - 2][c], 0, CHUNK)
+                dx = product(b, c * CHUNK, (c + 1) * CHUNK, ((6, 7), (1, 2))[b - 2][c], lo_first=True)
                 nc.scalar.copy(plain[b][:, c * CHUNK : (c + 1) * CHUNK], dx[:])
 
         y_in = [sb("y_in%d" % g, [P, b - a, PACK], BF16) for g, (a, b) in enumerate(SPANS)]
@@ -303,31 +327,19 @@ def tile_list_embg_tgq4_resP_kernel(
                 elif i >= 2:
                     nc.scalar.copy(dst, src)
 
-        place(0, 0, HALF, first[:])
-        sums = [vector_sum("sum10_0", kept[:], 1, 0, "dy6")[:], early[:, 1, :]]
-        place(0, HALF, CHUNK, second[:])
-        total = sb("total10", [P, CHUNK], F32, tag="dy4")
-        for h in range(2):
-            cols = slice(h * HALF, (h + 1) * HALF)
-            nc.gpsimd.tensor_tensor(total[:, cols], sums[h], gate[0][:, cols], ALU.mult)
-        place(1, 0, CHUNK, total[:])
-        sums = []
+        sums = [sb("both%d1" % b, [P, CHUNK], F32) for b in range(2)]
         for b in range(2):
-            sums.append(sb("both%d" % b, [P, CHUNK], F32, tag=("both0", "dy6")[b]))
-            nc.gpsimd.tensor_tensor(sums[b][:], plain[b, 1, 0][:], res_sb[b, 1][:], ALU.add)
+            add(nc.gpsimd, sums[b][:], late[b], b, CHUNK)
         for b in range(2):
-            total = sb("total%d1" % b, [P, CHUNK], F32)
-            nc.gpsimd.tensor_tensor(total[:], sums[b][:], gate[1], ALU.mult)
-            place(b, CHUNK, J, total[:])
+            place(b, CHUNK, weigh("total%d1" % b, sums[b], CHUNK))
             if b == 0:
                 finish(0)
         for b in (2, 3):
-            both = sb("both%d" % b, [P, J], F32, tag=("plain11_0", "plain2")[b - 2])
-            nc.gpsimd.tensor_tensor(both[:], plain[b][:], res_sb[b][:], ALU.add)
-            total = sb("total%d" % b, [P, J], F32)
-            nc.gpsimd.tensor_tensor(total[:], both[:], gates[:], ALU.mult)
+            both = sb("both%d" % b, [P, J], F32, tag=("plain11", "plain2")[b - 2])
+            add(nc.gpsimd, both[:], plain[b], b, 0)
+            weighted = weigh("total%d" % b, both, 0)
             finish(b - 1)
-            place(b, 0, J, total[:])
+            place(b, 0, weighted)
         finish(3)
 
         for g, (a, b) in enumerate(SPANS):

@@ -23,6 +23,7 @@ QUARTER = 256
 CHUNK = 2 * QUARTER
 LATE = 3 * QUARTER
 DIRECT = 512
+POOL_PAIRS = 3
 BESIDE = 639
 SPANS = [(0, 512), (512, 896), (896, 1408), (1408, 1792), (1792, 2048)]
 
@@ -295,6 +296,8 @@ def tile_list_embg_tgq4_resP_kernel(
 
         flat = [sb("flat0", [P, 2, DIRECT], BF16), sb("flat1", [P, 2, T - DIRECT], BF16)]
 
+        later = []
+
         def finish(i):
             if i == 0:
                 staged = sb("staged", [P, T - DIRECT], F32)
@@ -309,19 +312,22 @@ def tile_list_embg_tgq4_resP_kernel(
                 nc.scalar.copy(flat[0][:, i, :], window[i][:, 0:DIRECT])
                 nc.scalar.copy(flat[1][:, i, :], window[i][:, DIRECT:T])
             if i == 2:
-                one = sb("one", [P, 1], F32, tag="plain3")
-                nc.gpsimd.memset(one[:], 1.0)
+                unit = sb("unit", [P, 1], F32, tag="flat1")
+                nc.gpsimd.memset(unit[:], 1.0)
             for g, (a, b) in enumerate(SPANS):
                 src = window[i][:, a:b]
                 dst = y_in[g][:, :, i]
                 if i == 1:
                     pair = flat[1][:, :, a - DIRECT : b - DIRECT] if g else flat[0][:]
-                    nc.scalar.copy(y_in[g][:, :, 0:2], pair.rearrange("p e t -> p t e"))
+                    if g < POOL_PAIRS:
+                        nc.scalar.copy(y_in[g][:, :, 0:2], pair.rearrange("p e t -> p t e"))
+                    else:
+                        later.append((y_in[g][:, :, 0:2], pair.rearrange("p e t -> p t e")))
                 if i == 2:
                     src = src.unsqueeze(2).to_broadcast([P, b - a, 2])
                     dst = y_in[g][:, :, 2:4]
                 if i == 2 and g >= 2:
-                    nc.gpsimd.tensor_scalar(dst, src, one[:], 0.0, ALU.mult, ALU.add)
+                    nc.gpsimd.tensor_scalar(dst, src, unit[:], 0.0, ALU.mult, ALU.add)
                 elif i == 3 and g < 2:
                     nc.vector.tensor_copy(dst, src)
                 elif i >= 2:
@@ -338,6 +344,11 @@ def tile_list_embg_tgq4_resP_kernel(
             both = sb("both%d" % b, [P, J], F32, tag=("plain11", "plain2")[b - 2])
             add(nc.gpsimd, both[:], plain[b], b, 0)
             weighted = weigh("total%d" % b, both, 0)
+            if b == 3:
+                dealt["one"] = sb("one", [P, 1], F32, tag="plain2")
+                nc.gpsimd.memset(dealt["one"][:], 1.0)
+                for dst, src in later:
+                    nc.gpsimd.tensor_scalar(dst, src, dealt["one"][:], 0.0, ALU.mult, ALU.add)
             finish(b - 1)
             place(b, 0, weighted)
         finish(3)

@@ -24,7 +24,8 @@ CHUNK = 2 * QUARTER
 LATE = 3 * QUARTER
 DIRECT = 512
 POOL_PAIRS = 3
-BESIDE = 639
+BESIDE = 1023
+LEAD = 16
 SPANS = [(0, 512), (512, 896), (896, 1408), (1408, 1792), (1792, 2048)]
 
 
@@ -102,26 +103,25 @@ def tile_list_embg_tgq4_resP_kernel(
             channel_multiplier=-2,
         )
         diag = diag_words[:].bitcast(BF16)
-        eye = [sb("eye%d" % h, [P, 2, K], BF16, tag=("hi_in0", "w_codes")[h]) for h in range(2)]
-        for i in range(PACK):
-            nc.scalar.copy(eye[i // 2][:, i % 2, :], diag[:, PACK - 1 - i : PACK - 1 - i + K])
+        eye = sb("eye", [P, 2, K], BF16, tag="hi_in0")
+        for i in range(2):
+            nc.scalar.copy(eye[:, i, :], diag[:, PACK - 1 - i : PACK - 1 - i + K])
 
         window = {}
         for b in range(2):
             window[b] = window[b + 2] = sb("window%d" % b, [P, T], F32)
+        lead = sb("eye_lead", [P, LEAD + 2 * P], U32)
+        eye_codes = [lead[:, LEAD:], sb("eye_moved", [P, 2 * P], U32)[:]]
+        eye_scales = sb("eye_scales", [P, 2 * P], U8)
+        nc.vector.memset(lead[:, LEAD - 1 : LEAD].bitcast(I32), 0)
         nc.vector.memset(window[0][:, 0:BESIDE].bitcast(I32), 0)
         nc.vector.memset(window[1][:].bitcast(I32), 0)
         for a, z in ((BESIDE, T - 1), (T - 1, T)):
             nc.vector.memset(window[0][:, a:z].bitcast(I32), 0)
-
-        eye_codes = sb("eye_codes", [P, K], U32)
-        eye_scales = sb("eye_scales", [P, K], U8)
-        for h in range(2):
-            nc.vector.quantize_mx(
-                out=eye_codes[:, h * QUARTER : (h + 1) * QUARTER].bitcast(E4M3),
-                scales=eye_scales[:, h * QUARTER : (h + 1) * QUARTER],
-                in_=eye[h][:].rearrange("p i k -> p (i k)"),
-            )
+        nc.vector.quantize_mx(
+            out=eye_codes[0].bitcast(E4M3), scales=eye_scales[:], in_=eye[:].rearrange("p i k -> p (i k)")
+        )
+        nc.vector.tensor_copy(eye_codes[1].bitcast(U16), lead[:].bitcast(U16)[:, 2 * LEAD - 1 : 2 * LEAD - 1 + 4 * P])
 
         hi_codes = [sb("hi_codes0", [P, LATE], U32)]
         hi_scales = [sb("hi_scales%d" % c, [P, w], U8) for c, w in enumerate((LATE, QUARTER))]
@@ -167,8 +167,8 @@ def tile_list_embg_tgq4_resP_kernel(
             for i in range(PACK):
                 nc.tensor.matmul_mx(
                     out=back[u][:, i, :],
-                    lhsT=eye_codes[:, i * P : (i + 1) * P].bitcast(E4M3),
-                    lhsT_scale=eye_scales[:, i * P : (i + 1) * P],
+                    lhsT=eye_codes[i // 2][:, i % 2 * P : (i % 2 + 1) * P].bitcast(E4M3),
+                    lhsT_scale=eye_scales[:, i % 2 * P : (i % 2 + 1) * P],
                     rhs=hi_codes[c][:, cols].bitcast(E5M2),
                     rhs_scale=hi_scales[c][:, cols],
                     start=True,
@@ -195,15 +195,16 @@ def tile_list_embg_tgq4_resP_kernel(
         dealt = {}
 
         def deal_codes():
-            dealt["codes"] = sb("w_codes", [P, PACK, 2 * P], U8)
+            both = sb("w_dealt", [P, 3 * N], U8, tag="hi_in0")
+            dealt["codes"] = both[:, 0 : 2 * N].rearrange("p (i m) -> p i m", i=PACK)
+            dealt["scales"] = both[:, 2 * N :].rearrange("p (i m) -> p i m", i=PACK)
             nc.vector.tensor_copy(
-                dealt["codes"][:].bitcast(U16),
+                dealt["codes"].bitcast(U16),
                 w_raw[:].bitcast(U16).rearrange("p (m i) -> p i m", i=PACK),
             )
 
         def deal_scales():
-            dealt["scales"] = sb("w_sc", [P, PACK, P], U8, tag="hi_in0")
-            nc.vector.tensor_copy(dealt["scales"][:], ws_raw[:].rearrange("p (m i) -> p i m", i=PACK))
+            nc.vector.tensor_copy(dealt["scales"], ws_raw[:].rearrange("p (m i) -> p i m", i=PACK))
 
         def product(b, a, z, index, lo_first=False):
             dx = bank("dx%d_%d" % (b, a), index, [P, z - a])

@@ -24,7 +24,7 @@ CHUNK = 2 * QUARTER
 LATE = 3 * QUARTER
 DIRECT = 512
 POOL_PAIRS = 3
-BESIDE = 1023
+BESIDE = 639
 LEAD = 16
 SPANS = [(0, 512), (512, 896), (896, 1408), (1408, 1792), (1792, 2048)]
 
@@ -41,10 +41,14 @@ def tile_list_embg_tgq4_resP_kernel(
 
     with ExitStack() as ctx:
         held = ctx.enter_context(tc.tile_pool(name="held", bufs=1))
+        placed = ctx.enter_context(tc.tile_pool(name="placed", bufs=1))
         psum = ctx.enter_context(tc.psum_pool(name="psum", bufs=1))
 
         def sb(name, shape, dtype, tag=None):
             return held.tile(shape, dtype, name=name, tag=tag or name, align_bytes=64)
+
+        def at(name, shape, dtype, offset):
+            return placed.tile(shape, dtype, name=name, offset=offset, align_bytes=64)
 
         def bank(name, index, shape):
             return psum.tile(shape, F32, name=name, tag="bank%d" % index)
@@ -103,7 +107,7 @@ def tile_list_embg_tgq4_resP_kernel(
             channel_multiplier=-2,
         )
         diag = diag_words[:].bitcast(BF16)
-        eye = sb("eye", [P, 2, K], BF16, tag="hi_in0")
+        eye = at("eye", [P, 2, K], BF16, 1024)
         for i in range(2):
             nc.scalar.copy(eye[:, i, :], diag[:, PACK - 1 - i : PACK - 1 - i + K])
 
@@ -121,7 +125,7 @@ def tile_list_embg_tgq4_resP_kernel(
         nc.vector.quantize_mx(
             out=eye_codes[0].bitcast(E4M3), scales=eye_scales[:], in_=eye[:].rearrange("p i k -> p (i k)")
         )
-        nc.vector.tensor_copy(eye_codes[1].bitcast(U16), lead[:].bitcast(U16)[:, 2 * LEAD - 1 : 2 * LEAD - 1 + 4 * P])
+        nc.scalar.copy(eye_codes[1].bitcast(U16), lead[:].bitcast(U16)[:, 2 * LEAD - 1 : 2 * LEAD - 1 + 4 * P])
 
         hi_codes = [sb("hi_codes0", [P, LATE], U32)]
         hi_scales = [sb("hi_scales%d" % c, [P, w], U8) for c, w in enumerate((LATE, QUARTER))]
@@ -132,7 +136,11 @@ def tile_list_embg_tgq4_resP_kernel(
             2: sb("lo_in2", [P, QUARTER, PACK], BF16),
             4: sb("lo_in4", [P, CHUNK, PACK], BF16),
         }
-        hi_in = {0: sb("hi_in0", [P, UNIT, PACK], BF16), 1: sb("hi_in1", [P, J - UNIT, PACK], BF16)}
+        hi_in = {
+            0: at("hi_in0", [P, UNIT, PACK], BF16, 512),
+            1: sb("hi_in1", [P, UNIT, PACK], BF16),
+            2: at("hi_in2", [P, J - QUARTER, PACK], BF16, 2560),
+        }
         back = {}
 
         def run_of(runs, u):
@@ -195,15 +203,14 @@ def tile_list_embg_tgq4_resP_kernel(
         dealt = {}
 
         def deal_codes():
-            both = sb("w_dealt", [P, 3 * N], U8, tag="hi_in0")
-            dealt["codes"] = both[:, 0 : 2 * N].rearrange("p (i m) -> p i m", i=PACK)
-            dealt["scales"] = both[:, 2 * N :].rearrange("p (i m) -> p i m", i=PACK)
+            dealt["codes"] = at("w_codes", [P, PACK, 2 * P], U8, 1536)[:]
             nc.vector.tensor_copy(
                 dealt["codes"].bitcast(U16),
                 w_raw[:].bitcast(U16).rearrange("p (m i) -> p i m", i=PACK),
             )
 
         def deal_scales():
+            dealt["scales"] = at("w_sc", [P, PACK, P], U8, 512)[:]
             nc.vector.tensor_copy(dealt["scales"], ws_raw[:].rearrange("p (m i) -> p i m", i=PACK))
 
         def product(b, a, z, index, lo_first=False):
@@ -275,7 +282,7 @@ def tile_list_embg_tgq4_resP_kernel(
         dx11 = product(1, QUARTER, CHUNK, 0, lo_first=True)
         leftover(5)
         add(nc.vector, both0[:, QUARTER:CHUNK], dx01, 0, QUARTER)
-        both1 = sb("both10", [P, CHUNK], F32, tag="hi_in1")
+        both1 = at("both10", [P, CHUNK], F32, 4096)
         add(nc.gpsimd, both1[:, 0:QUARTER], plain10, 1, 0)
         total = {(0, 0): weigh("total00", both0, 0)}
         leftover(6)

from contextlib import ExitStack

import concourse.mybir as mybir

K, N, T, J = 512, 512, 2048, 1024
FLOPS = 1610612736

F32 = mybir.dt.float32
BF16 = mybir.dt.bfloat16
I32 = mybir.dt.int32
U32 = mybir.dt.uint32
U16 = mybir.dt.uint16
U8 = mybir.dt.uint8
E4M3 = mybir.dt.float8_e4m3fn_x4
E5M2 = mybir.dt.float8_e5m2_x4
E2M1 = mybir.dt.float4_e2m1fn_x4
ALU = mybir.AluOpType

P = 128
PACK = 4
UNIT = 128
QUARTER = 256
CHUNK = 2 * QUARTER
LATE = 3 * QUARTER
DIRECT = 512
POOL_PAIRS = 3
BESIDE = 639
LEAD = 16
SPANS = [(0, 512), (512, 896), (896, 1408), (1408, 1792), (1792, 2048)]


def tile_list_embg_tgq4_resP_kernel(
    tc, dy, w_words, w_scales, res, wgo, offs, out_0, out_1, out_2
):
    nc = tc.nc
    dy_v = dy.rearrange("(p i) j -> p i j", i=PACK)
    res_v = res.rearrange("(p i) j -> p i j", i=PACK)
    out_v = out_0.rearrange("(p i) t -> p i t", i=PACK)
    codes_v = out_1[0].rearrange("p t i -> p (t i)").bitcast(I32)
    scales_v = out_2[0].bitcast(I32)

    with ExitStack() as ctx:
        held = ctx.enter_context(tc.tile_pool(name="held", bufs=1))
        placed = ctx.enter_context(tc.tile_pool(name="placed", bufs=1))
        psum = ctx.enter_context(tc.psum_pool(name="psum", bufs=1))

        def sb(name, shape, dtype, tag=None):
            return held.tile(shape, dtype, name=name, tag=tag or name, align_bytes=64)

        def at(name, shape, dtype, offset):
            return placed.tile(shape, dtype, name=name, offset=offset, align_bytes=64)

        def bank(name, index, shape):
            return psum.tile(shape, F32, name=name, tag="bank%d" % index)

        offsets = held.tile([P, J // 16], U16, name="offsets")
        w_raw = sb("w_raw", [P, 2 * N], U8)
        ws_raw = sb("ws_raw", [P, N], U8)
        gates = sb("gates", [P, J], F32)
        nc.vector.memset(ws_raw[:].bitcast(I32), 0)
        dy_sb, dy_unit, res_sb = {}, {}, {}

        def load_dy(q):
            raw = dy_sb[q] = sb("dy%d" % q, [P, PACK, QUARTER], F32)
            nc.sync.dma_start(raw[:], dy_v[:, :, q * QUARTER : (q + 1) * QUARTER])
            for h in range(2):
                dy_unit[2 * q + h] = raw[:, :, h * UNIT : (h + 1) * UNIT]

        def load_res(b, a, z):
            res_sb[b, a] = sb("res%d_%d" % (b, a), [P, z - a], F32)
            nc.sync.dma_start(res_sb[b, a][:], res_v[:, b, a:z])

        def load_gate(a, z):
            nc.sync.dma_start(gates[:, a:z], wgo[:, a:z])

        load_dy(0)
        nc.sync.dma_start(w_raw[:].bitcast(I32), w_words[0].bitcast(I32))
        for q in range(4):
            nc.sync.dma_start(
                ws_raw[32 * q : 32 * q + 4, :].bitcast(I32),
                w_scales[0, 4 * q : 4 * q + 4, :].bitcast(I32),
            )
        load_dy(1)
        load_dy(2)
        load_dy(3)
        load_res(0, 0, CHUNK)
        load_res(1, 0, CHUNK)
        load_gate(0, CHUNK)
        nc.sync.dma_start(offsets[:], offs)
        load_res(0, CHUNK, J)
        load_res(1, CHUNK, J)
        load_gate(CHUNK, J)
        load_res(2, 0, J)
        load_res(3, 0, J)

        pairs = (K + PACK) // 2
        diag_words = sb("diag", [P, pairs], F32, tag="hi_in1")
        zeros = sb("zeros", [P, pairs], F32, tag="window1")
        nc.gpsimd.memset(zeros[:], 0.0)
        nc.gpsimd.affine_select(
            out=diag_words[:],
            in_=zeros[:],
            compare_op=ALU.not_equal,
            fill=1.0,
            base=-1,
            pattern=[[1, pairs]],
            channel_multiplier=-2,
        )
        diag = diag_words[:].bitcast(BF16)
        eye = at("eye", [P, 2, K], BF16, 1024)
        for i in range(2):
            nc.scalar.copy(eye[:, i, :], diag[:, PACK - 1 - i : PACK - 1 - i + K])

        window = {}
        for b in range(2):
            window[b] = window[b + 2] = sb("window%d" % b, [P, T], F32)
        lead = sb("eye_lead", [P, LEAD + 2 * P], U32)
        eye_codes = [lead[:, LEAD:], sb("eye_moved", [P, 2 * P], U32)[:]]
        eye_scales = sb("eye_scales", [P, 2 * P], U8)
        nc.vector.memset(lead[:, LEAD - 1 : LEAD].bitcast(I32), 0)
        nc.vector.memset(window[0][:, 0:BESIDE].bitcast(I32), 0)
        nc.vector.memset(window[1][:].bitcast(I32), 0)
        for a, z in ((BESIDE, T - 1), (T - 1, T)):
            nc.vector.memset(window[0][:, a:z].bitcast(I32), 0)
        nc.vector.quantize_mx(
            out=eye_codes[0].bitcast(E4M3), scales=eye_scales[:], in_=eye[:].rearrange("p i k -> p (i k)")
        )
        nc.scalar.copy(eye_codes[1].bitcast(U16), lead[:].bitcast(U16)[:, 2 * LEAD - 1 : 2 * LEAD - 1 + 4 * P])

        hi_codes = [sb("hi_codes0", [P, LATE], U32)]
        hi_scales = [sb("hi_scales%d" % c, [P, w], U8) for c, w in enumerate((LATE, QUARTER))]
        lo_codes = sb("lo_codes", [P, J], U32)
        lo_scales = sb("lo_scales", [P, J], U8)
        lo_in = {
            0: sb("lo_in0", [P, QUARTER, PACK], BF16),
            2: sb("lo_in2", [P, QUARTER, PACK], BF16),
            4: sb("lo_in4", [P, CHUNK, PACK], BF16),
        }
        hi_in = {
            0: at("hi_in0", [P, UNIT, PACK], BF16, 512),
            1: sb("hi_in1", [P, UNIT, PACK], BF16),
            2: at("hi_in2", [P, J - QUARTER, PACK], BF16, 2560),
        }
        back = {}

        def run_of(runs, u):
            first = max(a for a in runs if a <= u)
            return runs[first], u - first

        def part(a, z):
            c = a // LATE
            return c, slice(a - c * LATE, z - c * LATE)

        def weave(a, b):
            tile, k = run_of(hi_in, a)
            copy = nc.scalar.copy if a else nc.vector.tensor_copy
            rows = dy_sb[a // 2][:, :, a % 2 * UNIT : (a % 2 + b - a) * UNIT]
            copy(
                tile[:, k * UNIT : (k + b - a) * UNIT, :].rearrange("p (c e) i -> p c i e", e=4),
                rows.rearrange("p i (c e) -> p c i e", e=4),
            )

        def first_tier(a, b):
            tile, k = run_of(hi_in, a)
            c, cols = part(a * UNIT, b * UNIT)
            nc.vector.quantize_mx(
                out=hi_codes[c][:, cols].bitcast(E5M2),
                scales=hi_scales[c][:, cols],
                in_=tile[:, k * UNIT : (k + b - a) * UNIT, :].rearrange("p j i -> p (j i)"),
            )

        def values(u):
            c, cols = part(u * UNIT, (u + 1) * UNIT)
            back[u] = bank("back%d" % u, (0, 1, 2, 0, 1, 2, 6, 7)[u], [P, PACK, UNIT])
            for i in range(PACK):
                nc.tensor.matmul_mx(
                    out=back[u][:, i, :],
                    lhsT=eye_codes[i // 2][:, i % 2 * P : (i % 2 + 1) * P].bitcast(E4M3),
                    lhsT_scale=eye_scales[:, i % 2 * P : (i % 2 + 1) * P],
                    rhs=hi_codes[c][:, cols].bitcast(E5M2),
                    rhs_scale=hi_scales[c][:, cols],
                    start=True,
                    stop=True,
                )

        def leftover(u):
            tile, k = run_of(lo_in, u)
            nc.vector.tensor_tensor(
                tile[:, k * UNIT : (k + 1) * UNIT, :].rearrange("p (c e) i -> p c i e", e=2),
                dy_unit[u].rearrange("p i (c e) -> p c i e", e=2),
                back[u][:].rearrange("p i (c e) -> p c i e", e=2),
                ALU.subtract,
            )

        def second_tier(a, b):
            cols = slice(a * UNIT, b * UNIT)
            nc.vector.quantize_mx(
                out=lo_codes[:, cols].bitcast(E4M3),
                scales=lo_scales[:, cols],
                in_=lo_in[a][:].rearrange("p j i -> p (j i)"),
            )

        dealt = {}

        def deal_codes():
            dealt["codes"] = at("w_codes", [P, PACK, 2 * P], U8, 1536)[:]
            nc.vector.tensor_copy(
                dealt["codes"].bitcast(U16),
                w_raw[:].bitcast(U16).rearrange("p (m i) -> p i m", i=PACK),
            )

        def deal_scales():
            dealt["scales"] = at("w_sc", [P, PACK, P], U8, 512)[:]
            nc.vector.tensor_copy(dealt["scales"], ws_raw[:].rearrange("p (m i) -> p i m", i=PACK))

        def product(b, a, z, index, lo_first=False):
            dx = bank("dx%d_%d" % (b, a), index, [P, z - a])
            cuts = [a, LATE, z] if a < LATE < z else [a, z]
            for x, y in zip(cuts, cuts[1:]):
                c, cols = part(x, y)
                tiers = [
                    (hi_codes[c][:, cols], hi_scales[c][:, cols], E5M2),
                    (lo_codes[:, x:y], lo_scales[:, x:y], E4M3),
                ]
                for n, (codes, scales, fmt) in enumerate(tiers[::-1] if lo_first else tiers):
                    nc.tensor.matmul_mx(
                        out=dx[:, x - a : y - a],
                        lhsT=dealt["codes"][:, b, :].bitcast(E2M1),
                        lhsT_scale=dealt["scales"][:, b, :],
                        rhs=codes.bitcast(fmt),
                        rhs_scale=scales,
                        start=n == 0,
                        stop=n == 1,
                    )
            return dx

        def empty(name, dx):
            plain = sb(name, dx.shape, F32)
            nc.scalar.copy(plain[:], dx[:])
            return plain

        def add(engine, both, dx, b, a):
            first = max(x for plane, x in res_sb if plane == b and x <= a)
            engine.tensor_tensor(both, dx[:], res_sb[b, first][:, a - first : a - first + dx.shape[1]], ALU.add)

        def weigh(name, both, a, tag=None):
            total = sb(name, both.shape, F32, tag=tag)
            nc.gpsimd.tensor_tensor(total[:], both[:], gates[:, a : a + both.shape[1]], ALU.mult)
            return total

        def place(b, a, total):
            z = a + total.shape[1]
            nc.vector.tensor_copy(window[b][:].indirect(offsets[:, a // 16 : z // 16]), total[:])

        def start(a, b):
            weave(a, b)
            first_tier(a, b)
            for u in range(a, b):
                values(u)

        start(0, 1)
        deal_codes()
        deal_scales()
        start(1, 2)
        leftover(0)
        start(2, 3)
        leftover(1)
        start(3, 4)
        leftover(2)
        second_tier(0, 2)
        dx00 = product(0, 0, QUARTER, 3)
        start(4, 6)
        leftover(3)
        both0 = sb("both00", [P, CHUNK], F32)
        add(nc.vector, both0[:, 0:QUARTER], dx00, 0, 0)
        second_tier(2, 4)
        dx01 = product(0, QUARTER, CHUNK, 4)
        leftover(4)
        hi_codes.append(sb("hi_codes1", [P, QUARTER], U32, tag="lo_in2"))
        start(6, 8)
        plain10 = empty("plain10", product(1, 0, QUARTER, 5, lo_first=True))
        dx11 = product(1, QUARTER, CHUNK, 0, lo_first=True)
        leftover(5)
        add(nc.vector, both0[:, QUARTER:CHUNK], dx01, 0, QUARTER)
        both1 = at("both10", [P, CHUNK], F32, 4096)
        add(nc.gpsimd, both1[:, 0:QUARTER], plain10, 1, 0)
        total = {(0, 0): weigh("total00", both0, 0)}
        leftover(6)
        leftover(7)
        add(nc.vector, both1[:, QUARTER:CHUNK], dx11, 1, QUARTER)
        second_tier(4, 8)
        place(0, 0, total[0, 0])
        place(1, 0, weigh("total10", both1, 0, tag="lo_in4"))
        late = [empty("plain%d1" % b, product(b, CHUNK, J, 1 + b)) for b in range(2)]
        plain = {}
        for b in (2, 3):
            plain[b] = sb("plain%d" % b, [P, J], F32)
            for c in range(2):
                dx = product(b, c * CHUNK, (c + 1) * CHUNK, ((6, 7), (1, 2))[b - 2][c], lo_first=True)
                nc.scalar.copy(plain[b][:, c * CHUNK : (c + 1) * CHUNK], dx[:])

        y_in = [sb("y_in%d" % g, [P, b - a, PACK], BF16) for g, (a, b) in enumerate(SPANS)]
        y_scales = sb("y_scales", [P, T], U8)

        flat = [sb("flat0", [P, 2, DIRECT], BF16), sb("flat1", [P, 2, T - DIRECT], BF16)]

        later = []

        def finish(i):
            if i == 0:
                staged = sb("staged", [P, T - DIRECT], F32)
                nc.sync.dma_start(out_v[:, i, 0:DIRECT], window[i][:, 0:DIRECT])
                nc.scalar.copy(staged[:], window[i][:, DIRECT:T])
                nc.scalar.copy(flat[0][:, i, :], window[i][:, 0:DIRECT])
                nc.sync.dma_start(out_v[:, i, DIRECT:T], staged[:])
                nc.scalar.copy(flat[1][:, i, :], staged[:])
            else:
                nc.sync.dma_start(out_v[:, i, :], window[i][:])
            if i == 1:
                nc.scalar.copy(flat[0][:, i, :], window[i][:, 0:DIRECT])
                nc.scalar.copy(flat[1][:, i, :], window[i][:, DIRECT:T])
            if i == 2:
                unit = sb("unit", [P, 1], F32, tag="flat1")
                nc.gpsimd.memset(unit[:], 1.0)
            for g, (a, b) in enumerate(SPANS):
                src = window[i][:, a:b]
                dst = y_in[g][:, :, i]
                if i == 1:
                    pair = flat[1][:, :, a - DIRECT : b - DIRECT] if g else flat[0][:]
                    if g < POOL_PAIRS:
                        nc.scalar.copy(y_in[g][:, :, 0:2], pair.rearrange("p e t -> p t e"))
                    else:
                        later.append((y_in[g][:, :, 0:2], pair.rearrange("p e t -> p t e")))
                if i == 2:
                    src = src.unsqueeze(2).to_broadcast([P, b - a, 2])
                    dst = y_in[g][:, :, 2:4]
                if i == 2 and g >= 2:
                    nc.gpsimd.tensor_scalar(dst, src, unit[:], 0.0, ALU.mult, ALU.add)
                elif i == 3 and g < 2:
                    nc.vector.tensor_copy(dst, src)
                elif i >= 2:
                    nc.scalar.copy(dst, src)

        sums = [sb("both%d1" % b, [P, CHUNK], F32) for b in range(2)]
        for b in range(2):
            add(nc.gpsimd, sums[b][:], late[b], b, CHUNK)
        for b in range(2):
            place(b, CHUNK, weigh("total%d1" % b, sums[b], CHUNK))
            if b == 0:
                finish(0)
        for b in (2, 3):
            both = sb("both%d" % b, [P, J], F32, tag=("plain11", "plain2")[b - 2])
            add(nc.gpsimd, both[:], plain[b], b, 0)
            weighted = weigh("total%d" % b, both, 0)
            if b == 3:
                dealt["one"] = sb("one", [P, 1], F32, tag="plain2")
                nc.gpsimd.memset(dealt["one"][:], 1.0)
                for dst, src in later:
                    nc.gpsimd.tensor_scalar(dst, src, dealt["one"][:], 0.0, ALU.mult, ALU.add)
            finish(b - 1)
            place(b, 0, weighted)
        finish(3)

        for g, (a, b) in enumerate(SPANS):
            y_codes = sb("y_codes%d" % g, [P, b - a], U32)
            nc.vector.quantize_mx(
                out=y_codes[:].bitcast(E4M3),
                scales=y_scales[:, a:b],
                in_=y_in[g][:].rearrange("p j i -> p (j i)"),
            )
            nc.sync.dma_start(codes_v[:, a:b], y_codes[:].bitcast(I32))
        for q in range(4):
            queue = nc.scalar if q % 2 else nc.sync
            queue.dma_start(scales_v[4 * q : 4 * q + 4, :], y_scales[32 * q : 32 * q + 4, :].bitcast(I32))
